import numpy as np
import ml_dtypes


def mxq(x, axis, fmt="e4m3"):
    dtype, down = {"e4m3": (ml_dtypes.float8_e4m3fn, 7), "e5m2": (ml_dtypes.float8_e5m2, 14)}[fmt]
    v = np.moveaxis(np.asarray(x, np.float32).astype(ml_dtypes.bfloat16).astype(np.float64), axis, -1)
    blocks = v.reshape(v.shape[:-1] + (-1, 32))
    amax = np.abs(blocks).max(-1, keepdims=True)
    byte = np.maximum(np.where(amax > 0, np.frexp(amax)[1] - 1 + 127, 0) - down, 1)
    scale = np.exp2(byte - 127.0)
    codes = (blocks / scale).astype(np.float32).astype(dtype).astype(np.float64)
    return np.moveaxis((codes * scale).reshape(v.shape), -1, axis)


WIDE = False


def mx_kscale(k):
    if not WIDE:
        return np.ones(k)
    levels = np.array([18, -18])
    if k % 512:
        return np.exp2(np.random.permutation(np.resize(levels, k // 32))).repeat(32)
    a = np.empty((k // 512, 16))
    for p in range(k // 512):
        a[p, :8] = np.random.permutation(np.resize(levels, 8))
        for g in range(8):
            far = levels[np.abs(levels - a[p, g]) >= 10]
            a[p, g + 8] = far[np.random.randint(len(far))]
    return np.exp2(a.ravel()).repeat(32)


def f64(x):
    return np.asarray(x).astype(np.float64)


def striped(idx):
    return np.tile(np.asarray(idx).reshape(-1, 16).T, (8, 1)).astype(np.uint16)


def unstriped(offs):
    return offs[:16].T.reshape(-1).astype(np.int64)

def planes(y):
    n, m = y.shape
    v = y.astype(np.float32).astype(ml_dtypes.bfloat16).astype(np.float64).reshape(n // 32, 32, m)
    top = np.abs(v).max(1)
    byte = np.clip(np.where(top > 0, np.frexp(top)[1] - 1 + 127 - 7, 1), 1, 254)
    codes = (v * np.exp2(127.0 - byte)[:, None, :]).reshape(n, m).astype(np.float32).astype(ml_dtypes.float8_e4m3fn).view(np.uint8)
    words = codes.reshape(n // 512, 128, 4, m).transpose(0, 1, 3, 2)
    return np.ascontiguousarray(words), np.ascontiguousarray(byte.astype(np.uint8).reshape(n // 512, 16, m))


def setup_inputs():
    n = np.random.standard_normal
    uni = np.random.uniform
    idx = np.random.permutation(2048)[:512]
    jdx = np.random.permutation(2048)[:512]
    soft_y = np.exp(0.4 * n((512, 512)))
    f_d = mx_kscale(512)
    f_j = np.ones(2048)
    f_j[jdx] = mx_kscale(512)
    return {
        "uT": (0.35 * n((512, 2048)) / np.sqrt(512) * f_d[:, None]).astype(np.float32),
        "vT": (n((512, 2048)) / f_d[:, None] * f_j[None, :]).astype(np.float32),
        "su": np.tile(uni(0.75, 1.3, 2048), (128, 1)).astype(np.float32),
        "sv": np.tile(uni(0.75, 1.3, 2048) / f_j, (128, 1)).astype(np.float32),
        "y": (soft_y / soft_y.sum(-1, keepdims=True)).astype(np.float32),
        "offs": striped(idx),
        "qoffs": striped(jdx),
    }


def reference(uT, vT, su, sv, y, offs, qoffs):
    idx = unstriped(offs)
    jdx = unstriped(qoffs)
    uT_i = f64(uT)[:, idx]
    vT_j = f64(vT)[:, jdx]
    su_i = f64(su)[:1][:, idx]
    sv_j = f64(sv)[:1][:, jdx]
    suc = su_i.T
    a = mxq(uT_i, 0, "e4m3").T @ mxq(vT_j, 0, "e4m3")
    e = np.exp(suc * sv_j * a)
    r1 = (e).sum(-1, keepdims=True)
    f = e / r1
    ft = f.T
    c1 = (ft).sum(-1, keepdims=True)
    cr = c1.T
    g = suc * sv_j * (f / cr - f64(y))
    du = mxq(vT_j, 1, "e4m3") @ mxq(g, 1, "e5m2").T
    out_0 = np.zeros((512, 2048))
    out_0[:, idx] = du
    return (out_0,) + planes(out_0)

@@ -1,0 +1,292 @@
+from contextlib import ExitStack
+
+import concourse.mybir as mybir
+from concourse.masks import make_identity
+
+FLOPS = 536870912
+
+F32 = mybir.dt.float32
+BF16 = mybir.dt.bfloat16
+I32 = mybir.dt.int32
+U32 = mybir.dt.uint32
+U16 = mybir.dt.uint16
+U8 = mybir.dt.uint8
+E4M3 = mybir.dt.float8_e4m3fn_x4
+E5M2 = mybir.dt.float8_e5m2_x4
+ALU = mybir.AluOpType
+ACT = mybir.ActivationFunctionType
+
+P = 128
+LANES = 4
+POOL = 2048
+SLOTS = 512
+HALF = SLOTS // 2
+WIDTHS = (256, 512, 512, 256, 256, 256)
+ON_VECTOR = 4
+STARTS = [sum(WIDTHS[:c]) for c in range(len(WIDTHS))]
+
+
+def tile_attend_gsink_u_pl_kernel(tc, uT, vT, su, sv, y, offs, qoffs, out_0, out_1, out_2):
+    nc = tc.nc
+    with ExitStack() as ctx:
+        lists = ctx.enter_context(tc.tile_pool(name="lists", bufs=1))
+        sb = ctx.enter_context(tc.tile_pool(name="sb", bufs=1))
+        ps = ctx.enter_context(tc.psum_pool(name="ps", bufs=1))
+
+        def sbuf(shape, dtype, name, tag=None):
+            return sb.tile(shape, dtype, name=name, tag=tag or name, align_bytes=64)
+
+        def bank(n, name):
+            return ps.tile([P, LANES, P], F32, name=name, tag="bank%d" % n)
+
+        def flat(ap):
+            return ap.rearrange("p a b -> p (a b)")
+
+        jlist = lists.tile([P, SLOTS // 16], U16, name="jlist")
+        ilist = lists.tile([P, SLOTS // 16], U16, name="ilist")
+        v_rows = vT.rearrange("(p t) c -> p t c", t=LANES)
+        u_rows = uT.rearrange("(p t) c -> p t c", t=LANES)
+        v_pool = [sbuf([P, POOL], F32, "v_pool%d" % t) for t in range(LANES)]
+        u_pool = [sbuf([P, POOL], F32, "u_pool%d" % t) for t in range(LANES)]
+        y_tile = [sbuf([P, SLOTS], F32, "y%d" % b) for b in range(LANES)]
+        sv_pool = sbuf([P, POOL], F32, "sv_pool")
+        su_pool = sbuf([P, POOL], F32, "su_pool")
+        nc.sync.dma_start(v_pool[0][:], v_rows[:, 0, :])
+        nc.sync.dma_start(jlist[:], qoffs)
+        nc.sync.dma_start(ilist[:], offs)
+        nc.scalar.dma_start(sv_pool[P - 1 : P, :], sv[0:1, :])
+        nc.scalar.dma_start(su_pool[P - 1 : P, :], su[0:1, :])
+        nc.vector.memset(sv_pool[0 : P - 1, :], 0.0)
+        nc.vector.memset(su_pool[0 : P - 1, :], 0.0)
+        for t in range(1, LANES):
+            nc.sync.dma_start(v_pool[t][:], v_rows[:, t, :])
+        for t in range(LANES):
+            nc.sync.dma_start(u_pool[t][:], u_rows[:, t, :])
+        for b in range(LANES):
+            nc.sync.dma_start(y_tile[b][:], y[b * P : (b + 1) * P, :])
+
+        ident = sbuf([P, P], F32, "ident")
+        make_identity(nc, ident[:])
+
+        window = [sbuf([P, POOL], F32, "window%d" % t) for t in range(LANES)]
+        for t in range(LANES):
+            nc.vector.memset(window[t][:], 0.0)
+
+        v_planes = sbuf([P, LANES, SLOTS], BF16, "v_planes")
+        for t in range(LANES):
+            nc.vector.tensor_copy(v_planes[:, t, :], v_pool[t][:].indirect(jlist[:]))
+        v_by_d = sbuf([P, SLOTS, LANES], BF16, "v_by_d")
+        nc.scalar.copy(v_by_d[:], v_planes[:].rearrange("p t j -> p j t"))
+        vd_codes = sbuf([P, SLOTS], U32, "vd_codes")
+        vd_scales = sbuf([P, SLOTS], U8, "vd_scales")
+        nc.vector.quantize_mx(vd_codes[:].bitcast(E4M3), vd_scales[:], flat(v_by_d[:]))
+
+        sv_listed = sbuf([P, SLOTS], F32, "sv_listed")
+        nc.vector.tensor_copy(sv_listed[:], sv_pool[:].indirect(jlist[:]))
+        su_listed = sbuf([P, SLOTS], F32, "su_listed")
+        nc.vector.tensor_copy(su_listed[:], su_pool[:].indirect(ilist[:]))
+        sv_turned = bank(0, "sv_turned")
+        for r in range(LANES):
+            nc.tensor.transpose(sv_turned[:, r, :], sv_listed[:, r::LANES], ident[:])
+        sv_col = sbuf([P, LANES], F32, "sv_col")
+        nc.scalar.copy(sv_col[:], sv_turned[:, :, P - 1])
+        su_turned = bank(1, "su_turned")
+        for b in range(LANES):
+            nc.tensor.transpose(su_turned[:, b, :], su_listed[:, b * P : (b + 1) * P], ident[:])
+        su_col = sbuf([P, LANES], F32, "su_col")
+        nc.scalar.copy(su_col[:], su_turned[:, :, P - 1])
+        sv_spread = bank(2, "sv_spread")
+        for r in range(LANES):
+            nc.tensor.transpose(sv_spread[:, r, :], sv_col[:, r : r + 1].to_broadcast([P, P]), ident[:])
+        sv_row = sbuf([P, LANES, P], F32, "sv_row")
+        nc.scalar.copy(sv_row[:], sv_spread[:])
+
+        v_words = flat(v_by_d[:]).bitcast(F32)
+        v_by_j = sbuf([P, LANES, P, LANES], BF16, "v_by_j")
+        for u in range(2):
+            turned = bank(4 + u, "v_turned%d" % u)
+            for r in range(LANES):
+                nc.tensor.transpose(turned[:, r, :], v_words[:, 2 * r + u :: 2 * LANES], ident[:])
+            nc.scalar.copy(
+                v_by_j[:, 2 * u : 2 * u + 2, :, :],
+                flat(turned[:]).bitcast(BF16).rearrange("s (r p e) -> s e p r", r=LANES, e=2),
+            )
+        vj_codes = sbuf([P, SLOTS], U32, "vj_codes")
+        vj_scales = sbuf([P, SLOTS], U8, "vj_scales")
+        nc.vector.quantize_mx(vj_codes[:].bitcast(E4M3), vj_scales[:], v_by_j[:].rearrange("s t p r -> s (t p r)"))
+
+        u_by_d = sbuf([P, SLOTS, LANES], BF16, "u_by_d")
+        for t in range(LANES - 1):
+            nc.vector.tensor_copy(u_by_d[:, :, t], u_pool[t][:].indirect(ilist[:]))
+        u_codes = sbuf([P, SLOTS], U32, "u_codes")
+        u_scales = sbuf([P, SLOTS], U8, "u_scales")
+        for h in range(2):
+            cols = slice(h * HALF, (h + 1) * HALF)
+            nc.vector.tensor_copy(
+                u_by_d[:, cols, LANES - 1],
+                u_pool[LANES - 1][:].indirect(ilist[:, h * HALF // 16 : (h + 1) * HALF // 16]),
+            )
+        for h in range(2):
+            cols = slice(h * HALF, (h + 1) * HALF)
+            nc.vector.quantize_mx(u_codes[:, cols].bitcast(E4M3), u_scales[:, cols], flat(u_by_d[:, cols, :]))
+
+        scaled = [sbuf([P, LANES, P], F32, "scaled%d" % b) for b in range(LANES)]
+        expd = [sbuf([P, SLOTS], F32, "expd%d" % b) for b in range(LANES)]
+        r1 = [sbuf([P, 2], F32, "r1_%d" % h) for h in range(2)]
+        for b in range(LANES):
+            cols = slice(b * P, (b + 1) * P)
+            score = bank(b, "score%d" % b)
+            nc.tensor.matmul_mx(
+                flat(score[:]),
+                lhsT=u_codes[:, cols].bitcast(E4M3),
+                lhsT_scale=u_scales[:, cols],
+                rhs=vd_codes[:].bitcast(E4M3),
+                rhs_scale=vd_scales[:],
+                start=True,
+                stop=True,
+            )
+            nc.vector.tensor_tensor(
+                scaled[b][:], flat(score[:]).rearrange("p (s r) -> p r s", r=LANES), sv_row[:], ALU.mult
+            )
+            nc.scalar.activation(expd[b][:], flat(scaled[b][:]), ACT.Exp, scale=su_col[:, b : b + 1], accum_out=r1[b // 2][:, b % 2 : b % 2 + 1])
+
+        y_turned = [bank(4 + r, "y_turned%d" % r) for r in range(LANES)]
+        for b in range(LANES):
+            y_su = sbuf([P, LANES, P], F32, "y_su%d" % b)
+            nc.scalar.activation(
+                y_su[:].rearrange("p r s -> p s r"),
+                y_tile[b][:].rearrange("p (s r) -> p s r", r=LANES),
+                ACT.Copy,
+                scale=su_col[:, b : b + 1],
+            )
+            for r in range(LANES):
+                nc.tensor.transpose(y_turned[r][:, b, :], y_su[:, r, :], ident[:])
+        y_both = [sbuf([P, SLOTS], F32, "y_both%d" % r, tag="y%d" % r) for r in range(LANES)]
+
+        def finish_y(r):
+            nc.scalar.activation(y_both[r][:], flat(y_turned[r][:]), ACT.Copy, scale=sv_col[:, r : r + 1])
+
+        finish_y(0)
+
+        rinv_pair = [sbuf([P, 2], F32, "rinv%d" % h) for h in range(2)]
+        rinv = [rinv_pair[b // 2][:, b % 2 : b % 2 + 1] for b in range(LANES)]
+        rsu = [sbuf([P, 1], F32, "rsu%d" % b) for b in range(LANES)]
+        partial = [[sbuf([P, HALF], F32, "partial%d_%d" % (b, h)) for h in range(2)] for b in range(LANES)]
+        for b in range(LANES):
+            if b % 2 == 0:
+                nc.vector.reciprocal(rinv_pair[b // 2][:], r1[b // 2][:])
+            for h in range(2):
+                e_half = expd[b][:, h * HALF : (h + 1) * HALF]
+                if b == 0:
+                    nc.vector.tensor_scalar(partial[0][h][:], e_half, rinv[0], None, ALU.mult)
+                else:
+                    nc.vector.scalar_tensor_tensor(
+                        partial[b][h][:], e_half, rinv[b], partial[b - 1][h][:], ALU.mult, ALU.add
+                    )
+        sums_turned = bank(4, "sums_turned")
+        for r in range(LANES):
+            nc.tensor.transpose(sums_turned[:, r, :], partial[LANES - 1][r // 2][:, r % 2 * P : (r % 2 + 1) * P], ident[:])
+        c1 = sbuf([P, LANES], F32, "c1")
+        nc.vector.tensor_reduce(c1[:], sums_turned[:], mybir.AxisListType.X, ALU.add)
+        cinv = sbuf([P, LANES], F32, "cinv")
+        nc.vector.reciprocal(cinv[:], c1[:])
+        csv = sbuf([P, LANES], F32, "csv")
+        nc.vector.tensor_tensor(csv[:], cinv[:], sv_col[:], ALU.mult)
+
+        f_turned = [bank(r, "f_turned%d" % r) for r in range(LANES)]
+        for b in range(LANES):
+            f_su = sbuf([P, SLOTS], F32, "f_su%d" % b, tag="scaled%d" % b)
+            nc.scalar.activation(rsu[b][:], rinv[b], ACT.Copy, scale=su_col[:, b : b + 1])
+            nc.scalar.activation(f_su[:], expd[b][:], ACT.Copy, scale=rsu[b][:])
+            for r in range(LANES):
+                nc.tensor.transpose(f_turned[r][:, b, :], f_su[:, r * P : (r + 1) * P], ident[:])
+        for r in range(1, LANES):
+            finish_y(r)
+
+        g_codes = sbuf([P, HALF + SLOTS], U32, "g_codes")
+        g_scales = sbuf([P, HALF + SLOTS], U8, "g_scales")
+        nc.vector.memset(g_codes[:, 0:HALF].bitcast(I32), 0)
+        nc.vector.memset(g_scales[:, 0:HALF].bitcast(I32), 0)
+        g_planes = [sbuf([P, LANES, HALF], BF16, "g_planes%d" % h) for h in range(2)]
+        g_by_j = [sbuf([P, HALF, LANES], BF16, "g_by_j%d" % h) for h in range(2)]
+        for h in range(2):
+            cols = slice(h * HALF, (h + 1) * HALF)
+            for r in range(LANES):
+                nc.vector.scalar_tensor_tensor(
+                    g_planes[h][:, r, :],
+                    flat(f_turned[r][:])[:, cols],
+                    csv[:, r : r + 1],
+                    y_both[r][:, cols],
+                    ALU.mult,
+                    ALU.subtract,
+                )
+        nc.scalar.copy(g_by_j[0][:], g_planes[0][:].rearrange("s r i -> s i r"))
+
+        def quantise_g(h):
+            cols = slice((h + 1) * HALF, (h + 2) * HALF)
+            nc.vector.quantize_mx(g_codes[:, cols].bitcast(E5M2), g_scales[:, cols], flat(g_by_j[h][:]))
+
+        def product(t, first, n, name):
+            cols = slice(t * P, (t + 1) * P)
+            acc = bank(n, name)
+            nc.tensor.matmul_mx(
+                flat(acc[:]),
+                lhsT=vj_codes[:, cols].bitcast(E4M3),
+                lhsT_scale=vj_scales[:, cols],
+                rhs=g_codes[:, first : first + SLOTS].bitcast(E5M2),
+                rhs_scale=g_scales[:, first : first + SLOTS],
+                start=True,
+                stop=True,
+            )
+            return flat(acc[:])
+
+        quantise_g(0)
+        du_early = sbuf([P, HALF], F32, "du_early")
+        nc.scalar.copy(du_early[:], product(0, 0, 4, "du_acc_early")[:, HALF:SLOTS])
+        nc.vector.tensor_copy(g_by_j[1][:], g_planes[1][:].rearrange("s r i -> s i r"))
+        quantise_g(1)
+
+        out_rows = out_0.rearrange("(p t) c -> p t c", t=LANES)
+        du = [sbuf([P, SLOTS], F32, "du%d" % t, tag="expd%d" % t) for t in range(LANES)]
+        nc.scalar.copy(du[0][:, HALF:SLOTS], product(0, HALF, 5, "du_acc0")[:, HALF:SLOTS])
+        for t in range(1, LANES):
+            nc.scalar.copy(du[t][:], product(t, HALF, (5 + t) % 8, "du_acc%d" % t))
+        pairs = [sbuf([P, 2, w, 2], BF16, "pairs%d" % c) for c, w in enumerate(WIDTHS)]
+        for t in range(LANES):
+            if t == 0:
+                nc.vector.tensor_copy(window[0][:].indirect(ilist[:, 0 : HALF // 16]), du_early[:])
+                nc.vector.tensor_copy(window[0][:].indirect(ilist[:, HALF // 16 : SLOTS // 16]), du[0][:, HALF:SLOTS])
+            else:
+                nc.vector.tensor_copy(window[t][:].indirect(ilist[:]), du[t][:])
+            nc.sync.dma_start(out_rows[:, t, :], window[t][:])
+            for c, w in enumerate(WIDTHS):
+                nc.scalar.copy(pairs[c][:, t // 2, :, t % 2], window[t][:, STARTS[c] : STARTS[c] + w])
+
+        o_codes = sbuf([P, POOL], U32, "o_codes", tag="v_pool0")
+        o_scales = sbuf([P, POOL], U8, "o_scales")
+        words_out = out_1.rearrange("a p c l -> p (a c l)").bitcast(I32)
+        scales_out = out_2.rearrange("a q c -> q (a c)").bitcast(I32)
+        spare = ["u_pool0", "u_pool1", "u_pool2", "u_pool3", "v_pool1", "v_pool2"]
+        o_by_d = [sbuf([P, w * LANES], BF16, "o_by_d%d" % c, tag=spare[c]) for c, w in enumerate(WIDTHS)]
+
+        def weave(c):
+            dst = o_by_d[c][:].bitcast(F32).rearrange("p (c u) -> p c u", u=2)
+            src = pairs[c][:].rearrange("p u c e -> p (u c e)").bitcast(F32).rearrange("p (u c) -> p c u", u=2)
+            if c < ON_VECTOR:
+                nc.vector.tensor_copy(dst, src)
+            else:
+                nc.scalar.copy(dst, src)
+
+        def quantise_out(c):
+            cols = slice(STARTS[c], STARTS[c] + WIDTHS[c])
+            nc.vector.quantize_mx(o_codes[:, cols].bitcast(E4M3), o_scales[:, cols], o_by_d[c][:])
+            nc.sync.dma_start(words_out[:, cols], o_codes[:, cols].bitcast(I32))
+
+        weave(0)
+        for c in range(1, len(WIDTHS)):
+            weave(c)
+            quantise_out(c - 1)
+        quantise_out(len(WIDTHS) - 1)
+        for q in range(4):
+            queue = nc.scalar if q % 2 else nc.sync
+            queue.dma_start(scales_out[4 * q : 4 * q + 4, :], o_scales[32 * q : 32 * q + 4, :].bitcast(I32))

@@ -111,9 +111,6 @@ def tile_attend_gsink_u_pl_kernel(tc, uT, vT, su, sv, y, offs, qoffs, out_0, out
                 v_by_j[:, 2 * u : 2 * u + 2, :, :],
                 flat(turned[:]).bitcast(BF16).rearrange("s (r p e) -> s e p r", r=LANES, e=2),
             )
-        vj_codes = sbuf([P, SLOTS], U32, "vj_codes")
-        vj_scales = sbuf([P, SLOTS], U8, "vj_scales")
-        nc.vector.quantize_mx(vj_codes[:].bitcast(E4M3), vj_scales[:], v_by_j[:].rearrange("s t p r -> s (t p r)"))
 
         u_by_d = sbuf([P, SLOTS, LANES], BF16, "u_by_d")
         for t in range(LANES - 1):
@@ -130,9 +127,13 @@ def tile_attend_gsink_u_pl_kernel(tc, uT, vT, su, sv, y, offs, qoffs, out_0, out
             cols = slice(h * HALF, (h + 1) * HALF)
             nc.vector.quantize_mx(u_codes[:, cols].bitcast(E4M3), u_scales[:, cols], flat(u_by_d[:, cols, :]))
 
+        vj_codes = sbuf([P, SLOTS], U32, "vj_codes", tag="u_by_d")
+        vj_scales = sbuf([P, SLOTS], U8, "vj_scales")
+        nc.vector.quantize_mx(vj_codes[:].bitcast(E4M3), vj_scales[:], v_by_j[:].rearrange("s t p r -> s (t p r)"))
+
         scaled = [sbuf([P, LANES, P], F32, "scaled%d" % b) for b in range(LANES)]
         expd = [sbuf([P, SLOTS], F32, "expd%d" % b) for b in range(LANES)]
-        r1 = [sbuf([P, 2], F32, "r1_%d" % h) for h in range(2)]
+        r1 = [sbuf([P, 1], F32, "r1_%d" % b) for b in range(LANES)]
         for b in range(LANES):
             cols = slice(b * P, (b + 1) * P)
             score = bank(b, "score%d" % b)
@@ -148,7 +149,7 @@ def tile_attend_gsink_u_pl_kernel(tc, uT, vT, su, sv, y, offs, qoffs, out_0, out
             nc.vector.tensor_tensor(
                 scaled[b][:], flat(score[:]).rearrange("p (s r) -> p r s", r=LANES), sv_row[:], ALU.mult
             )
-            nc.scalar.activation(expd[b][:], flat(scaled[b][:]), ACT.Exp, scale=su_col[:, b : b + 1], accum_out=r1[b // 2][:, b % 2 : b % 2 + 1])
+            nc.scalar.activation(expd[b][:], flat(scaled[b][:]), ACT.Exp, scale=su_col[:, b : b + 1], accum_out=r1[b][:])
 
         y_turned = [bank(4 + r, "y_turned%d" % r) for r in range(LANES)]
         for b in range(LANES):
@@ -166,42 +167,56 @@ def tile_attend_gsink_u_pl_kernel(tc, uT, vT, su, sv, y, offs, qoffs, out_0, out
         def finish_y(r):
             nc.scalar.activation(y_both[r][:], flat(y_turned[r][:]), ACT.Copy, scale=sv_col[:, r : r + 1])
 
-        finish_y(0)
+        rinv = [sbuf([P, 1], F32, "rinv%d" % b) for b in range(LANES)]
+        f_even = [sbuf([P, SLOTS], F32, "f_even%d" % k) for k in range(2)]
+        f_pair = [[sbuf([P, HALF], F32, "f_pair%d_%d" % (k, h)) for h in range(2)] for k in range(2)]
+        sums_turned = [bank(2 + h, "sums_turned%d" % h) for h in range(2)]
+        for b in range(LANES):
+            nc.vector.reciprocal(rinv[b][:], r1[b][:])
+        for k in range(2):
+            nc.vector.tensor_scalar(f_even[k][:], expd[2 * k][:], rinv[2 * k][:], None, ALU.mult)
+        for k in range(2):
+            for h in range(2):
+                cols = slice(h * HALF, (h + 1) * HALF)
+                nc.vector.scalar_tensor_tensor(
+                    f_pair[k][h][:], expd[2 * k + 1][:, cols], rinv[2 * k + 1][:], f_even[k][:, cols], ALU.mult, ALU.add
+                )
+                for e in range(2):
+                    nc.tensor.matmul(
+                        sums_turned[h][:, e, :],
+                        f_pair[k][h][:, e * P : (e + 1) * P],
+                        ident[:],
+                        start=k == 0 and e == 0,
+                        stop=k == 1 and e == 1,
+                        is_transpose=True,
+                    )
+        c1 = [sbuf([P, 2], F32, "c1_%d" % h) for h in range(2)]
+        cinv = [sbuf([P, 2], F32, "cinv%d" % h) for h in range(2)]
+        csv = [sbuf([P, 2], F32, "csv%d" % h) for h in range(2)]
+        for h in range(2):
+            nc.vector.tensor_reduce(c1[h][:], sums_turned[h][:, 0:2, :], mybir.AxisListType.X, ALU.add)
+        for h in range(2):
+            nc.vector.reciprocal(cinv[h][:], c1[h][:])
+        for h in range(2):
+            nc.vector.tensor_tensor(csv[h][:], cinv[h][:], sv_col[:, 2 * h : 2 * h + 2], ALU.mult)
 
-        rinv_pair = [sbuf([P, 2], F32, "rinv%d" % h) for h in range(2)]
-        rinv = [rinv_pair[b // 2][:, b % 2 : b % 2 + 1] for b in range(LANES)]
-        rsu = [sbuf([P, 1], F32, "rsu%d" % b) for b in range(LANES)]
-        partial = [[sbuf([P, HALF], F32, "partial%d_%d" % (b, h)) for h in range(2)] for b in range(LANES)]
+        f_turned = [[None, None], [None, None]]
+        f_su = [sbuf([P, SLOTS], F32, "f_su%d" % b, tag="scaled%d" % b) for b in range(LANES)]
         for b in range(LANES):
             if b % 2 == 0:
-                nc.vector.reciprocal(rinv_pair[b // 2][:], r1[b // 2][:])
-            for h in range(2):
-                e_half = expd[b][:, h * HALF : (h + 1) * HALF]
-                if b == 0:
-                    nc.vector.tensor_scalar(partial[0][h][:], e_half, rinv[0], None, ALU.mult)
-                else:
-                    nc.vector.scalar_tensor_tensor(
-                        partial[b][h][:], e_half, rinv[b], partial[b - 1][h][:], ALU.mult, ALU.add
-                    )
-        sums_turned = bank(4, "sums_turned")
+                nc.scalar.activation(f_su[b][:], f_even[b // 2][:], ACT.Copy, scale=su_col[:, b : b + 1])
+            else:
+                nc.vector.tensor_scalar(f_su[b][:], expd[b][:], rinv[b][:], su_col[:, b : b + 1], ALU.mult, ALU.mult)
         for r in range(LANES):
-            nc.tensor.transpose(sums_turned[:, r, :], partial[LANES - 1][r // 2][:, r % 2 * P : (r % 2 + 1) * P], ident[:])
-        c1 = sbuf([P, LANES], F32, "c1")
-        nc.vector.tensor_reduce(c1[:], sums_turned[:], mybir.AxisListType.X, ALU.add)
-        cinv = sbuf([P, LANES], F32, "cinv")
-        nc.vector.reciprocal(cinv[:], c1[:])
-        csv = sbuf([P, LANES], F32, "csv")
-        nc.vector.tensor_tensor(csv[:], cinv[:], sv_col[:], ALU.mult)
-
-        f_turned = [bank(r, "f_turned%d" % r) for r in range(LANES)]
-        for b in range(LANES):
-            f_su = sbuf([P, SLOTS], F32, "f_su%d" % b, tag="scaled%d" % b)
-            nc.scalar.activation(rsu[b][:], rinv[b], ACT.Copy, scale=su_col[:, b : b + 1])
-            nc.scalar.activation(f_su[:], expd[b][:], ACT.Copy, scale=rsu[b][:])
-            for r in range(LANES):
-                nc.tensor.transpose(f_turned[r][:, b, :], f_su[:, r * P : (r + 1) * P], ident[:])
-        for r in range(1, LANES):
             finish_y(r)
+        for h in range(2):
+            for k in range(2):
+                f_turned[h][k] = bank(4 * h + k, "f_turned%d_%d" % (h, k))
+            for e in range(2):
+                for r in range(LANES):
+                    nc.tensor.transpose(
+                        f_turned[h][r // 2][:, 2 * (r % 2) + e, :], f_su[2 * h + e][:, r * P : (r + 1) * P], ident[:]
+                    )
 
         g_codes = sbuf([P, HALF + SLOTS], U32, "g_codes")
         g_scales = sbuf([P, HALF + SLOTS], U8, "g_scales")
@@ -214,8 +229,8 @@ def tile_attend_gsink_u_pl_kernel(tc, uT, vT, su, sv, y, offs, qoffs, out_0, out
             for r in range(LANES):
                 nc.vector.scalar_tensor_tensor(
                     g_planes[h][:, r, :],
-                    flat(f_turned[r][:])[:, cols],
-                    csv[:, r : r + 1],
+                    flat(f_turned[h][r // 2][:])[:, r % 2 * HALF : (r % 2 + 1) * HALF],
+                    csv[r // 2][:, r % 2 : r % 2 + 1],
                     y_both[r][:, cols],
                     ALU.mult,
                     ALU.subtract,
@@ -242,13 +257,13 @@ def tile_attend_gsink_u_pl_kernel(tc, uT, vT, su, sv, y, offs, qoffs, out_0, out
 
         quantise_g(0)
         du_early = sbuf([P, HALF], F32, "du_early")
-        nc.scalar.copy(du_early[:], product(0, 0, 4, "du_acc_early")[:, HALF:SLOTS])
+        nc.scalar.copy(du_early[:], product(0, 0, 2, "du_acc_early")[:, HALF:SLOTS])
         nc.vector.tensor_copy(g_by_j[1][:], g_planes[1][:].rearrange("s r i -> s i r"))
         quantise_g(1)
 
         out_rows = out_0.rearrange("(p t) c -> p t c", t=LANES)
         du = [sbuf([P, SLOTS], F32, "du%d" % t, tag="expd%d" % t) for t in range(LANES)]
-        nc.scalar.copy(du[0][:, HALF:SLOTS], product(0, HALF, 5, "du_acc0")[:, HALF:SLOTS])
+        nc.scalar.copy(du[0][:, HALF:SLOTS], product(0, HALF, 3, "du_acc0")[:, HALF:SLOTS])
         for t in range(1, LANES):
             nc.scalar.copy(du[t][:], product(t, HALF, (5 + t) % 8, "du_acc%d" % t))
         pairs = [sbuf([P, 2, w, 2], BF16, "pairs%d" % c) for c, w in enumerate(WIDTHS)]

@@ -223,7 +223,7 @@ def tile_attend_gsink_u_pl_kernel(tc, uT, vT, su, sv, y, offs, qoffs, out_0, out
         nc.vector.memset(g_codes[:, 0:HALF].bitcast(I32), 0)
         nc.vector.memset(g_scales[:, 0:HALF].bitcast(I32), 0)
         g_planes = [sbuf([P, LANES, HALF], BF16, "g_planes%d" % h) for h in range(2)]
-        g_by_j = [sbuf([P, HALF, LANES], BF16, "g_by_j%d" % h) for h in range(2)]
+        g_by_j = [sbuf([P, HALF, LANES], BF16, "g_by_j%d" % h, tag="g_by_j") for h in range(2)]
         for h in range(2):
             cols = slice(h * HALF, (h + 1) * HALF)
             for r in range(LANES):
@@ -235,7 +235,9 @@ def tile_attend_gsink_u_pl_kernel(tc, uT, vT, su, sv, y, offs, qoffs, out_0, out
                     ALU.mult,
                     ALU.subtract,
                 )
-        nc.scalar.copy(g_by_j[0][:], g_planes[0][:].rearrange("s r i -> s i r"))
+        nc.scalar.copy(
+            g_by_j[0][:].rearrange("s (c n) r -> s c r n", n=LANES), g_planes[0][:].rearrange("s r (c n) -> s c r n", n=LANES)
+        )
 
         def quantise_g(h):
             cols = slice((h + 1) * HALF, (h + 2) * HALF)
@@ -258,7 +260,9 @@ def tile_attend_gsink_u_pl_kernel(tc, uT, vT, su, sv, y, offs, qoffs, out_0, out
         quantise_g(0)
         du_early = sbuf([P, HALF], F32, "du_early")
         nc.scalar.copy(du_early[:], product(0, 0, 2, "du_acc_early")[:, HALF:SLOTS])
-        nc.vector.tensor_copy(g_by_j[1][:], g_planes[1][:].rearrange("s r i -> s i r"))
+        nc.vector.tensor_copy(
+            g_by_j[1][:].rearrange("s (c n) r -> s c r n", n=LANES), g_planes[1][:].rearrange("s r (c n) -> s c r n", n=LANES)
+        )
         quantise_g(1)
 
         out_rows = out_0.rearrange("(p t) c -> p t c", t=LANES)

@@ -23,6 +23,7 @@ SLOTS = 512
 HALF = SLOTS // 2
 WIDTHS = (256, 512, 512, 256, 256, 256)
 ON_VECTOR = 4
+ORDER = (0, 2, 1, 3)
 STARTS = [sum(WIDTHS[:c]) for c in range(len(WIDTHS))]
 
 
@@ -151,7 +152,7 @@ def tile_attend_gsink_u_pl_kernel(tc, uT, vT, su, sv, y, offs, qoffs, out_0, out
             )
             nc.scalar.activation(expd[b][:], flat(scaled[b][:]), ACT.Exp, scale=su_col[:, b : b + 1], accum_out=r1[b][:])
 
-        y_turned = [bank(4 + r, "y_turned%d" % r) for r in range(LANES)]
+        y_turned = [[bank(4 + 2 * h + k, "y_turned%d_%d" % (h, k)) for k in range(2)] for h in range(2)]
         for b in range(LANES):
             y_su = sbuf([P, LANES, P], F32, "y_su%d" % b)
             nc.scalar.activation(
@@ -161,11 +162,13 @@ def tile_attend_gsink_u_pl_kernel(tc, uT, vT, su, sv, y, offs, qoffs, out_0, out
                 scale=su_col[:, b : b + 1],
             )
             for r in range(LANES):
-                nc.tensor.transpose(y_turned[r][:, b, :], y_su[:, r, :], ident[:])
-        y_both = [sbuf([P, SLOTS], F32, "y_both%d" % r, tag="y%d" % r) for r in range(LANES)]
+                nc.tensor.transpose(y_turned[b // 2][r // 2][:, 2 * (r % 2) + b % 2, :], y_su[:, r, :], ident[:])
+        y_both = [[sbuf([P, HALF], F32, "y_both%d_%d" % (h, r)) for r in range(LANES)] for h in range(2)]
 
-        def finish_y(r):
-            nc.scalar.activation(y_both[r][:], flat(y_turned[r][:]), ACT.Copy, scale=sv_col[:, r : r + 1])
+        def finish_y(h):
+            for r in range(LANES):
+                turned_y = flat(y_turned[h][r // 2][:])[:, r % 2 * HALF : (r % 2 + 1) * HALF]
+                nc.scalar.activation(y_both[h][r][:], turned_y, ACT.Copy, scale=sv_col[:, r : r + 1])
 
         rinv = [sbuf([P, 1], F32, "rinv%d" % b) for b in range(LANES)]
         f_even = [sbuf([P, SLOTS], F32, "f_even%d" % k) for k in range(2)]
@@ -201,14 +204,15 @@ def tile_attend_gsink_u_pl_kernel(tc, uT, vT, su, sv, y, offs, qoffs, out_0, out
             nc.vector.tensor_tensor(csv[h][:], cinv[h][:], sv_col[:, 2 * h : 2 * h + 2], ALU.mult)
 
         f_turned = [[None, None], [None, None]]
-        f_su = [sbuf([P, SLOTS], F32, "f_su%d" % b, tag="scaled%d" % b) for b in range(LANES)]
+        f_su = [sbuf([P, SLOTS], F32, "f_su%d" % b, tag="scaled%d" % b if b < 3 else "f_pair1_1") for b in range(LANES)]
         for b in range(LANES):
+            if b == 2:
+                finish_y(0)
             if b % 2 == 0:
                 nc.scalar.activation(f_su[b][:], f_even[b // 2][:], ACT.Copy, scale=su_col[:, b : b + 1])
             else:
                 nc.vector.tensor_scalar(f_su[b][:], expd[b][:], rinv[b][:], su_col[:, b : b + 1], ALU.mult, ALU.mult)
-        for r in range(LANES):
-            finish_y(r)
+        finish_y(1)
         for h in range(2):
             for k in range(2):
                 f_turned[h][k] = bank(4 * h + k, "f_turned%d_%d" % (h, k))
@@ -223,7 +227,8 @@ def tile_attend_gsink_u_pl_kernel(tc, uT, vT, su, sv, y, offs, qoffs, out_0, out
         nc.vector.memset(g_codes[:, 0:HALF].bitcast(I32), 0)
         nc.vector.memset(g_scales[:, 0:HALF].bitcast(I32), 0)
         g_planes = [sbuf([P, LANES, HALF], BF16, "g_planes%d" % h) for h in range(2)]
-        g_by_j = [sbuf([P, HALF, LANES], BF16, "g_by_j%d" % h, tag="g_by_j") for h in range(2)]
+        g_first = sbuf([P, HALF, LANES], BF16, "g_first")
+        g_rest = [sbuf([P, P, LANES], BF16, "g_rest0"), sbuf([P, P, LANES], BF16, "g_rest1", tag="g_first")]
         for h in range(2):
             cols = slice(h * HALF, (h + 1) * HALF)
             for r in range(LANES):
@@ -231,17 +236,17 @@ def tile_attend_gsink_u_pl_kernel(tc, uT, vT, su, sv, y, offs, qoffs, out_0, out
                     g_planes[h][:, r, :],
                     flat(f_turned[h][r // 2][:])[:, r % 2 * HALF : (r % 2 + 1) * HALF],
                     csv[r // 2][:, r % 2 : r % 2 + 1],
-                    y_both[r][:, cols],
+                    y_both[h][r][:],
                     ALU.mult,
                     ALU.subtract,
                 )
         nc.scalar.copy(
-            g_by_j[0][:].rearrange("s (c n) r -> s c r n", n=LANES), g_planes[0][:].rearrange("s r (c n) -> s c r n", n=LANES)
+            g_first[:].rearrange("s (c n) r -> s c r n", n=LANES), g_planes[0][:].rearrange("s r (c n) -> s c r n", n=LANES)
         )
 
-        def quantise_g(h):
-            cols = slice((h + 1) * HALF, (h + 2) * HALF)
-            nc.vector.quantize_mx(g_codes[:, cols].bitcast(E5M2), g_scales[:, cols], flat(g_by_j[h][:]))
+        def quantise_g(first, woven):
+            cols = slice(HALF + first, HALF + first + woven.shape[1])
+            nc.vector.quantize_mx(g_codes[:, cols].bitcast(E5M2), g_scales[:, cols], flat(woven))
 
         def product(t, first, n, name):
             cols = slice(t * P, (t + 1) * P)
@@ -257,29 +262,36 @@ def tile_attend_gsink_u_pl_kernel(tc, uT, vT, su, sv, y, offs, qoffs, out_0, out
             )
             return flat(acc[:])
 
-        quantise_g(0)
+        quantise_g(0, g_first[:])
+        for e, copy in enumerate((nc.scalar.copy, nc.vector.tensor_copy)):
+            copy(
+                g_rest[e][:].rearrange("s (c n) r -> s c r n", n=LANES),
+                g_planes[1][:, :, e * P : (e + 1) * P].rearrange("s r (c n) -> s c r n", n=LANES),
+            )
         du_early = sbuf([P, HALF], F32, "du_early")
         nc.scalar.copy(du_early[:], product(0, 0, 2, "du_acc_early")[:, HALF:SLOTS])
-        nc.vector.tensor_copy(
-            g_by_j[1][:].rearrange("s (c n) r -> s c r n", n=LANES), g_planes[1][:].rearrange("s r (c n) -> s c r n", n=LANES)
-        )
-        quantise_g(1)
+        for e in range(2):
+            quantise_g(HALF + e * P, g_rest[e][:])
 
         out_rows = out_0.rearrange("(p t) c -> p t c", t=LANES)
         du = [sbuf([P, SLOTS], F32, "du%d" % t, tag="expd%d" % t) for t in range(LANES)]
         nc.scalar.copy(du[0][:, HALF:SLOTS], product(0, HALF, 3, "du_acc0")[:, HALF:SLOTS])
         for t in range(1, LANES):
-            nc.scalar.copy(du[t][:], product(t, HALF, (5 + t) % 8, "du_acc%d" % t))
+            nc.scalar.copy(du[t][:], product(ORDER[t], HALF, (5 + t) % 8, "du_acc%d" % t))
         pairs = [sbuf([P, 2, w, 2], BF16, "pairs%d" % c) for c, w in enumerate(WIDTHS)]
-        for t in range(LANES):
+        for n, t in enumerate(ORDER):
             if t == 0:
                 nc.vector.tensor_copy(window[0][:].indirect(ilist[:, 0 : HALF // 16]), du_early[:])
                 nc.vector.tensor_copy(window[0][:].indirect(ilist[:, HALF // 16 : SLOTS // 16]), du[0][:, HALF:SLOTS])
             else:
-                nc.vector.tensor_copy(window[t][:].indirect(ilist[:]), du[t][:])
+                nc.vector.tensor_copy(window[t][:].indirect(ilist[:]), du[n][:])
             nc.sync.dma_start(out_rows[:, t, :], window[t][:])
             for c, w in enumerate(WIDTHS):
-                nc.scalar.copy(pairs[c][:, t // 2, :, t % 2], window[t][:, STARTS[c] : STARTS[c] + w])
+                src = window[t][:, STARTS[c] : STARTS[c] + w]
+                if c >= ON_VECTOR and t < 2:
+                    nc.gpsimd.tensor_scalar(pairs[c][:, 0, :, t], src, 1.0, 0.0, ALU.mult, ALU.add)
+                else:
+                    nc.scalar.copy(pairs[c][:, t // 2, :, t % 2], src)
 
         o_codes = sbuf([P, POOL], U32, "o_codes", tag="v_pool0")
         o_scales = sbuf([P, POOL], U8, "o_scales")

@@ -21,10 +21,17 @@ LANES = 4
 POOL = 2048
 SLOTS = 512
 HALF = SLOTS // 2
-WIDTHS = (256, 512, 512, 256, 256, 256)
-ON_VECTOR = 4
-ORDER = (0, 2, 1, 3)
+HALF_LIST = HALF // 16
+RUN = 4
+
+ORDER = (2, 0, 1, 3)
+WINDOWS = 3
+EARLY = 2
+
+WIDTHS = (512, 256, 512, 256, 256, 256)
+DIRECT = 2
 STARTS = [sum(WIDTHS[:c]) for c in range(len(WIDTHS))]
+STORE_AFTER = (1, 2, 4, 5)
 
 
 def tile_attend_gsink_u_pl_kernel(tc, uT, vT, su, sv, y, offs, qoffs, out_0, out_1, out_2):
@@ -37,11 +44,14 @@ def tile_attend_gsink_u_pl_kernel(tc, uT, vT, su, sv, y, offs, qoffs, out_0, out
         def sbuf(shape, dtype, name, tag=None):
             return sb.tile(shape, dtype, name=name, tag=tag or name, align_bytes=64)
 
-        def bank(n, name):
-            return ps.tile([P, LANES, P], F32, name=name, tag="bank%d" % n)
+        def bank(number, name):
+            return ps.tile([P, LANES, P], F32, name=name, tag="bank%d" % number)
 
         def flat(ap):
             return ap.rearrange("p a b -> p (a b)")
+
+        def round_on_gpsimd(dst, src):
+            nc.gpsimd.tensor_scalar(dst, src, 1.0, 0.0, ALU.mult, ALU.add)
 
         jlist = lists.tile([P, SLOTS // 16], U16, name="jlist")
         ilist = lists.tile([P, SLOTS // 16], U16, name="ilist")
@@ -69,16 +79,16 @@ def tile_attend_gsink_u_pl_kernel(tc, uT, vT, su, sv, y, offs, qoffs, out_0, out
         ident = sbuf([P, P], F32, "ident")
         make_identity(nc, ident[:])
 
-        window = [sbuf([P, POOL], F32, "window%d" % t) for t in range(LANES)]
-        for t in range(LANES):
-            nc.vector.memset(window[t][:], 0.0)
+        window = [sbuf([P, POOL], F32, "window%d" % w) for w in range(WINDOWS)]
+        for w in range(WINDOWS):
+            nc.vector.memset(window[w][:], 0.0)
 
         v_planes = sbuf([P, LANES, SLOTS], BF16, "v_planes")
         for t in range(LANES):
             nc.vector.tensor_copy(v_planes[:, t, :], v_pool[t][:].indirect(jlist[:]))
         v_by_d = sbuf([P, SLOTS, LANES], BF16, "v_by_d")
         nc.scalar.copy(v_by_d[:], v_planes[:].rearrange("p t j -> p j t"))
-        vd_codes = sbuf([P, SLOTS], U32, "vd_codes")
+        vd_codes = sbuf([P, SLOTS], U32, "vd_codes", tag="u_pool1")
         vd_scales = sbuf([P, SLOTS], U8, "vd_scales")
         nc.vector.quantize_mx(vd_codes[:].bitcast(E4M3), vd_scales[:], flat(v_by_d[:]))
 
@@ -104,13 +114,13 @@ def tile_attend_gsink_u_pl_kernel(tc, uT, vT, su, sv, y, offs, qoffs, out_0, out
 
         v_words = flat(v_by_d[:]).bitcast(F32)
         v_by_j = sbuf([P, LANES, P, LANES], BF16, "v_by_j")
-        for u in range(2):
-            turned = bank(4 + u, "v_turned%d" % u)
+        for pair in range(2):
+            v_turned = bank(4 + pair, "v_turned%d" % pair)
             for r in range(LANES):
-                nc.tensor.transpose(turned[:, r, :], v_words[:, 2 * r + u :: 2 * LANES], ident[:])
+                nc.tensor.transpose(v_turned[:, r, :], v_words[:, 2 * r + pair :: 2 * LANES], ident[:])
             nc.scalar.copy(
-                v_by_j[:, 2 * u : 2 * u + 2, :, :],
-                flat(turned[:]).bitcast(BF16).rearrange("s (r p e) -> s e p r", r=LANES, e=2),
+                v_by_j[:, 2 * pair : 2 * pair + 2, :, :],
+                flat(v_turned[:]).bitcast(BF16).rearrange("s (r p e) -> s e p r", r=LANES, e=2),
             )
 
         u_by_d = sbuf([P, SLOTS, LANES], BF16, "u_by_d")
@@ -119,10 +129,9 @@ def tile_attend_gsink_u_pl_kernel(tc, uT, vT, su, sv, y, offs, qoffs, out_0, out
         u_codes = sbuf([P, SLOTS], U32, "u_codes")
         u_scales = sbuf([P, SLOTS], U8, "u_scales")
         for h in range(2):
-            cols = slice(h * HALF, (h + 1) * HALF)
             nc.vector.tensor_copy(
-                u_by_d[:, cols, LANES - 1],
-                u_pool[LANES - 1][:].indirect(ilist[:, h * HALF // 16 : (h + 1) * HALF // 16]),
+                u_by_d[:, h * HALF : (h + 1) * HALF, LANES - 1],
+                u_pool[LANES - 1][:].indirect(ilist[:, h * HALF_LIST : (h + 1) * HALF_LIST]),
             )
         for h in range(2):
             cols = slice(h * HALF, (h + 1) * HALF)
@@ -152,6 +161,12 @@ def tile_attend_gsink_u_pl_kernel(tc, uT, vT, su, sv, y, offs, qoffs, out_0, out
             )
             nc.scalar.activation(expd[b][:], flat(scaled[b][:]), ACT.Exp, scale=su_col[:, b : b + 1], accum_out=r1[b][:])
 
+        def quarter(banks, r, b):
+            return banks[r // 2][:, 2 * (r % 2) + b % 2, :]
+
+        def lane_of(banks, r):
+            return flat(banks[r // 2][:])[:, r % 2 * HALF : (r % 2 + 1) * HALF]
+
         y_turned = [[bank(4 + 2 * h + k, "y_turned%d_%d" % (h, k)) for k in range(2)] for h in range(2)]
         for b in range(LANES):
             y_su = sbuf([P, LANES, P], F32, "y_su%d" % b)
@@ -162,13 +177,12 @@ def tile_attend_gsink_u_pl_kernel(tc, uT, vT, su, sv, y, offs, qoffs, out_0, out
                 scale=su_col[:, b : b + 1],
             )
             for r in range(LANES):
-                nc.tensor.transpose(y_turned[b // 2][r // 2][:, 2 * (r % 2) + b % 2, :], y_su[:, r, :], ident[:])
+                nc.tensor.transpose(quarter(y_turned[b // 2], r, b), y_su[:, r, :], ident[:])
         y_both = [[sbuf([P, HALF], F32, "y_both%d_%d" % (h, r)) for r in range(LANES)] for h in range(2)]
 
         def finish_y(h):
             for r in range(LANES):
-                turned_y = flat(y_turned[h][r // 2][:])[:, r % 2 * HALF : (r % 2 + 1) * HALF]
-                nc.scalar.activation(y_both[h][r][:], turned_y, ACT.Copy, scale=sv_col[:, r : r + 1])
+                nc.scalar.activation(y_both[h][r][:], lane_of(y_turned[h], r), ACT.Copy, scale=sv_col[:, r : r + 1])
 
         rinv = [sbuf([P, 1], F32, "rinv%d" % b) for b in range(LANES)]
         f_even = [sbuf([P, SLOTS], F32, "f_even%d" % k) for k in range(2)]
@@ -203,54 +217,52 @@ def tile_attend_gsink_u_pl_kernel(tc, uT, vT, su, sv, y, offs, qoffs, out_0, out
         for h in range(2):
             nc.vector.tensor_tensor(csv[h][:], cinv[h][:], sv_col[:, 2 * h : 2 * h + 2], ALU.mult)
 
-        f_turned = [[None, None], [None, None]]
-        f_su = [sbuf([P, SLOTS], F32, "f_su%d" % b, tag="scaled%d" % b if b < 3 else "f_pair1_1") for b in range(LANES)]
-        for b in range(LANES):
-            if b == 2:
-                finish_y(0)
-            if b % 2 == 0:
-                nc.scalar.activation(f_su[b][:], f_even[b // 2][:], ACT.Copy, scale=su_col[:, b : b + 1])
-            else:
-                nc.vector.tensor_scalar(f_su[b][:], expd[b][:], rinv[b][:], su_col[:, b : b + 1], ALU.mult, ALU.mult)
-        finish_y(1)
+        f_tags = ["scaled0", "scaled1", "scaled2", "f_pair1_1"]
+        f_su = [sbuf([P, SLOTS], F32, "f_su%d" % b, tag=f_tags[b]) for b in range(LANES)]
         for h in range(2):
-            for k in range(2):
-                f_turned[h][k] = bank(4 * h + k, "f_turned%d_%d" % (h, k))
-            for e in range(2):
+            even, odd = 2 * h, 2 * h + 1
+            nc.scalar.activation(f_su[even][:], f_even[h][:], ACT.Copy, scale=su_col[:, even : even + 1])
+            nc.vector.tensor_scalar(f_su[odd][:], expd[odd][:], rinv[odd][:], su_col[:, odd : odd + 1], ALU.mult, ALU.mult)
+            finish_y(h)
+        f_turned = []
+        for h in range(2):
+            f_turned.append([bank(4 * h + k, "f_turned%d_%d" % (h, k)) for k in range(2)])
+            for b in (2 * h, 2 * h + 1):
                 for r in range(LANES):
-                    nc.tensor.transpose(
-                        f_turned[h][r // 2][:, 2 * (r % 2) + e, :], f_su[2 * h + e][:, r * P : (r + 1) * P], ident[:]
-                    )
+                    nc.tensor.transpose(quarter(f_turned[h], r, b), f_su[b][:, r * P : (r + 1) * P], ident[:])
 
         g_codes = sbuf([P, HALF + SLOTS], U32, "g_codes")
         g_scales = sbuf([P, HALF + SLOTS], U8, "g_scales")
         nc.vector.memset(g_codes[:, 0:HALF].bitcast(I32), 0)
         nc.vector.memset(g_scales[:, 0:HALF].bitcast(I32), 0)
         g_planes = [sbuf([P, LANES, HALF], BF16, "g_planes%d" % h) for h in range(2)]
-        g_first = sbuf([P, HALF, LANES], BF16, "g_first")
-        g_rest = [sbuf([P, P, LANES], BF16, "g_rest0"), sbuf([P, P, LANES], BF16, "g_rest1", tag="g_first")]
-        for h in range(2):
-            cols = slice(h * HALF, (h + 1) * HALF)
+        g_by_j = [sbuf([P, HALF, LANES], BF16, "g_by_j%d" % h) for h in range(2)]
+
+        def form_g(h):
             for r in range(LANES):
                 nc.vector.scalar_tensor_tensor(
                     g_planes[h][:, r, :],
-                    flat(f_turned[h][r // 2][:])[:, r % 2 * HALF : (r % 2 + 1) * HALF],
+                    lane_of(f_turned[h], r),
                     csv[r // 2][:, r % 2 : r % 2 + 1],
                     y_both[h][r][:],
                     ALU.mult,
                     ALU.subtract,
                 )
-        nc.scalar.copy(
-            g_first[:].rearrange("s (c n) r -> s c r n", n=LANES), g_planes[0][:].rearrange("s r (c n) -> s c r n", n=LANES)
-        )
 
-        def quantise_g(first, woven):
-            cols = slice(HALF + first, HALF + first + woven.shape[1])
-            nc.vector.quantize_mx(g_codes[:, cols].bitcast(E5M2), g_scales[:, cols], flat(woven))
+        def weave_g(h):
+            nc.scalar.copy(
+                g_by_j[h][:, 0:P, :].rearrange("s (c n) r -> s c r n", n=RUN),
+                g_planes[h][:, :, 0:P].rearrange("s r (c n) -> s c r n", n=RUN),
+            )
+            round_on_gpsimd(g_by_j[h][:, P:HALF, :], g_planes[h][:, :, P:HALF].rearrange("s r c -> s c r"))
 
-        def product(t, first, n, name):
+        def quantise_g(h):
+            cols = slice((h + 1) * HALF, (h + 2) * HALF)
+            nc.vector.quantize_mx(g_codes[:, cols].bitcast(E5M2), g_scales[:, cols], flat(g_by_j[h][:]))
+
+        def product(t, first, number, name):
             cols = slice(t * P, (t + 1) * P)
-            acc = bank(n, name)
+            acc = bank(number, name)
             nc.tensor.matmul_mx(
                 flat(acc[:]),
                 lhsT=vj_codes[:, cols].bitcast(E4M3),
@@ -262,62 +274,70 @@ def tile_attend_gsink_u_pl_kernel(tc, uT, vT, su, sv, y, offs, qoffs, out_0, out
             )
             return flat(acc[:])
 
-        quantise_g(0, g_first[:])
-        for e, copy in enumerate((nc.scalar.copy, nc.vector.tensor_copy)):
-            copy(
-                g_rest[e][:].rearrange("s (c n) r -> s c r n", n=LANES),
-                g_planes[1][:, :, e * P : (e + 1) * P].rearrange("s r (c n) -> s c r n", n=LANES),
-            )
-        du_early = sbuf([P, HALF], F32, "du_early")
-        nc.scalar.copy(du_early[:], product(0, 0, 2, "du_acc_early")[:, HALF:SLOTS])
-        for e in range(2):
-            quantise_g(HALF + e * P, g_rest[e][:])
+        def early_pass(n):
+            nc.scalar.copy(du_early[n][:], product(ORDER[n], 0, 2 + n, "du_acc_early%d" % n)[:, HALF:SLOTS])
+
+        def early_scatter(n):
+            nc.vector.tensor_copy(window[n][:].indirect(ilist[:, 0:HALF_LIST]), du_early[n][:])
+
+        du_early = [sbuf([P, HALF], F32, "du_early%d" % n) for n in range(EARLY)]
+        form_g(0)
+        weave_g(0)
+        quantise_g(0)
+        form_g(1)
+        early_pass(0)
+        weave_g(1)
+        early_pass(1)
+        early_scatter(0)
+        quantise_g(1)
+        early_scatter(1)
 
         out_rows = out_0.rearrange("(p t) c -> p t c", t=LANES)
-        du = [sbuf([P, SLOTS], F32, "du%d" % t, tag="expd%d" % t) for t in range(LANES)]
-        nc.scalar.copy(du[0][:, HALF:SLOTS], product(0, HALF, 3, "du_acc0")[:, HALF:SLOTS])
-        for t in range(1, LANES):
-            nc.scalar.copy(du[t][:], product(ORDER[t], HALF, (5 + t) % 8, "du_acc%d" % t))
-        pairs = [sbuf([P, 2, w, 2], BF16, "pairs%d" % c) for c, w in enumerate(WIDTHS)]
+        left = [slice(HALF if n < EARLY else 0, SLOTS) for n in range(LANES)]
+        du = [sbuf([P, SLOTS], F32, "du%d" % n, tag="expd%d" % n) for n in range(LANES)]
+        for n, number in enumerate((0, 1, 6, 7)):
+            nc.scalar.copy(du[n][:, left[n]], product(ORDER[n], HALF, number, "du_acc%d" % n)[:, left[n]])
+
+        spare = ["u_pool0", "u_pool1", "u_pool2", "u_pool3", "v_pool1", "v_pool2"]
+        o_by_d = [sbuf([P, width, LANES], BF16, "o_by_d%d" % c, tag=spare[c]) for c, width in enumerate(WIDTHS)]
+        paired = STARTS[DIRECT]
+        pairs = sbuf([P, 2, POOL - paired, 2], BF16, "pairs")
         for n, t in enumerate(ORDER):
-            if t == 0:
-                nc.vector.tensor_copy(window[0][:].indirect(ilist[:, 0 : HALF // 16]), du_early[:])
-                nc.vector.tensor_copy(window[0][:].indirect(ilist[:, HALF // 16 : SLOTS // 16]), du[0][:, HALF:SLOTS])
+            target = window[n % WINDOWS]
+            last = n == LANES - 1
+            entries = ilist[:, HALF_LIST : 2 * HALF_LIST] if n < EARLY else ilist[:]
+            nc.vector.tensor_copy(target[:].indirect(entries), du[n][:, left[n]])
+            nc.sync.dma_start(out_rows[:, t, :], target[:])
+            for c in range(DIRECT):
+                copy = nc.vector.tensor_copy if last else nc.scalar.copy
+                copy(o_by_d[c][:, :, t], target[:, STARTS[c] : STARTS[c] + WIDTHS[c]])
+            if last:
+                for c in range(DIRECT, len(WIDTHS)):
+                    at = STARTS[c] - paired
+                    nc.scalar.copy(pairs[:, t // 2, at : at + WIDTHS[c], t % 2], target[:, STARTS[c] : STARTS[c] + WIDTHS[c]])
             else:
-                nc.vector.tensor_copy(window[t][:].indirect(ilist[:]), du[n][:])
-            nc.sync.dma_start(out_rows[:, t, :], window[t][:])
-            for c, w in enumerate(WIDTHS):
-                src = window[t][:, STARTS[c] : STARTS[c] + w]
-                if c >= ON_VECTOR and t < 2:
-                    nc.gpsimd.tensor_scalar(pairs[c][:, 0, :, t], src, 1.0, 0.0, ALU.mult, ALU.add)
-                else:
-                    nc.scalar.copy(pairs[c][:, t // 2, :, t % 2], src)
+                round_on_gpsimd(pairs[:, t // 2, :, t % 2], target[:, paired:POOL])
 
         o_codes = sbuf([P, POOL], U32, "o_codes", tag="v_pool0")
         o_scales = sbuf([P, POOL], U8, "o_scales")
         words_out = out_1.rearrange("a p c l -> p (a c l)").bitcast(I32)
         scales_out = out_2.rearrange("a q c -> q (a c)").bitcast(I32)
-        spare = ["u_pool0", "u_pool1", "u_pool2", "u_pool3", "v_pool1", "v_pool2"]
-        o_by_d = [sbuf([P, w * LANES], BF16, "o_by_d%d" % c, tag=spare[c]) for c, w in enumerate(WIDTHS)]
+        pair_words = pairs[:].rearrange("p u c e -> p (u c e)").bitcast(F32).rearrange("p (u c) -> p c u", u=2)
 
-        def weave(c):
-            dst = o_by_d[c][:].bitcast(F32).rearrange("p (c u) -> p c u", u=2)
-            src = pairs[c][:].rearrange("p u c e -> p (u c e)").bitcast(F32).rearrange("p (u c) -> p c u", u=2)
-            if c < ON_VECTOR:
-                nc.vector.tensor_copy(dst, src)
-            else:
-                nc.scalar.copy(dst, src)
+        def weave_out(c):
+            at = STARTS[c] - paired
+            copy = nc.vector.tensor_copy if c == DIRECT else nc.scalar.copy
+            copy(flat(o_by_d[c][:]).bitcast(F32).rearrange("p (c u) -> p c u", u=2), pair_words[:, at : at + WIDTHS[c], :])
 
-        def quantise_out(c):
+        stored = 0
+        for c in range(len(WIDTHS)):
+            if DIRECT <= c + 1 < len(WIDTHS):
+                weave_out(c + 1)
             cols = slice(STARTS[c], STARTS[c] + WIDTHS[c])
-            nc.vector.quantize_mx(o_codes[:, cols].bitcast(E4M3), o_scales[:, cols], o_by_d[c][:])
-            nc.sync.dma_start(words_out[:, cols], o_codes[:, cols].bitcast(I32))
-
-        weave(0)
-        for c in range(1, len(WIDTHS)):
-            weave(c)
-            quantise_out(c - 1)
-        quantise_out(len(WIDTHS) - 1)
+            nc.vector.quantize_mx(o_codes[:, cols].bitcast(E4M3), o_scales[:, cols], flat(o_by_d[c][:]))
+            if c in STORE_AFTER:
+                nc.sync.dma_start(words_out[:, stored : cols.stop], o_codes[:, stored : cols.stop].bitcast(I32))
+                stored = cols.stop
         for q in range(4):
             queue = nc.scalar if q % 2 else nc.sync
             queue.dma_start(scales_out[4 * q : 4 * q + 4, :], o_scales[32 * q : 32 * q + 4, :].bitcast(I32))

@@ -24,14 +24,11 @@ HALF = SLOTS // 2
 HALF_LIST = HALF // 16
 RUN = 4
 
-ORDER = (2, 0, 1, 3)
-WINDOWS = 3
-EARLY = 2
-
-WIDTHS = (512, 256, 512, 256, 256, 256)
-DIRECT = 2
+WIDTHS = (256, 512, 512, 512, 256)
+LOWER_ON_GPSIMD = 3
 STARTS = [sum(WIDTHS[:c]) for c in range(len(WIDTHS))]
-STORE_AFTER = (1, 2, 4, 5)
+ON_VECTOR = (0, 4)
+STORE_AFTER = (2, 3, 4)
 
 
 def tile_attend_gsink_u_pl_kernel(tc, uT, vT, su, sv, y, offs, qoffs, out_0, out_1, out_2):
@@ -79,13 +76,13 @@ def tile_attend_gsink_u_pl_kernel(tc, uT, vT, su, sv, y, offs, qoffs, out_0, out
         ident = sbuf([P, P], F32, "ident")
         make_identity(nc, ident[:])
 
-        window = [sbuf([P, POOL], F32, "window%d" % w) for w in range(WINDOWS)]
-        for w in range(WINDOWS):
+        window = [sbuf([P, POOL], F32, "window%d" % w) for w in range(LANES)]
+        for w in range(LANES):
             nc.vector.memset(window[w][:], 0.0)
 
         v_planes = sbuf([P, LANES, SLOTS], BF16, "v_planes")
         for t in range(LANES):
-            nc.vector.tensor_copy(v_planes[:, t, :], v_pool[t][:].indirect(jlist[:]))
+            nc.scalar.activation(v_planes[:, t, :], v_pool[t][:].indirect(jlist[:]), ACT.Copy)
         v_by_d = sbuf([P, SLOTS, LANES], BF16, "v_by_d")
         nc.scalar.copy(v_by_d[:], v_planes[:].rearrange("p t j -> p j t"))
         vd_codes = sbuf([P, SLOTS], U32, "vd_codes", tag="u_pool1")
@@ -231,10 +228,8 @@ def tile_attend_gsink_u_pl_kernel(tc, uT, vT, su, sv, y, offs, qoffs, out_0, out
                 for r in range(LANES):
                     nc.tensor.transpose(quarter(f_turned[h], r, b), f_su[b][:, r * P : (r + 1) * P], ident[:])
 
-        g_codes = sbuf([P, HALF + SLOTS], U32, "g_codes")
-        g_scales = sbuf([P, HALF + SLOTS], U8, "g_scales")
-        nc.vector.memset(g_codes[:, 0:HALF].bitcast(I32), 0)
-        nc.vector.memset(g_scales[:, 0:HALF].bitcast(I32), 0)
+        g_codes = sbuf([P, SLOTS], U32, "g_codes")
+        g_scales = sbuf([P, SLOTS], U8, "g_scales")
         g_planes = [sbuf([P, LANES, HALF], BF16, "g_planes%d" % h) for h in range(2)]
         g_by_j = [sbuf([P, HALF, LANES], BF16, "g_by_j%d" % h) for h in range(2)]
 
@@ -257,81 +252,91 @@ def tile_attend_gsink_u_pl_kernel(tc, uT, vT, su, sv, y, offs, qoffs, out_0, out
             round_on_gpsimd(g_by_j[h][:, P:HALF, :], g_planes[h][:, :, P:HALF].rearrange("s r c -> s c r"))
 
         def quantise_g(h):
-            cols = slice((h + 1) * HALF, (h + 2) * HALF)
+            cols = slice(h * HALF, (h + 1) * HALF)
             nc.vector.quantize_mx(g_codes[:, cols].bitcast(E5M2), g_scales[:, cols], flat(g_by_j[h][:]))
 
-        def product(t, first, number, name):
+        du = [sbuf([P, SLOTS], F32, "du%d" % t, tag="expd%d" % t) for t in range(LANES)]
+        out_rows = out_0.rearrange("(p t) c -> p t c", t=LANES)
+
+        def product(t, sources, number):
             cols = slice(t * P, (t + 1) * P)
-            acc = bank(number, name)
+            acc = flat(bank(number, "du_acc%d_%d" % (t, sources.start))[:])[:, 0 : sources.stop - sources.start]
             nc.tensor.matmul_mx(
-                flat(acc[:]),
+                acc,
                 lhsT=vj_codes[:, cols].bitcast(E4M3),
                 lhsT_scale=vj_scales[:, cols],
-                rhs=g_codes[:, first : first + SLOTS].bitcast(E5M2),
-                rhs_scale=g_scales[:, first : first + SLOTS],
+                rhs=g_codes[:, sources].bitcast(E5M2),
+                rhs_scale=g_scales[:, sources],
                 start=True,
                 stop=True,
             )
-            return flat(acc[:])
+            copy = nc.vector.tensor_copy if t % 2 else nc.scalar.copy
+            copy(du[t][:, sources], acc)
 
-        def early_pass(n):
-            nc.scalar.copy(du_early[n][:], product(ORDER[n], 0, 2 + n, "du_acc_early%d" % n)[:, HALF:SLOTS])
+        def scatter(t, sources):
+            target = window[t][:].indirect(ilist[:, sources.start // 16 : sources.stop // 16])
+            if t % 2:
+                nc.vector.tensor_copy(target, du[t][:, sources])
+            else:
+                nc.scalar.activation(target, du[t][:, sources], ACT.Copy)
 
-        def early_scatter(n):
-            nc.vector.tensor_copy(window[n][:].indirect(ilist[:, 0:HALF_LIST]), du_early[n][:])
-
-        du_early = [sbuf([P, HALF], F32, "du_early%d" % n) for n in range(EARLY)]
+        halves = [slice(h * HALF, (h + 1) * HALF) for h in range(2)]
+        whole = slice(0, SLOTS)
         form_g(0)
         weave_g(0)
         quantise_g(0)
         form_g(1)
-        early_pass(0)
         weave_g(1)
-        early_pass(1)
-        early_scatter(0)
+        product(0, halves[0], 2)
         quantise_g(1)
-        early_scatter(1)
-
-        out_rows = out_0.rearrange("(p t) c -> p t c", t=LANES)
-        left = [slice(HALF if n < EARLY else 0, SLOTS) for n in range(LANES)]
-        du = [sbuf([P, SLOTS], F32, "du%d" % n, tag="expd%d" % n) for n in range(LANES)]
-        for n, number in enumerate((0, 1, 6, 7)):
-            nc.scalar.copy(du[n][:, left[n]], product(ORDER[n], HALF, number, "du_acc%d" % n)[:, left[n]])
-
-        spare = ["u_pool0", "u_pool1", "u_pool2", "u_pool3", "v_pool1", "v_pool2"]
+        product(1, halves[0], 3)
+        scatter(0, halves[0])
+        scatter(1, halves[0])
+        product(0, halves[1], 6)
+        product(1, halves[1], 7)
+        scatter(0, halves[1])
+        scatter(1, halves[1])
+        spare = ["u_pool0", "u_pool1", "u_pool2", "u_pool3", "v_pool1"]
         o_by_d = [sbuf([P, width, LANES], BF16, "o_by_d%d" % c, tag=spare[c]) for c, width in enumerate(WIDTHS)]
-        paired = STARTS[DIRECT]
-        pairs = sbuf([P, 2, POOL - paired, 2], BF16, "pairs")
-        for n, t in enumerate(ORDER):
-            target = window[n % WINDOWS]
-            last = n == LANES - 1
-            entries = ilist[:, HALF_LIST : 2 * HALF_LIST] if n < EARLY else ilist[:]
-            nc.vector.tensor_copy(target[:].indirect(entries), du[n][:, left[n]])
-            nc.sync.dma_start(out_rows[:, t, :], target[:])
-            for c in range(DIRECT):
-                copy = nc.vector.tensor_copy if last else nc.scalar.copy
-                copy(o_by_d[c][:, :, t], target[:, STARTS[c] : STARTS[c] + WIDTHS[c]])
-            if last:
-                for c in range(DIRECT, len(WIDTHS)):
-                    at = STARTS[c] - paired
-                    nc.scalar.copy(pairs[:, t // 2, at : at + WIDTHS[c], t % 2], target[:, STARTS[c] : STARTS[c] + WIDTHS[c]])
-            else:
-                round_on_gpsimd(pairs[:, t // 2, :, t % 2], target[:, paired:POOL])
+        pairs = [sbuf([P, 2, width, 2], BF16, "pairs%d" % c) for c, width in enumerate(WIDTHS)]
+        for t in range(2):
+            nc.sync.dma_start(out_rows[:, t, :], window[t][:])
+            for c in range(LOWER_ON_GPSIMD):
+                round_on_gpsimd(pairs[c][:, 0, :, t], window[t][:, STARTS[c] : STARTS[c] + WIDTHS[c]])
+        product(2, whole, 0)
+        product(3, whole, 1)
+        scatter(2, halves[0])
+        scatter(2, halves[1])
+        scatter(3, whole)
+        for t in range(2, LANES):
+            nc.sync.dma_start(out_rows[:, t, :], window[t][:])
+
+        def round_upper(c):
+            cols = slice(STARTS[c], STARTS[c] + WIDTHS[c])
+            copy = nc.vector.tensor_copy if c in ON_VECTOR else nc.scalar.copy
+            for t in range(2, LANES):
+                copy(pairs[c][:, 1, :, t % 2], window[t][:, cols])
 
         o_codes = sbuf([P, POOL], U32, "o_codes", tag="v_pool0")
         o_scales = sbuf([P, POOL], U8, "o_scales")
         words_out = out_1.rearrange("a p c l -> p (a c l)").bitcast(I32)
         scales_out = out_2.rearrange("a q c -> q (a c)").bitcast(I32)
-        pair_words = pairs[:].rearrange("p u c e -> p (u c e)").bitcast(F32).rearrange("p (u c) -> p c u", u=2)
 
         def weave_out(c):
-            at = STARTS[c] - paired
-            copy = nc.vector.tensor_copy if c == DIRECT else nc.scalar.copy
-            copy(flat(o_by_d[c][:]).bitcast(F32).rearrange("p (c u) -> p c u", u=2), pair_words[:, at : at + WIDTHS[c], :])
+            words = pairs[c][:].rearrange("p u c e -> p (u c e)").bitcast(F32).rearrange("p (u c) -> p c u", u=2)
+            nc.vector.tensor_copy(flat(o_by_d[c][:]).bitcast(F32).rearrange("p (c u) -> p c u", u=2), words)
 
+        for c in range(len(WIDTHS) - 1):
+            round_upper(c)
+        weave_out(0)
+        for c in range(LOWER_ON_GPSIMD, len(WIDTHS)):
+            for t in range(2):
+                nc.vector.tensor_copy(pairs[c][:, 0, :, t], window[t][:, STARTS[c] : STARTS[c] + WIDTHS[c]])
         stored = 0
         for c in range(len(WIDTHS)):
-            if DIRECT <= c + 1 < len(WIDTHS):
+            if c == 1:
+                round_upper(len(WIDTHS) - 1)
+            if c + 1 < len(WIDTHS):
                 weave_out(c + 1)
             cols = slice(STARTS[c], STARTS[c] + WIDTHS[c])
             nc.vector.quantize_mx(o_codes[:, cols].bitcast(E4M3), o_scales[:, cols], flat(o_by_d[c][:]))

@@ -24,11 +24,9 @@ HALF = SLOTS // 2
 HALF_LIST = HALF // 16
 RUN = 4
 
-WIDTHS = (256, 512, 512, 512, 256)
-LOWER_ON_GPSIMD = 3
+WIDTHS = (512, 512, 256, 256, 256, 256)
+SHARED = 3
 STARTS = [sum(WIDTHS[:c]) for c in range(len(WIDTHS))]
-ON_VECTOR = (0, 4)
-STORE_AFTER = (2, 3, 4)
 
 
 def tile_attend_gsink_u_pl_kernel(tc, uT, vT, su, sv, y, offs, qoffs, out_0, out_1, out_2):
@@ -82,7 +80,7 @@ def tile_attend_gsink_u_pl_kernel(tc, uT, vT, su, sv, y, offs, qoffs, out_0, out
 
         v_planes = sbuf([P, LANES, SLOTS], BF16, "v_planes")
         for t in range(LANES):
-            nc.scalar.activation(v_planes[:, t, :], v_pool[t][:].indirect(jlist[:]), ACT.Copy)
+            nc.vector.tensor_copy(v_planes[:, t, :], v_pool[t][:].indirect(jlist[:]))
         v_by_d = sbuf([P, SLOTS, LANES], BF16, "v_by_d")
         nc.scalar.copy(v_by_d[:], v_planes[:].rearrange("p t j -> p j t"))
         vd_codes = sbuf([P, SLOTS], U32, "vd_codes", tag="u_pool1")
@@ -90,9 +88,9 @@ def tile_attend_gsink_u_pl_kernel(tc, uT, vT, su, sv, y, offs, qoffs, out_0, out
         nc.vector.quantize_mx(vd_codes[:].bitcast(E4M3), vd_scales[:], flat(v_by_d[:]))
 
         sv_listed = sbuf([P, SLOTS], F32, "sv_listed")
-        nc.vector.tensor_copy(sv_listed[:], sv_pool[:].indirect(jlist[:]))
+        nc.scalar.activation(sv_listed[:], sv_pool[:].indirect(jlist[:]), ACT.Copy)
         su_listed = sbuf([P, SLOTS], F32, "su_listed")
-        nc.vector.tensor_copy(su_listed[:], su_pool[:].indirect(ilist[:]))
+        nc.scalar.activation(su_listed[:], su_pool[:].indirect(ilist[:]), ACT.Copy)
         sv_turned = bank(0, "sv_turned")
         for r in range(LANES):
             nc.tensor.transpose(sv_turned[:, r, :], sv_listed[:, r::LANES], ident[:])
@@ -164,7 +162,7 @@ def tile_attend_gsink_u_pl_kernel(tc, uT, vT, su, sv, y, offs, qoffs, out_0, out
         def lane_of(banks, r):
             return flat(banks[r // 2][:])[:, r % 2 * HALF : (r % 2 + 1) * HALF]
 
-        y_turned = [[bank(4 + 2 * h + k, "y_turned%d_%d" % (h, k)) for k in range(2)] for h in range(2)]
+        y_turned = [[bank(2 * h + k, "y_turned%d_%d" % (h, k)) for k in range(2)] for h in range(2)]
         for b in range(LANES):
             y_su = sbuf([P, LANES, P], F32, "y_su%d" % b)
             nc.scalar.activation(
@@ -184,7 +182,7 @@ def tile_attend_gsink_u_pl_kernel(tc, uT, vT, su, sv, y, offs, qoffs, out_0, out
         rinv = [sbuf([P, 1], F32, "rinv%d" % b) for b in range(LANES)]
         f_even = [sbuf([P, SLOTS], F32, "f_even%d" % k) for k in range(2)]
         f_pair = [[sbuf([P, HALF], F32, "f_pair%d_%d" % (k, h)) for h in range(2)] for k in range(2)]
-        sums_turned = [bank(2 + h, "sums_turned%d" % h) for h in range(2)]
+        sums_turned = [bank(4 + h, "sums_turned%d" % h) for h in range(2)]
         for b in range(LANES):
             nc.vector.reciprocal(rinv[b][:], r1[b][:])
         for k in range(2):
@@ -223,7 +221,7 @@ def tile_attend_gsink_u_pl_kernel(tc, uT, vT, su, sv, y, offs, qoffs, out_0, out
             finish_y(h)
         f_turned = []
         for h in range(2):
-            f_turned.append([bank(4 * h + k, "f_turned%d_%d" % (h, k)) for k in range(2)])
+            f_turned.append([bank(6 - 2 * h + k, "f_turned%d_%d" % (h, k)) for k in range(2)])
             for b in (2 * h, 2 * h + 1):
                 for r in range(LANES):
                     nc.tensor.transpose(quarter(f_turned[h], r, b), f_su[b][:, r * P : (r + 1) * P], ident[:])
@@ -255,12 +253,11 @@ def tile_attend_gsink_u_pl_kernel(tc, uT, vT, su, sv, y, offs, qoffs, out_0, out
             cols = slice(h * HALF, (h + 1) * HALF)
             nc.vector.quantize_mx(g_codes[:, cols].bitcast(E5M2), g_scales[:, cols], flat(g_by_j[h][:]))
 
-        du = [sbuf([P, SLOTS], F32, "du%d" % t, tag="expd%d" % t) for t in range(LANES)]
         out_rows = out_0.rearrange("(p t) c -> p t c", t=LANES)
 
-        def product(t, sources, number):
+        def product(t, first, count, acc):
             cols = slice(t * P, (t + 1) * P)
-            acc = flat(bank(number, "du_acc%d_%d" % (t, sources.start))[:])[:, 0 : sources.stop - sources.start]
+            sources = slice(first * HALF, (first + count) * HALF)
             nc.tensor.matmul_mx(
                 acc,
                 lhsT=vj_codes[:, cols].bitcast(E4M3),
@@ -270,79 +267,98 @@ def tile_attend_gsink_u_pl_kernel(tc, uT, vT, su, sv, y, offs, qoffs, out_0, out
                 start=True,
                 stop=True,
             )
-            copy = nc.vector.tensor_copy if t % 2 else nc.scalar.copy
-            copy(du[t][:, sources], acc)
+            return acc
 
-        def scatter(t, sources):
-            target = window[t][:].indirect(ilist[:, sources.start // 16 : sources.stop // 16])
-            if t % 2:
-                nc.vector.tensor_copy(target, du[t][:, sources])
+        du = {}
+
+        def copy_out(parts, acc, tag=None):
+            held = sbuf([P, len(parts) * HALF], F32, "du%d_%d" % parts[0], tag=tag)
+            nc.scalar.copy(held[:], acc)
+            for n, part in enumerate(parts):
+                du[part] = held[:, n * HALF : (n + 1) * HALF]
+
+        def scatter(t, h):
+            target = window[t][:].indirect(ilist[:, h * HALF_LIST : (h + 1) * HALF_LIST])
+            if t == 2 or (t, h) == (1, 0):
+                nc.scalar.activation(target, du[t, h], ACT.Copy)
             else:
-                nc.scalar.activation(target, du[t][:, sources], ACT.Copy)
+                nc.vector.tensor_copy(target, du[t, h])
 
-        halves = [slice(h * HALF, (h + 1) * HALF) for h in range(2)]
-        whole = slice(0, SLOTS)
         form_g(0)
         weave_g(0)
         quantise_g(0)
         form_g(1)
         weave_g(1)
-        product(0, halves[0], 2)
+        accs = [flat(bank(number, "du_acc%d" % number)[:]) for number in (0, 1, 2, 3, 6)]
+        lower, upper = slice(0, HALF), slice(HALF, SLOTS)
+        copy_out([(0, 0)], product(0, 0, 1, accs[0][:, lower]))
+        product(1, 0, 1, accs[1][:, lower])
         quantise_g(1)
-        product(1, halves[0], 3)
-        scatter(0, halves[0])
-        scatter(1, halves[0])
-        product(0, halves[1], 6)
-        product(1, halves[1], 7)
-        scatter(0, halves[1])
-        scatter(1, halves[1])
-        spare = ["u_pool0", "u_pool1", "u_pool2", "u_pool3", "v_pool1"]
+        scatter(0, 0)
+        product(0, 1, 1, accs[1][:, upper])
+        copy_out([(1, 0), (0, 1)], accs[1])
+        scatter(0, 1)
+        scatter(1, 0)
+        copy_out([(1, 1)], product(1, 1, 1, accs[2][:, lower]))
+        product(2, 0, 2, accs[3])
+        product(3, 0, 2, accs[4])
+        copy_out([(2, 0)], accs[3][:, lower], tag="du0_0")
+        scatter(1, 1)
+        copy_out([(3, 0)], accs[4][:, lower], tag="du1_0")
+        scatter(2, 0)
+        copy_out([(2, 1)], accs[3][:, upper])
+        copy_out([(3, 1)], accs[4][:, upper], tag="du0_0")
+        scatter(3, 0)
+        scatter(2, 1)
+        scatter(3, 1)
+        spare = ["u_pool0", "u_pool1", "u_pool2", "u_pool3", "v_pool1", "v_pool2"]
         o_by_d = [sbuf([P, width, LANES], BF16, "o_by_d%d" % c, tag=spare[c]) for c, width in enumerate(WIDTHS)]
-        pairs = [sbuf([P, 2, width, 2], BF16, "pairs%d" % c) for c, width in enumerate(WIDTHS)]
-        for t in range(2):
-            nc.sync.dma_start(out_rows[:, t, :], window[t][:])
-            for c in range(LOWER_ON_GPSIMD):
-                round_on_gpsimd(pairs[c][:, 0, :, t], window[t][:, STARTS[c] : STARTS[c] + WIDTHS[c]])
-        product(2, whole, 0)
-        product(3, whole, 1)
-        scatter(2, halves[0])
-        scatter(2, halves[1])
-        scatter(3, whole)
-        for t in range(2, LANES):
-            nc.sync.dma_start(out_rows[:, t, :], window[t][:])
+        own = STARTS[SHARED]
+        pairs_shared = sbuf([P, 2, own, 2], BF16, "pairs_shared")
+        pairs_own = sbuf([P, 2, POOL - own, 2], BF16, "pairs_own", tag="du0_0")
 
-        def round_upper(c):
-            cols = slice(STARTS[c], STARTS[c] + WIDTHS[c])
-            copy = nc.vector.tensor_copy if c in ON_VECTOR else nc.scalar.copy
-            for t in range(2, LANES):
-                copy(pairs[c][:, 1, :, t % 2], window[t][:, cols])
+        for t in range(LANES):
+            nc.sync.dma_start(out_rows[:, t, :], window[t][:])
+        nc.scalar.copy(pairs_shared[:, 1, :, 0], window[2][:, 0:own])
+        for t in range(2):
+            round_on_gpsimd(pairs_shared[:, 0, :, t], window[t][:, 0:own])
+        for t in range(LANES):
+            nc.vector.tensor_copy(pairs_own[:, t // 2, :, t % 2], window[t][:, own:POOL])
 
         o_codes = sbuf([P, POOL], U32, "o_codes", tag="v_pool0")
         o_scales = sbuf([P, POOL], U8, "o_scales")
         words_out = out_1.rearrange("a p c l -> p (a c l)").bitcast(I32)
         scales_out = out_2.rearrange("a q c -> q (a c)").bitcast(I32)
 
-        def weave_out(c):
-            words = pairs[c][:].rearrange("p u c e -> p (u c e)").bitcast(F32).rearrange("p (u c) -> p c u", u=2)
-            nc.vector.tensor_copy(flat(o_by_d[c][:]).bitcast(F32).rearrange("p (c u) -> p c u", u=2), words)
+        def weave_out(c, copy):
+            pairs, at = (pairs_shared, STARTS[c]) if c < SHARED else (pairs_own, STARTS[c] - own)
+            words = pairs[:].rearrange("p u c e -> p (u c e)").bitcast(F32).rearrange("p (u c) -> p c u", u=2)
+            copy(flat(o_by_d[c][:]).bitcast(F32).rearrange("p (c u) -> p c u", u=2), words[:, at : at + WIDTHS[c], :])
 
-        for c in range(len(WIDTHS) - 1):
-            round_upper(c)
-        weave_out(0)
-        for c in range(LOWER_ON_GPSIMD, len(WIDTHS)):
-            for t in range(2):
-                nc.vector.tensor_copy(pairs[c][:, 0, :, t], window[t][:, STARTS[c] : STARTS[c] + WIDTHS[c]])
-        stored = 0
-        for c in range(len(WIDTHS)):
-            if c == 1:
-                round_upper(len(WIDTHS) - 1)
-            if c + 1 < len(WIDTHS):
-                weave_out(c + 1)
+        def quantise_out(c):
             cols = slice(STARTS[c], STARTS[c] + WIDTHS[c])
             nc.vector.quantize_mx(o_codes[:, cols].bitcast(E4M3), o_scales[:, cols], flat(o_by_d[c][:]))
-            if c in STORE_AFTER:
-                nc.sync.dma_start(words_out[:, stored : cols.stop], o_codes[:, stored : cols.stop].bitcast(I32))
-                stored = cols.stop
+
+        def store_codes(first, last):
+            cols = slice(STARTS[first], STARTS[last] + WIDTHS[last])
+            nc.sync.dma_start(words_out[:, cols], o_codes[:, cols].bitcast(I32))
+
+        for c in range(SHARED):
+            cols = slice(STARTS[c], STARTS[c] + WIDTHS[c])
+            nc.scalar.copy(pairs_shared[:, 1, cols, 1], window[3][:, cols])
+            if c < SHARED - 1:
+                weave_out(c, nc.scalar.copy)
+        for c in (5, 4, 3):
+            weave_out(c, nc.vector.tensor_copy)
+        for c in (0, 5, 4):
+            quantise_out(c)
+        weave_out(2, nc.vector.tensor_copy)
+        quantise_out(3)
+        store_codes(3, 5)
+        quantise_out(1)
+        store_codes(0, 1)
+        quantise_out(2)
+        store_codes(2, 2)
         for q in range(4):
             queue = nc.scalar if q % 2 else nc.sync
             queue.dma_start(scales_out[4 * q : 4 * q + 4, :], o_scales[32 * q : 32 * q + 4, :].bitcast(I32))

@@ -22,6 +22,7 @@ POOL = 2048
 SLOTS = 512
 HALF = SLOTS // 2
 HALF_LIST = HALF // 16
+SU_ROW = 63
 RUN = 4
 
 WIDTHS = (512, 512, 256, 256, 256, 256)
@@ -61,9 +62,7 @@ def tile_attend_gsink_u_pl_kernel(tc, uT, vT, su, sv, y, offs, qoffs, out_0, out
         nc.sync.dma_start(jlist[:], qoffs)
         nc.sync.dma_start(ilist[:], offs)
         nc.scalar.dma_start(sv_pool[P - 1 : P, :], sv[0:1, :])
-        nc.scalar.dma_start(su_pool[P - 1 : P, :], su[0:1, :])
-        nc.vector.memset(sv_pool[0 : P - 1, :], 0.0)
-        nc.vector.memset(su_pool[0 : P - 1, :], 0.0)
+        nc.scalar.dma_start(su_pool[SU_ROW : SU_ROW + 1, :], su[0:1, :])
         for t in range(1, LANES):
             nc.sync.dma_start(v_pool[t][:], v_rows[:, t, :])
         for t in range(LANES):
@@ -73,10 +72,13 @@ def tile_attend_gsink_u_pl_kernel(tc, uT, vT, su, sv, y, offs, qoffs, out_0, out
 
         ident = sbuf([P, P], F32, "ident")
         make_identity(nc, ident[:])
+        nc.gpsimd.memset(sv_pool[0 : P - 1, :], 0.0)
+        nc.gpsimd.memset(su_pool[0:SU_ROW, :], 0.0)
+        nc.gpsimd.memset(su_pool[SU_ROW + 1 : P, :], 0.0)
 
         window = [sbuf([P, POOL], F32, "window%d" % w) for w in range(LANES)]
         for w in range(LANES):
-            nc.vector.memset(window[w][:], 0.0)
+            nc.gpsimd.memset(window[w][:], 0.0)
 
         v_planes = sbuf([P, LANES, SLOTS], BF16, "v_planes")
         for t in range(LANES):
@@ -100,7 +102,7 @@ def tile_attend_gsink_u_pl_kernel(tc, uT, vT, su, sv, y, offs, qoffs, out_0, out
         for b in range(LANES):
             nc.tensor.transpose(su_turned[:, b, :], su_listed[:, b * P : (b + 1) * P], ident[:])
         su_col = sbuf([P, LANES], F32, "su_col")
-        nc.scalar.copy(su_col[:], su_turned[:, :, P - 1])
+        nc.scalar.copy(su_col[:], su_turned[:, :, SU_ROW])
         sv_spread = bank(2, "sv_spread")
         for r in range(LANES):
             nc.tensor.transpose(sv_spread[:, r, :], sv_col[:, r : r + 1].to_broadcast([P, P]), ident[:])

@@ -55,7 +55,6 @@ def tile_attend_gsink_u_pl_kernel(tc, uT, vT, su, sv, y, offs, qoffs, out_0, out
         u_rows = uT.rearrange("(p t) c -> p t c", t=LANES)
         v_pool = [sbuf([P, POOL], F32, "v_pool%d" % t) for t in range(LANES)]
         u_pool = [sbuf([P, POOL], F32, "u_pool%d" % t) for t in range(LANES)]
-        y_tile = [sbuf([P, SLOTS], F32, "y%d" % b) for b in range(LANES)]
         sv_pool = sbuf([P, POOL], F32, "sv_pool")
         su_pool = sbuf([P, POOL], F32, "su_pool")
         nc.sync.dma_start(v_pool[0][:], v_rows[:, 0, :])
@@ -67,8 +66,6 @@ def tile_attend_gsink_u_pl_kernel(tc, uT, vT, su, sv, y, offs, qoffs, out_0, out
             nc.sync.dma_start(v_pool[t][:], v_rows[:, t, :])
         for t in range(LANES):
             nc.sync.dma_start(u_pool[t][:], u_rows[:, t, :])
-        for b in range(LANES):
-            nc.sync.dma_start(y_tile[b][:], y[b * P : (b + 1) * P, :])
 
         ident = sbuf([P, P], F32, "ident")
         make_identity(nc, ident[:])
@@ -80,12 +77,13 @@ def tile_attend_gsink_u_pl_kernel(tc, uT, vT, su, sv, y, offs, qoffs, out_0, out
         for w in range(LANES):
             nc.gpsimd.memset(window[w][:], 0.0)
 
-        v_planes = sbuf([P, LANES, SLOTS], BF16, "v_planes")
-        for t in range(LANES):
-            nc.vector.tensor_copy(v_planes[:, t, :], v_pool[t][:].indirect(jlist[:]))
         v_by_d = sbuf([P, SLOTS, LANES], BF16, "v_by_d")
-        nc.scalar.copy(v_by_d[:], v_planes[:].rearrange("p t j -> p j t"))
-        vd_codes = sbuf([P, SLOTS], U32, "vd_codes", tag="u_pool1")
+        for t in range(LANES):
+            nc.vector.tensor_copy(v_by_d[:, :, t], v_pool[t][:].indirect(jlist[:]))
+        y_tile = [sbuf([P, SLOTS], F32, "y%d" % b, tag="v_pool%d" % b) for b in range(LANES)]
+        for b in range(LANES):
+            nc.sync.dma_start(y_tile[b][:], y[b * P : (b + 1) * P, :])
+        vd_codes = sbuf([P, SLOTS], U32, "vd_codes")
         vd_scales = sbuf([P, SLOTS], U8, "vd_scales")
         nc.vector.quantize_mx(vd_codes[:].bitcast(E4M3), vd_scales[:], flat(v_by_d[:]))
 
@@ -134,11 +132,20 @@ def tile_attend_gsink_u_pl_kernel(tc, uT, vT, su, sv, y, offs, qoffs, out_0, out
             cols = slice(h * HALF, (h + 1) * HALF)
             nc.vector.quantize_mx(u_codes[:, cols].bitcast(E4M3), u_scales[:, cols], flat(u_by_d[:, cols, :]))
 
-        vj_codes = sbuf([P, SLOTS], U32, "vj_codes", tag="u_by_d")
+        vj_codes = sbuf([P, SLOTS], U32, "vj_codes")
         vj_scales = sbuf([P, SLOTS], U8, "vj_scales")
         nc.vector.quantize_mx(vj_codes[:].bitcast(E4M3), vj_scales[:], v_by_j[:].rearrange("s t p r -> s (t p r)"))
 
         scaled = [sbuf([P, LANES, P], F32, "scaled%d" % b) for b in range(LANES)]
+        y_late = sbuf([P, 2, LANES, P], F32, "y_late", tag="u_by_d")
+        y_su = [sbuf([P, LANES, P], F32, "y_su%d" % b)[:] for b in range(2)] + [y_late[:, b, :, :] for b in range(2)]
+        for b in range(LANES):
+            planes = y_su[b].rearrange("p r (c n) -> p c r n", n=RUN)
+            rows = y_tile[b][:].rearrange("p (c n r) -> p c r n", n=RUN, r=LANES)
+            if b < 2:
+                nc.scalar.activation(planes, rows, ACT.Copy, scale=su_col[:, b : b + 1])
+            else:
+                nc.gpsimd.tensor_scalar(planes, rows, su_col[:, b : b + 1], 0.0, ALU.mult, ALU.add)
         expd = [sbuf([P, SLOTS], F32, "expd%d" % b) for b in range(LANES)]
         r1 = [sbuf([P, 1], F32, "r1_%d" % b) for b in range(LANES)]
         for b in range(LANES):
@@ -164,17 +171,10 @@ def tile_attend_gsink_u_pl_kernel(tc, uT, vT, su, sv, y, offs, qoffs, out_0, out
         def lane_of(banks, r):
             return flat(banks[r // 2][:])[:, r % 2 * HALF : (r % 2 + 1) * HALF]
 
-        y_turned = [[bank(2 * h + k, "y_turned%d_%d" % (h, k)) for k in range(2)] for h in range(2)]
+        y_turned = [[bank(6 - 6 * h + k, "y_turned%d_%d" % (h, k)) for k in range(2)] for h in range(2)]
         for b in range(LANES):
-            y_su = sbuf([P, LANES, P], F32, "y_su%d" % b)
-            nc.scalar.activation(
-                y_su[:].rearrange("p r s -> p s r"),
-                y_tile[b][:].rearrange("p (s r) -> p s r", r=LANES),
-                ACT.Copy,
-                scale=su_col[:, b : b + 1],
-            )
             for r in range(LANES):
-                nc.tensor.transpose(quarter(y_turned[b // 2], r, b), y_su[:, r, :], ident[:])
+                nc.tensor.transpose(quarter(y_turned[b // 2], r, b), y_su[b][:, r, :], ident[:])
         y_both = [[sbuf([P, HALF], F32, "y_both%d_%d" % (h, r)) for r in range(LANES)] for h in range(2)]
 
         def finish_y(h):
@@ -204,26 +204,34 @@ def tile_attend_gsink_u_pl_kernel(tc, uT, vT, su, sv, y, offs, qoffs, out_0, out
                         stop=k == 1 and e == 1,
                         is_transpose=True,
                     )
+        sv_inv = sbuf([P, LANES], F32, "sv_inv")
+        nc.vector.reciprocal(sv_inv[:], sv_col[:])
+        terms = sbuf([P, LANES, P], F32, "terms")
         c1 = [sbuf([P, 2], F32, "c1_%d" % h) for h in range(2)]
-        cinv = [sbuf([P, 2], F32, "cinv%d" % h) for h in range(2)]
         csv = [sbuf([P, 2], F32, "csv%d" % h) for h in range(2)]
         for h in range(2):
-            nc.vector.tensor_reduce(c1[h][:], sums_turned[h][:, 0:2, :], mybir.AxisListType.X, ALU.add)
+            for e in range(2):
+                r = 2 * h + e
+                nc.vector.tensor_scalar(
+                    terms[:, r, :], sums_turned[h][:, e, :], sv_inv[:, r : r + 1], None, ALU.mult, ALU.add,
+                    accum_out=c1[h][:, e : e + 1],
+                )
         for h in range(2):
-            nc.vector.reciprocal(cinv[h][:], c1[h][:])
-        for h in range(2):
-            nc.vector.tensor_tensor(csv[h][:], cinv[h][:], sv_col[:, 2 * h : 2 * h + 2], ALU.mult)
+            nc.vector.reciprocal(csv[h][:], c1[h][:])
 
-        f_tags = ["scaled0", "scaled1", "scaled2", "f_pair1_1"]
+        f_tags = ["scaled0", "scaled1", "f_pair1_0", "f_pair1_1"]
         f_su = [sbuf([P, SLOTS], F32, "f_su%d" % b, tag=f_tags[b]) for b in range(LANES)]
+        su_rinv = sbuf([P, 1], F32, "su_rinv")
+        nc.vector.tensor_scalar(su_rinv[:], rinv[1][:], su_col[:, 1:2], None, ALU.mult)
+        nc.scalar.activation(f_su[0][:], f_even[0][:], ACT.Copy, scale=su_col[:, 0:1])
+        nc.scalar.activation(f_su[1][:], expd[1][:], ACT.Copy, scale=su_rinv[:])
+        for b in (2, 3):
+            nc.gpsimd.tensor_scalar(f_su[b][:], expd[b][:], rinv[b][:], su_col[:, b : b + 1], ALU.mult, ALU.mult)
         for h in range(2):
-            even, odd = 2 * h, 2 * h + 1
-            nc.scalar.activation(f_su[even][:], f_even[h][:], ACT.Copy, scale=su_col[:, even : even + 1])
-            nc.vector.tensor_scalar(f_su[odd][:], expd[odd][:], rinv[odd][:], su_col[:, odd : odd + 1], ALU.mult, ALU.mult)
             finish_y(h)
         f_turned = []
         for h in range(2):
-            f_turned.append([bank(6 - 2 * h + k, "f_turned%d_%d" % (h, k)) for k in range(2)])
+            f_turned.append([bank(2 + 4 * h + k, "f_turned%d_%d" % (h, k)) for k in range(2)])
             for b in (2 * h, 2 * h + 1):
                 for r in range(LANES):
                     nc.tensor.transpose(quarter(f_turned[h], r, b), f_su[b][:, r * P : (r + 1) * P], ident[:])
@@ -249,7 +257,13 @@ def tile_attend_gsink_u_pl_kernel(tc, uT, vT, su, sv, y, offs, qoffs, out_0, out
                 g_by_j[h][:, 0:P, :].rearrange("s (c n) r -> s c r n", n=RUN),
                 g_planes[h][:, :, 0:P].rearrange("s r (c n) -> s c r n", n=RUN),
             )
-            round_on_gpsimd(g_by_j[h][:, P:HALF, :], g_planes[h][:, :, P:HALF].rearrange("s r c -> s c r"))
+            if h == 0:
+                round_on_gpsimd(g_by_j[h][:, P:HALF, :], g_planes[h][:, :, P:HALF].rearrange("s r c -> s c r"))
+            else:
+                nc.vector.tensor_copy(
+                    g_by_j[h][:, P:HALF, :].rearrange("s (c n) r -> s c r n", n=RUN),
+                    g_planes[h][:, :, P:HALF].rearrange("s r (c n) -> s c r n", n=RUN),
+                )
 
         def quantise_g(h):
             cols = slice(h * HALF, (h + 1) * HALF)
@@ -288,10 +302,10 @@ def tile_attend_gsink_u_pl_kernel(tc, uT, vT, su, sv, y, offs, qoffs, out_0, out
 
         form_g(0)
         weave_g(0)
-        quantise_g(0)
         form_g(1)
+        quantise_g(0)
         weave_g(1)
-        accs = [flat(bank(number, "du_acc%d" % number)[:]) for number in (0, 1, 2, 3, 6)]
+        accs = [flat(bank(number, "du_acc%d" % number)[:]) for number in (0, 1, 4, 5, 2)]
         lower, upper = slice(0, HALF), slice(HALF, SLOTS)
         copy_out([(0, 0)], product(0, 0, 1, accs[0][:, lower]))
         product(1, 0, 1, accs[1][:, lower])

@@ -83,7 +83,7 @@ def tile_attend_gsink_u_pl_kernel(tc, uT, vT, su, sv, y, offs, qoffs, out_0, out
         y_tile = [sbuf([P, SLOTS], F32, "y%d" % b, tag="v_pool%d" % b) for b in range(LANES)]
         for b in range(LANES):
             nc.sync.dma_start(y_tile[b][:], y[b * P : (b + 1) * P, :])
-        vd_codes = sbuf([P, SLOTS], U32, "vd_codes")
+        vd_codes = sbuf([P, SLOTS], U32, "vd_codes", tag="u_pool1")
         vd_scales = sbuf([P, SLOTS], U8, "vd_scales")
         nc.vector.quantize_mx(vd_codes[:].bitcast(E4M3), vd_scales[:], flat(v_by_d[:]))
 
@@ -118,31 +118,33 @@ def tile_attend_gsink_u_pl_kernel(tc, uT, vT, su, sv, y, offs, qoffs, out_0, out
                 flat(v_turned[:]).bitcast(BF16).rearrange("s (r p e) -> s e p r", r=LANES, e=2),
             )
 
-        u_by_d = sbuf([P, SLOTS, LANES], BF16, "u_by_d")
-        for t in range(LANES - 1):
-            nc.vector.tensor_copy(u_by_d[:, :, t], u_pool[t][:].indirect(ilist[:]))
+        u_by_d = [sbuf([P, HALF, LANES], BF16, "u_by_d%d" % h) for h in range(2)]
+        u_last = sbuf([P, 2, HALF], BF16, "u_last")
+        half_list = [ilist[:, h * HALF_LIST : (h + 1) * HALF_LIST] for h in range(2)]
+        for t in range(LANES):
+            nc.vector.tensor_copy(u_by_d[0][:, :, t], u_pool[t][:].indirect(half_list[0]))
+            if t < 2:
+                nc.vector.tensor_copy(u_by_d[1][:, :, t], u_pool[t][:].indirect(half_list[1]))
+            else:
+                nc.scalar.activation(u_last[:, t - 2, :], u_pool[t][:].indirect(half_list[1]), ACT.Copy)
+        nc.scalar.copy(u_by_d[1][:, :, 2:LANES], u_last[:].rearrange("p e i -> p i e"))
         u_codes = sbuf([P, SLOTS], U32, "u_codes")
         u_scales = sbuf([P, SLOTS], U8, "u_scales")
         for h in range(2):
-            nc.vector.tensor_copy(
-                u_by_d[:, h * HALF : (h + 1) * HALF, LANES - 1],
-                u_pool[LANES - 1][:].indirect(ilist[:, h * HALF_LIST : (h + 1) * HALF_LIST]),
-            )
-        for h in range(2):
             cols = slice(h * HALF, (h + 1) * HALF)
-            nc.vector.quantize_mx(u_codes[:, cols].bitcast(E4M3), u_scales[:, cols], flat(u_by_d[:, cols, :]))
+            nc.vector.quantize_mx(u_codes[:, cols].bitcast(E4M3), u_scales[:, cols], flat(u_by_d[h][:]))
 
-        vj_codes = sbuf([P, SLOTS], U32, "vj_codes")
+        vj_codes = sbuf([P, SLOTS], U32, "vj_codes", tag="u_pool2")
         vj_scales = sbuf([P, SLOTS], U8, "vj_scales")
         nc.vector.quantize_mx(vj_codes[:].bitcast(E4M3), vj_scales[:], v_by_j[:].rearrange("s t p r -> s (t p r)"))
 
-        scaled = [sbuf([P, LANES, P], F32, "scaled%d" % b) for b in range(LANES)]
-        y_late = sbuf([P, 2, LANES, P], F32, "y_late", tag="u_by_d")
-        y_su = [sbuf([P, LANES, P], F32, "y_su%d" % b)[:] for b in range(2)] + [y_late[:, b, :, :] for b in range(2)]
+        late = sbuf([P, LANES, LANES, P], F32, "late", tag="u_by_d1")
+        y_su = [sbuf([P, LANES, P], F32, "y_su0", tag="u_last")[:]] + [late[:, b, :, :] for b in range(1, LANES)]
+        scaled = [late[:, 0, :, :]] + [sbuf([P, LANES, P], F32, "scaled%d" % b)[:] for b in range(1, LANES)]
         for b in range(LANES):
             planes = y_su[b].rearrange("p r (c n) -> p c r n", n=RUN)
             rows = y_tile[b][:].rearrange("p (c n r) -> p c r n", n=RUN, r=LANES)
-            if b < 2:
+            if b == 0:
                 nc.scalar.activation(planes, rows, ACT.Copy, scale=su_col[:, b : b + 1])
             else:
                 nc.gpsimd.tensor_scalar(planes, rows, su_col[:, b : b + 1], 0.0, ALU.mult, ALU.add)
@@ -161,9 +163,9 @@ def tile_attend_gsink_u_pl_kernel(tc, uT, vT, su, sv, y, offs, qoffs, out_0, out
                 stop=True,
             )
             nc.vector.tensor_tensor(
-                scaled[b][:], flat(score[:]).rearrange("p (s r) -> p r s", r=LANES), sv_row[:], ALU.mult
+                scaled[b], sv_row[:], flat(score[:]).rearrange("p (s r) -> p r s", r=LANES), ALU.mult
             )
-            nc.scalar.activation(expd[b][:], flat(scaled[b][:]), ACT.Exp, scale=su_col[:, b : b + 1], accum_out=r1[b][:])
+            nc.scalar.activation(expd[b][:], flat(scaled[b]), ACT.Exp, scale=su_col[:, b : b + 1], accum_out=r1[b][:])
 
         def quarter(banks, r, b):
             return banks[r // 2][:, 2 * (r % 2) + b % 2, :]
@@ -204,30 +206,22 @@ def tile_attend_gsink_u_pl_kernel(tc, uT, vT, su, sv, y, offs, qoffs, out_0, out
                         stop=k == 1 and e == 1,
                         is_transpose=True,
                     )
-        sv_inv = sbuf([P, LANES], F32, "sv_inv")
-        nc.vector.reciprocal(sv_inv[:], sv_col[:])
-        terms = sbuf([P, LANES, P], F32, "terms")
         c1 = [sbuf([P, 2], F32, "c1_%d" % h) for h in range(2)]
+        cinv = [sbuf([P, 2], F32, "cinv%d" % h) for h in range(2)]
         csv = [sbuf([P, 2], F32, "csv%d" % h) for h in range(2)]
         for h in range(2):
-            for e in range(2):
-                r = 2 * h + e
-                nc.vector.tensor_scalar(
-                    terms[:, r, :], sums_turned[h][:, e, :], sv_inv[:, r : r + 1], None, ALU.mult, ALU.add,
-                    accum_out=c1[h][:, e : e + 1],
-                )
+            nc.vector.tensor_reduce(c1[h][:], sums_turned[h][:, 0:2, :], mybir.AxisListType.X, ALU.add)
         for h in range(2):
-            nc.vector.reciprocal(csv[h][:], c1[h][:])
+            nc.vector.reciprocal(cinv[h][:], c1[h][:])
+        for h in range(2):
+            nc.vector.tensor_tensor(csv[h][:], cinv[h][:], sv_col[:, 2 * h : 2 * h + 2], ALU.mult)
 
-        f_tags = ["scaled0", "scaled1", "f_pair1_0", "f_pair1_1"]
+        f_tags = ["scaled1", "scaled2", "scaled3", "f_pair1_1"]
         f_su = [sbuf([P, SLOTS], F32, "f_su%d" % b, tag=f_tags[b]) for b in range(LANES)]
-        su_rinv = sbuf([P, 1], F32, "su_rinv")
-        nc.vector.tensor_scalar(su_rinv[:], rinv[1][:], su_col[:, 1:2], None, ALU.mult)
-        nc.scalar.activation(f_su[0][:], f_even[0][:], ACT.Copy, scale=su_col[:, 0:1])
-        nc.scalar.activation(f_su[1][:], expd[1][:], ACT.Copy, scale=su_rinv[:])
-        for b in (2, 3):
-            nc.gpsimd.tensor_scalar(f_su[b][:], expd[b][:], rinv[b][:], su_col[:, b : b + 1], ALU.mult, ALU.mult)
         for h in range(2):
+            even, odd = 2 * h, 2 * h + 1
+            nc.scalar.activation(f_su[even][:], f_even[h][:], ACT.Copy, scale=su_col[:, even : even + 1])
+            nc.vector.tensor_scalar(f_su[odd][:], expd[odd][:], rinv[odd][:], su_col[:, odd : odd + 1], ALU.mult, ALU.mult)
             finish_y(h)
         f_turned = []
         for h in range(2):
@@ -327,7 +321,7 @@ def tile_attend_gsink_u_pl_kernel(tc, uT, vT, su, sv, y, offs, qoffs, out_0, out
         scatter(3, 0)
         scatter(2, 1)
         scatter(3, 1)
-        spare = ["u_pool0", "u_pool1", "u_pool2", "u_pool3", "v_pool1", "v_pool2"]
+        spare = ["u_pool0", "u_pool1", "sv_pool", "u_pool3", "v_pool1", "v_pool2"]
         o_by_d = [sbuf([P, width, LANES], BF16, "o_by_d%d" % c, tag=spare[c]) for c, width in enumerate(WIDTHS)]
         own = STARTS[SHARED]
         pairs_shared = sbuf([P, 2, own, 2], BF16, "pairs_shared")

@@ -138,13 +138,16 @@ def tile_attend_gsink_u_pl_kernel(tc, uT, vT, su, sv, y, offs, qoffs, out_0, out
         vj_scales = sbuf([P, SLOTS], U8, "vj_scales")
         nc.vector.quantize_mx(vj_codes[:].bitcast(E4M3), vj_scales[:], v_by_j[:].rearrange("s t p r -> s (t p r)"))
 
-        late = sbuf([P, LANES, LANES, P], F32, "late", tag="u_by_d1")
-        y_su = [sbuf([P, LANES, P], F32, "y_su0", tag="u_last")[:]] + [late[:, b, :, :] for b in range(1, LANES)]
+        late = sbuf([P, 3, LANES, P], F32, "late", tag="u_by_d1")
+        early = sbuf([P, LANES, P], F32, "early", tag="u_last")
+        y_su = [sbuf([P, LANES, P], F32, "y_su0")[:], early[:], late[:, 1, :, :], late[:, 2, :, :]]
         scaled = [late[:, 0, :, :]] + [sbuf([P, LANES, P], F32, "scaled%d" % b)[:] for b in range(1, LANES)]
         for b in range(LANES):
             planes = y_su[b].rearrange("p r (c n) -> p c r n", n=RUN)
             rows = y_tile[b][:].rearrange("p (c n r) -> p c r n", n=RUN, r=LANES)
             if b == 0:
+                nc.vector.tensor_scalar(planes, rows, su_col[:, b : b + 1], None, ALU.mult)
+            elif b == 1:
                 nc.scalar.activation(planes, rows, ACT.Copy, scale=su_col[:, b : b + 1])
             else:
                 nc.gpsimd.tensor_scalar(planes, rows, su_col[:, b : b + 1], 0.0, ALU.mult, ALU.add)
@@ -173,7 +176,7 @@ def tile_attend_gsink_u_pl_kernel(tc, uT, vT, su, sv, y, offs, qoffs, out_0, out
         def lane_of(banks, r):
             return flat(banks[r // 2][:])[:, r % 2 * HALF : (r % 2 + 1) * HALF]
 
-        y_turned = [[bank(6 - 6 * h + k, "y_turned%d_%d" % (h, k)) for k in range(2)] for h in range(2)]
+        y_turned = [[bank(6 * h + k, "y_turned%d_%d" % (h, k)) for k in range(2)] for h in range(2)]
         for b in range(LANES):
             for r in range(LANES):
                 nc.tensor.transpose(quarter(y_turned[b // 2], r, b), y_su[b][:, r, :], ident[:])
@@ -184,7 +187,7 @@ def tile_attend_gsink_u_pl_kernel(tc, uT, vT, su, sv, y, offs, qoffs, out_0, out
                 nc.scalar.activation(y_both[h][r][:], lane_of(y_turned[h], r), ACT.Copy, scale=sv_col[:, r : r + 1])
 
         rinv = [sbuf([P, 1], F32, "rinv%d" % b) for b in range(LANES)]
-        f_even = [sbuf([P, SLOTS], F32, "f_even%d" % k) for k in range(2)]
+        f_even = [sbuf([P, SLOTS], F32, "f_even0", tag="sv_row"), sbuf([P, SLOTS], F32, "f_even1")]
         f_pair = [[sbuf([P, HALF], F32, "f_pair%d_%d" % (k, h)) for h in range(2)] for k in range(2)]
         sums_turned = [bank(4 + h, "sums_turned%d" % h) for h in range(2)]
         for b in range(LANES):
@@ -225,7 +228,7 @@ def tile_attend_gsink_u_pl_kernel(tc, uT, vT, su, sv, y, offs, qoffs, out_0, out
             finish_y(h)
         f_turned = []
         for h in range(2):
-            f_turned.append([bank(2 + 4 * h + k, "f_turned%d_%d" % (h, k)) for k in range(2)])
+            f_turned.append([bank(2 - 2 * h + k, "f_turned%d_%d" % (h, k)) for k in range(2)])
             for b in (2 * h, 2 * h + 1):
                 for r in range(LANES):
                     nc.tensor.transpose(quarter(f_turned[h], r, b), f_su[b][:, r * P : (r + 1) * P], ident[:])
@@ -299,7 +302,7 @@ def tile_attend_gsink_u_pl_kernel(tc, uT, vT, su, sv, y, offs, qoffs, out_0, out
         form_g(1)
         quantise_g(0)
         weave_g(1)
-        accs = [flat(bank(number, "du_acc%d" % number)[:]) for number in (0, 1, 4, 5, 2)]
+        accs = [flat(bank(number, "du_acc%d" % number)[:]) for number in (6, 7, 4, 5, 2)]
         lower, upper = slice(0, HALF), slice(HALF, SLOTS)
         copy_out([(0, 0)], product(0, 0, 1, accs[0][:, lower]))
         product(1, 0, 1, accs[1][:, lower])

@@ -130,9 +130,9 @@ def tile_attend_gsink_u_pl_kernel(tc, uT, vT, su, sv, y, offs, qoffs, out_0, out
         nc.scalar.copy(u_by_d[1][:, :, 2:LANES], u_last[:].rearrange("p e i -> p i e"))
         u_codes = sbuf([P, SLOTS], U32, "u_codes")
         u_scales = sbuf([P, SLOTS], U8, "u_scales")
-        for h in range(2):
-            cols = slice(h * HALF, (h + 1) * HALF)
-            nc.vector.quantize_mx(u_codes[:, cols].bitcast(E4M3), u_scales[:, cols], flat(u_by_d[h][:]))
+        for first, last in ((0, P), (P, HALF), (HALF, SLOTS)):
+            woven = u_by_d[first // HALF][:, first % HALF : first % HALF + last - first, :]
+            nc.vector.quantize_mx(u_codes[:, first:last].bitcast(E4M3), u_scales[:, first:last], flat(woven))
 
         vj_codes = sbuf([P, SLOTS], U32, "vj_codes", tag="u_pool2")
         vj_scales = sbuf([P, SLOTS], U8, "vj_scales")

@@ -83,9 +83,14 @@ def tile_attend_gsink_u_pl_kernel(tc, uT, vT, su, sv, y, offs, qoffs, out_0, out
         y_tile = [sbuf([P, SLOTS], F32, "y%d" % b, tag="v_pool%d" % b) for b in range(LANES)]
         for b in range(LANES):
             nc.sync.dma_start(y_tile[b][:], y[b * P : (b + 1) * P, :])
+        v_dealt = sbuf([P, SLOTS, LANES], BF16, "v_dealt")
+        nc.scalar.copy(
+            flat(v_dealt[:]).bitcast(F32).rearrange("p (r c n w) -> p c r n w", r=LANES, n=2, w=2),
+            flat(v_by_d[:]).bitcast(F32).rearrange("p (c n r w) -> p c r n w", r=LANES, n=2, w=2),
+        )
         vd_codes = sbuf([P, SLOTS], U32, "vd_codes", tag="u_pool1")
         vd_scales = sbuf([P, SLOTS], U8, "vd_scales")
-        nc.vector.quantize_mx(vd_codes[:].bitcast(E4M3), vd_scales[:], flat(v_by_d[:]))
+        nc.vector.quantize_mx(vd_codes[:].bitcast(E4M3), vd_scales[:], flat(v_dealt[:]))
 
         sv_listed = sbuf([P, SLOTS], F32, "sv_listed")
         nc.scalar.activation(sv_listed[:], sv_pool[:].indirect(jlist[:]), ACT.Copy)
@@ -107,12 +112,12 @@ def tile_attend_gsink_u_pl_kernel(tc, uT, vT, su, sv, y, offs, qoffs, out_0, out
         sv_row = sbuf([P, LANES, P], F32, "sv_row")
         nc.scalar.copy(sv_row[:], sv_spread[:])
 
-        v_words = flat(v_by_d[:]).bitcast(F32)
+        v_words = flat(v_dealt[:]).bitcast(F32)
         v_by_j = sbuf([P, LANES, P, LANES], BF16, "v_by_j")
         for pair in range(2):
             v_turned = bank(4 + pair, "v_turned%d" % pair)
             for r in range(LANES):
-                nc.tensor.transpose(v_turned[:, r, :], v_words[:, 2 * r + pair :: 2 * LANES], ident[:])
+                nc.tensor.transpose(v_turned[:, r, :], v_words[:, 2 * P * r + pair : 2 * P * (r + 1) : 2], ident[:])
             nc.scalar.copy(
                 v_by_j[:, 2 * pair : 2 * pair + 2, :, :],
                 flat(v_turned[:]).bitcast(BF16).rearrange("s (r p e) -> s e p r", r=LANES, e=2),
@@ -125,12 +130,17 @@ def tile_attend_gsink_u_pl_kernel(tc, uT, vT, su, sv, y, offs, qoffs, out_0, out
             nc.vector.tensor_copy(u_by_d[0][:, :, t], u_pool[t][:].indirect(half_list[0]))
             if t < 2:
                 nc.vector.tensor_copy(u_by_d[1][:, :, t], u_pool[t][:].indirect(half_list[1]))
-            else:
-                nc.scalar.activation(u_last[:, t - 2, :], u_pool[t][:].indirect(half_list[1]), ACT.Copy)
-        nc.scalar.copy(u_by_d[1][:, :, 2:LANES], u_last[:].rearrange("p e i -> p i e"))
+            elif t == 2:
+                nc.scalar.activation(u_last[:, 0, :], u_pool[t][:].indirect(half_list[1]), ACT.Copy)
+        tiles = [slice(n * P, (n + 1) * P) for n in range(2)]
+        for n in range(2):
+            entries = ilist[:, HALF_LIST + n * P // 16 : HALF_LIST + (n + 1) * P // 16]
+            nc.scalar.activation(u_last[:, 1, tiles[n]], u_pool[LANES - 1][:].indirect(entries), ACT.Copy)
+        for n in range(2):
+            nc.scalar.copy(u_by_d[1][:, tiles[n], 2:LANES], u_last[:, :, tiles[n]].rearrange("p e i -> p i e"))
         u_codes = sbuf([P, SLOTS], U32, "u_codes")
         u_scales = sbuf([P, SLOTS], U8, "u_scales")
-        for first, last in ((0, P), (P, HALF), (HALF, SLOTS)):
+        for first, last in ((b * P, (b + 1) * P) for b in range(LANES)):
             woven = u_by_d[first // HALF][:, first % HALF : first % HALF + last - first, :]
             nc.vector.quantize_mx(u_codes[:, first:last].bitcast(E4M3), u_scales[:, first:last], flat(woven))
 
@@ -138,10 +148,10 @@ def tile_attend_gsink_u_pl_kernel(tc, uT, vT, su, sv, y, offs, qoffs, out_0, out
         vj_scales = sbuf([P, SLOTS], U8, "vj_scales")
         nc.vector.quantize_mx(vj_codes[:].bitcast(E4M3), vj_scales[:], v_by_j[:].rearrange("s t p r -> s (t p r)"))
 
-        late = sbuf([P, 3, LANES, P], F32, "late", tag="u_by_d1")
-        early = sbuf([P, LANES, P], F32, "early", tag="u_last")
-        y_su = [sbuf([P, LANES, P], F32, "y_su0")[:], early[:], late[:, 1, :, :], late[:, 2, :, :]]
-        scaled = [late[:, 0, :, :]] + [sbuf([P, LANES, P], F32, "scaled%d" % b)[:] for b in range(1, LANES)]
+        late = sbuf([P, 2, LANES, P], F32, "late", tag="u_by_d1")
+        early = sbuf([P, 2, LANES, P], F32, "early", tag="u_last")
+        y_su = [sbuf([P, LANES, P], F32, "y_su0")[:], early[:, 1, :, :], late[:, 0, :, :], late[:, 1, :, :]]
+        scaled = [early[:, 0, :, :]] + [sbuf([P, LANES, P], F32, "scaled%d" % b)[:] for b in range(1, LANES)]
         for b in range(LANES):
             planes = y_su[b].rearrange("p r (c n) -> p c r n", n=RUN)
             rows = y_tile[b][:].rearrange("p (c n r) -> p c r n", n=RUN, r=LANES)
@@ -166,7 +176,7 @@ def tile_attend_gsink_u_pl_kernel(tc, uT, vT, su, sv, y, offs, qoffs, out_0, out
                 stop=True,
             )
             nc.vector.tensor_tensor(
-                scaled[b], sv_row[:], flat(score[:]).rearrange("p (s r) -> p r s", r=LANES), ALU.mult
+                scaled[b], sv_row[:], score[:], ALU.mult
             )
             nc.scalar.activation(expd[b][:], flat(scaled[b]), ACT.Exp, scale=su_col[:, b : b + 1], accum_out=r1[b][:])
 

@@ -25,9 +25,10 @@ HALF_LIST = HALF // 16
 SU_ROW = 63
 RUN = 4
 
-WIDTHS = (512, 512, 256, 256, 256, 256)
+WIDTHS = (512, 256, 256, 512, 512)
 SHARED = 3
 STARTS = [sum(WIDTHS[:c]) for c in range(len(WIDTHS))]
+SHARED_COLS = STARTS[SHARED]
 
 
 def tile_attend_gsink_u_pl_kernel(tc, uT, vT, su, sv, y, offs, qoffs, out_0, out_1, out_2):
@@ -46,7 +47,7 @@ def tile_attend_gsink_u_pl_kernel(tc, uT, vT, su, sv, y, offs, qoffs, out_0, out
         def flat(ap):
             return ap.rearrange("p a b -> p (a b)")
 
-        def round_on_gpsimd(dst, src):
+        def copy_on_gpsimd(dst, src):
             nc.gpsimd.tensor_scalar(dst, src, 1.0, 0.0, ALU.mult, ALU.add)
 
         jlist = lists.tile([P, SLOTS // 16], U16, name="jlist")
@@ -243,12 +244,19 @@ def tile_attend_gsink_u_pl_kernel(tc, uT, vT, su, sv, y, offs, qoffs, out_0, out
                 for r in range(LANES):
                     nc.tensor.transpose(quarter(f_turned[h], r, b), f_su[b][:, r * P : (r + 1) * P], ident[:])
 
+        tiles = [slice(b * P, (b + 1) * P) for b in range(LANES)]
+        halves = [slice(0, HALF), slice(HALF, SLOTS)]
+
+        def entries(first, count):
+            return ilist[:, first // 16 : (first + count) // 16]
+
         g_codes = sbuf([P, SLOTS], U32, "g_codes")
         g_scales = sbuf([P, SLOTS], U8, "g_scales")
-        g_planes = [sbuf([P, LANES, HALF], BF16, "g_planes%d" % h) for h in range(2)]
+        g_rows = sbuf([P, 6 * HALF], BF16, "g_rows")
+        g_planes = [g_rows[:, (2 - 2 * h) * HALF : (6 - 2 * h) * HALF].rearrange("s (r c) -> s r c", r=LANES) for h in range(2)]
         g_by_j = [sbuf([P, HALF, LANES], BF16, "g_by_j%d" % h) for h in range(2)]
 
-        def form_g(h):
+        def make_g(h):
             for r in range(LANES):
                 nc.vector.scalar_tensor_tensor(
                     g_planes[h][:, r, :],
@@ -258,33 +266,20 @@ def tile_attend_gsink_u_pl_kernel(tc, uT, vT, su, sv, y, offs, qoffs, out_0, out
                     ALU.mult,
                     ALU.subtract,
                 )
-
-        def weave_g(h):
-            nc.scalar.copy(
+            copy = nc.scalar.copy if h == 0 else nc.vector.tensor_copy
+            copy(
                 g_by_j[h][:, 0:P, :].rearrange("s (c n) r -> s c r n", n=RUN),
                 g_planes[h][:, :, 0:P].rearrange("s r (c n) -> s c r n", n=RUN),
             )
-            if h == 0:
-                round_on_gpsimd(g_by_j[h][:, P:HALF, :], g_planes[h][:, :, P:HALF].rearrange("s r c -> s c r"))
-            else:
-                nc.vector.tensor_copy(
-                    g_by_j[h][:, P:HALF, :].rearrange("s (c n) r -> s c r n", n=RUN),
-                    g_planes[h][:, :, P:HALF].rearrange("s r (c n) -> s c r n", n=RUN),
-                )
+            copy_on_gpsimd(g_by_j[h][:, P:HALF, :], g_planes[h][:, :, P:HALF].rearrange("s r c -> s c r"))
+            nc.vector.quantize_mx(g_codes[:, halves[h]].bitcast(E5M2), g_scales[:, halves[h]], flat(g_by_j[h][:]))
 
-        def quantise_g(h):
-            cols = slice(h * HALF, (h + 1) * HALF)
-            nc.vector.quantize_mx(g_codes[:, cols].bitcast(E5M2), g_scales[:, cols], flat(g_by_j[h][:]))
-
-        out_rows = out_0.rearrange("(p t) c -> p t c", t=LANES)
-
-        def product(t, first, count, acc):
-            cols = slice(t * P, (t + 1) * P)
-            sources = slice(first * HALF, (first + count) * HALF)
+        def product(t, sources, number, name):
+            acc = flat(bank(number, name)[:])[:, 0 : sources.stop - sources.start]
             nc.tensor.matmul_mx(
                 acc,
-                lhsT=vj_codes[:, cols].bitcast(E4M3),
-                lhsT_scale=vj_scales[:, cols],
+                lhsT=vj_codes[:, tiles[t]].bitcast(E4M3),
+                lhsT_scale=vj_scales[:, tiles[t]],
                 rhs=g_codes[:, sources].bitcast(E5M2),
                 rhs_scale=g_scales[:, sources],
                 start=True,
@@ -292,69 +287,52 @@ def tile_attend_gsink_u_pl_kernel(tc, uT, vT, su, sv, y, offs, qoffs, out_0, out
             )
             return acc
 
-        du = {}
+        def scatter_on_scalar(t, h, values):
+            nc.scalar.activation(window[t][:].indirect(entries(h * HALF, HALF)), values, ACT.Copy)
 
-        def copy_out(parts, acc, tag=None):
-            held = sbuf([P, len(parts) * HALF], F32, "du%d_%d" % parts[0], tag=tag)
-            nc.scalar.copy(held[:], acc)
-            for n, part in enumerate(parts):
-                du[part] = held[:, n * HALF : (n + 1) * HALF]
+        du = [[sbuf([P, HALF], F32, "du%d_%d" % (t, h)) for h in range(2)] for t in range(2)]
+        du = du + [sbuf([P, SLOTS], F32, "du2"), [sbuf([P, HALF], F32, "du3_%d" % h) for h in range(2)]]
+        ones = sbuf([P, 1], F32, "ones")
+        nc.vector.memset(ones[:], 1.0)
+        make_g(0)
+        for t in range(2):
+            nc.scalar.copy(du[t][0][:], product(t, halves[0], 4 + t, "du_a%d" % t))
+        for t in range(2):
+            scatter_on_scalar(t, 0, du[t][0][:])
+        make_g(1)
+        for t in range(2):
+            nc.vector.tensor_copy(du[t][1][:], product(t, halves[1], 2 + t, "du_b%d" % t))
+        for t in range(2):
+            nc.vector.tensor_copy(window[t][:].indirect(entries(HALF, HALF)), du[t][1][:])
+        nc.scalar.copy(du[2][:], product(2, slice(0, SLOTS), 2, "du_c2"))
+        last = product(3, slice(0, SLOTS), 3, "du_c3")
+        for h in range(2):
+            nc.scalar.copy(du[3][h][:], last[:, halves[h]])
+        nc.scalar.activation(window[2][:].indirect(ilist[:]), du[2][:], ACT.Copy, scale=ones[:])
+        nc.vector.tensor_copy(window[3][:].indirect(entries(0, HALF)), du[3][0][:])
+        scatter_on_scalar(3, 1, du[3][1][:])
 
-        def scatter(t, h):
-            target = window[t][:].indirect(ilist[:, h * HALF_LIST : (h + 1) * HALF_LIST])
-            if t == 2 or (t, h) == (1, 0):
-                nc.scalar.activation(target, du[t, h], ACT.Copy)
-            else:
-                nc.vector.tensor_copy(target, du[t, h])
-
-        form_g(0)
-        weave_g(0)
-        form_g(1)
-        quantise_g(0)
-        weave_g(1)
-        accs = [flat(bank(number, "du_acc%d" % number)[:]) for number in (6, 7, 4, 5, 2)]
-        lower, upper = slice(0, HALF), slice(HALF, SLOTS)
-        copy_out([(0, 0)], product(0, 0, 1, accs[0][:, lower]))
-        product(1, 0, 1, accs[1][:, lower])
-        quantise_g(1)
-        scatter(0, 0)
-        product(0, 1, 1, accs[1][:, upper])
-        copy_out([(1, 0), (0, 1)], accs[1])
-        scatter(0, 1)
-        scatter(1, 0)
-        copy_out([(1, 1)], product(1, 1, 1, accs[2][:, lower]))
-        product(2, 0, 2, accs[3])
-        product(3, 0, 2, accs[4])
-        copy_out([(2, 0)], accs[3][:, lower], tag="du0_0")
-        scatter(1, 1)
-        copy_out([(3, 0)], accs[4][:, lower], tag="du1_0")
-        scatter(2, 0)
-        copy_out([(2, 1)], accs[3][:, upper])
-        copy_out([(3, 1)], accs[4][:, upper], tag="du0_0")
-        scatter(3, 0)
-        scatter(2, 1)
-        scatter(3, 1)
-        spare = ["u_pool0", "u_pool1", "sv_pool", "u_pool3", "v_pool1", "v_pool2"]
-        o_by_d = [sbuf([P, width, LANES], BF16, "o_by_d%d" % c, tag=spare[c]) for c, width in enumerate(WIDTHS)]
-        own = STARTS[SHARED]
-        pairs_shared = sbuf([P, 2, own, 2], BF16, "pairs_shared")
-        pairs_own = sbuf([P, 2, POOL - own, 2], BF16, "pairs_own", tag="du0_0")
-
+        out_rows = out_0.rearrange("(p t) c -> p t c", t=LANES)
         for t in range(LANES):
             nc.sync.dma_start(out_rows[:, t, :], window[t][:])
-        nc.scalar.copy(pairs_shared[:, 1, :, 0], window[2][:, 0:own])
-        for t in range(2):
-            round_on_gpsimd(pairs_shared[:, 0, :, t], window[t][:, 0:own])
-        for t in range(LANES):
-            nc.vector.tensor_copy(pairs_own[:, t // 2, :, t % 2], window[t][:, own:POOL])
 
+        shared = sbuf([P, 2, SHARED_COLS, 2], BF16, "shared", tag="u_pool0")
+        own = sbuf([P, 2, POOL - SHARED_COLS, 2], BF16, "own", tag="du3_0")
+        for t in range(2):
+            copy_on_gpsimd(shared[:, 0, :, t], window[t][:, 0:SHARED_COLS])
+        nc.scalar.copy(shared[:, 1, :, 0], window[2][:, 0:SHARED_COLS])
+        for t in range(LANES):
+            nc.vector.tensor_copy(own[:, t // 2, :, t % 2], window[t][:, SHARED_COLS:POOL])
+
+        spare = ["u_pool1", "u_pool3", "sv_pool", "su_pool", "v_pool1", "v_pool2"]
+        o_by_d = [sbuf([P, width, LANES], BF16, "o_by_d%d" % c, tag=spare[c]) for c, width in enumerate(WIDTHS)]
         o_codes = sbuf([P, POOL], U32, "o_codes", tag="v_pool0")
         o_scales = sbuf([P, POOL], U8, "o_scales")
         words_out = out_1.rearrange("a p c l -> p (a c l)").bitcast(I32)
         scales_out = out_2.rearrange("a q c -> q (a c)").bitcast(I32)
 
         def weave_out(c, copy):
-            pairs, at = (pairs_shared, STARTS[c]) if c < SHARED else (pairs_own, STARTS[c] - own)
+            pairs, at = (shared, STARTS[c]) if c < SHARED else (own, STARTS[c] - SHARED_COLS)
             words = pairs[:].rearrange("p u c e -> p (u c e)").bitcast(F32).rearrange("p (u c) -> p c u", u=2)
             copy(flat(o_by_d[c][:]).bitcast(F32).rearrange("p (c u) -> p c u", u=2), words[:, at : at + WIDTHS[c], :])
 
@@ -366,18 +344,17 @@ def tile_attend_gsink_u_pl_kernel(tc, uT, vT, su, sv, y, offs, qoffs, out_0, out
             cols = slice(STARTS[first], STARTS[last] + WIDTHS[last])
             nc.sync.dma_start(words_out[:, cols], o_codes[:, cols].bitcast(I32))
 
-        for c in range(SHARED):
-            cols = slice(STARTS[c], STARTS[c] + WIDTHS[c])
-            nc.scalar.copy(pairs_shared[:, 1, cols, 1], window[3][:, cols])
-            if c < SHARED - 1:
-                weave_out(c, nc.scalar.copy)
-        for c in (5, 4, 3):
+        for c in range(2):
+            cols = slice(c * HALF * 2, (c + 1) * HALF * 2)
+            nc.scalar.copy(shared[:, 1, cols, 1], window[3][:, cols])
+            weave_out(c, nc.scalar.copy)
+        for c in range(SHARED, len(WIDTHS)):
             weave_out(c, nc.vector.tensor_copy)
-        for c in (0, 5, 4):
+        for c in range(SHARED, len(WIDTHS)):
             quantise_out(c)
-        weave_out(2, nc.vector.tensor_copy)
-        quantise_out(3)
-        store_codes(3, 5)
+        store_codes(SHARED, len(WIDTHS) - 1)
+        weave_out(2, nc.scalar.copy)
+        quantise_out(0)
         quantise_out(1)
         store_codes(0, 1)
         quantise_out(2)

@@ -266,16 +266,22 @@ def tile_attend_gsink_u_pl_kernel(tc, uT, vT, su, sv, y, offs, qoffs, out_0, out
                     ALU.mult,
                     ALU.subtract,
                 )
-            copy = nc.scalar.copy if h == 0 else nc.vector.tensor_copy
+
+        def weave_g(h, n, copy):
             copy(
-                g_by_j[h][:, 0:P, :].rearrange("s (c n) r -> s c r n", n=RUN),
-                g_planes[h][:, :, 0:P].rearrange("s r (c n) -> s c r n", n=RUN),
+                g_by_j[h][:, tiles[n], :].rearrange("s (c n) r -> s c r n", n=RUN),
+                g_planes[h][:, :, tiles[n]].rearrange("s r (c n) -> s c r n", n=RUN),
             )
-            copy_on_gpsimd(g_by_j[h][:, P:HALF, :], g_planes[h][:, :, P:HALF].rearrange("s r c -> s c r"))
-            nc.vector.quantize_mx(g_codes[:, halves[h]].bitcast(E5M2), g_scales[:, halves[h]], flat(g_by_j[h][:]))
+
+        def quantise_g(first, count):
+            woven = g_by_j[first // HALF][:, first % HALF : first % HALF + count, :]
+            cols = slice(first, first + count)
+            nc.vector.quantize_mx(g_codes[:, cols].bitcast(E5M2), g_scales[:, cols], flat(woven))
 
         def product(t, sources, number, name):
-            acc = flat(bank(number, name)[:])[:, 0 : sources.stop - sources.start]
+            return multiply(t, sources, flat(bank(number, name)[:])[:, 0 : sources.stop - sources.start])
+
+        def multiply(t, sources, acc):
             nc.tensor.matmul_mx(
                 acc,
                 lhsT=vj_codes[:, tiles[t]].bitcast(E4M3),
@@ -295,13 +301,23 @@ def tile_attend_gsink_u_pl_kernel(tc, uT, vT, su, sv, y, offs, qoffs, out_0, out
         ones = sbuf([P, 1], F32, "ones")
         nc.vector.memset(ones[:], 1.0)
         make_g(0)
+        weave_g(0, 0, nc.scalar.copy)
+        copy_on_gpsimd(g_by_j[0][:, P:HALF, :], g_planes[0][:, :, P:HALF].rearrange("s r c -> s c r"))
+        quantise_g(0, HALF)
         for t in range(2):
             nc.scalar.copy(du[t][0][:], product(t, halves[0], 4 + t, "du_a%d" % t))
         for t in range(2):
             scatter_on_scalar(t, 0, du[t][0][:])
         make_g(1)
-        for t in range(2):
-            nc.vector.tensor_copy(du[t][1][:], product(t, halves[1], 2 + t, "du_b%d" % t))
+        for n in range(2):
+            weave_g(1, n, nc.vector.tensor_copy)
+        for n in range(2):
+            quantise_g(HALF + n * P, P)
+        acc = bank(2, "du_b0")
+        for n in range(2):
+            multiply(0, tiles[2 + n], acc[:, n, :])
+        nc.vector.tensor_copy(du[0][1][:], flat(acc[:])[:, 0:HALF])
+        nc.vector.tensor_copy(du[1][1][:], product(1, halves[1], 3, "du_b1"))
         for t in range(2):
             nc.vector.tensor_copy(window[t][:].indirect(entries(HALF, HALF)), du[t][1][:])
         nc.scalar.copy(du[2][:], product(2, slice(0, SLOTS), 2, "du_c2"))

@@ -191,11 +191,11 @@ def tile_attend_gsink_u_pl_kernel(tc, uT, vT, su, sv, y, offs, qoffs, out_0, out
         for b in range(LANES):
             for r in range(LANES):
                 nc.tensor.transpose(quarter(y_turned[b // 2], r, b), y_su[b][:, r, :], ident[:])
-        y_both = [[sbuf([P, HALF], F32, "y_both%d_%d" % (h, r)) for r in range(LANES)] for h in range(2)]
+        y_both = [sbuf([P, LANES, HALF], F32, "y_both%d" % h) for h in range(2)]
 
         def finish_y(h):
             for r in range(LANES):
-                nc.scalar.activation(y_both[h][r][:], lane_of(y_turned[h], r), ACT.Copy, scale=sv_col[:, r : r + 1])
+                nc.scalar.activation(y_both[h][:, r, :], lane_of(y_turned[h], r), ACT.Copy, scale=sv_col[:, r : r + 1])
 
         rinv = [sbuf([P, 1], F32, "rinv%d" % b) for b in range(LANES)]
         f_even = [sbuf([P, SLOTS], F32, "f_even0", tag="sv_row"), sbuf([P, SLOTS], F32, "f_even1")]
@@ -236,7 +236,8 @@ def tile_attend_gsink_u_pl_kernel(tc, uT, vT, su, sv, y, offs, qoffs, out_0, out
             even, odd = 2 * h, 2 * h + 1
             nc.scalar.activation(f_su[even][:], f_even[h][:], ACT.Copy, scale=su_col[:, even : even + 1])
             nc.vector.tensor_scalar(f_su[odd][:], expd[odd][:], rinv[odd][:], su_col[:, odd : odd + 1], ALU.mult, ALU.mult)
-            finish_y(h)
+            if h == 0:
+                finish_y(h)
         f_turned = []
         for h in range(2):
             f_turned.append([bank(2 - 2 * h + k, "f_turned%d_%d" % (h, k)) for k in range(2)])
@@ -252,25 +253,23 @@ def tile_attend_gsink_u_pl_kernel(tc, uT, vT, su, sv, y, offs, qoffs, out_0, out
 
         g_codes = sbuf([P, SLOTS], U32, "g_codes")
         g_scales = sbuf([P, SLOTS], U8, "g_scales")
-        g_rows = sbuf([P, 6 * HALF], BF16, "g_rows")
-        g_planes = [g_rows[:, (2 - 2 * h) * HALF : (6 - 2 * h) * HALF].rearrange("s (r c) -> s r c", r=LANES) for h in range(2)]
+        plan = [sbuf([P, LANES, HALF], F32, "plan%d" % h) for h in range(2)]
         g_by_j = [sbuf([P, HALF, LANES], BF16, "g_by_j%d" % h) for h in range(2)]
 
-        def make_g(h):
+        def scale_plan(h):
             for r in range(LANES):
-                nc.vector.scalar_tensor_tensor(
-                    g_planes[h][:, r, :],
-                    lane_of(f_turned[h], r),
-                    csv[r // 2][:, r % 2 : r % 2 + 1],
-                    y_both[h][r][:],
-                    ALU.mult,
-                    ALU.subtract,
-                )
+                factor = csv[r // 2][:, r % 2 : r % 2 + 1]
+                if h == 0 and r < 2:
+                    nc.vector.tensor_scalar(plan[h][:, r, :], lane_of(f_turned[h], r), factor, None, ALU.mult)
+                else:
+                    nc.scalar.activation(plan[h][:, r, :], lane_of(f_turned[h], r), ACT.Copy, scale=factor)
 
-        def weave_g(h, n, copy):
-            copy(
-                g_by_j[h][:, tiles[n], :].rearrange("s (c n) r -> s c r n", n=RUN),
-                g_planes[h][:, :, tiles[n]].rearrange("s r (c n) -> s c r n", n=RUN),
+        def make_g(h, n):
+            nc.vector.tensor_tensor(
+                g_by_j[h][:, tiles[n], :].rearrange("s (c n) r -> s c r n", n=2),
+                plan[h][:, :, tiles[n]].rearrange("s r (c n) -> s c r n", n=2),
+                y_both[h][:, :, tiles[n]].rearrange("s r (c n) -> s c r n", n=2),
+                ALU.subtract,
             )
 
         def quantise_g(first, count):
@@ -300,17 +299,22 @@ def tile_attend_gsink_u_pl_kernel(tc, uT, vT, su, sv, y, offs, qoffs, out_0, out
         du = du + [sbuf([P, SLOTS], F32, "du2"), [sbuf([P, HALF], F32, "du3_%d" % h) for h in range(2)]]
         ones = sbuf([P, 1], F32, "ones")
         nc.vector.memset(ones[:], 1.0)
-        make_g(0)
-        weave_g(0, 0, nc.scalar.copy)
-        copy_on_gpsimd(g_by_j[0][:, P:HALF, :], g_planes[0][:, :, P:HALF].rearrange("s r c -> s c r"))
-        quantise_g(0, HALF)
-        for t in range(2):
-            nc.scalar.copy(du[t][0][:], product(t, halves[0], 4 + t, "du_a%d" % t))
+        scale_plan(0)
+        finish_y(1)
+        for n in range(2):
+            make_g(0, n)
+        for n in range(2):
+            quantise_g(n * P, P)
+        acc = bank(4, "du_a0")
+        for n in range(2):
+            multiply(0, tiles[n], acc[:, n, :])
+        nc.scalar.copy(du[0][0][:], flat(acc[:])[:, 0:HALF])
+        nc.scalar.copy(du[1][0][:], product(1, halves[0], 5, "du_a1"))
+        scale_plan(1)
         for t in range(2):
             scatter_on_scalar(t, 0, du[t][0][:])
-        make_g(1)
         for n in range(2):
-            weave_g(1, n, nc.vector.tensor_copy)
+            make_g(1, n)
         for n in range(2):
             quantise_g(HALF + n * P, P)
         acc = bank(2, "du_b0")

@@ -182,10 +182,40 @@ def tile_attend_gsink_u_pl_kernel(tc, uT, vT, su, sv, y, offs, qoffs, out_0, out
             nc.scalar.activation(expd[b][:], flat(scaled[b]), ACT.Exp, scale=su_col[:, b : b + 1], accum_out=r1[b][:])
 
         def quarter(banks, r, b):
-            return banks[r // 2][:, 2 * (r % 2) + b % 2, :]
+            return banks[r % 2][:, 2 * (r // 2) + b % 2, :]
 
         def lane_of(banks, r):
-            return flat(banks[r // 2][:])[:, r % 2 * HALF : (r % 2 + 1) * HALF]
+            return flat(banks[r % 2][:])[:, r // 2 * HALF : (r // 2 + 1) * HALF]
+
+        rinv = [sbuf([P, 1], F32, "rinv%d" % b) for b in range(LANES)]
+        f_tile = [sbuf([P, SLOTS], F32, "f%d" % b, tag="sv_row" if b == 0 else None) for b in range(LANES)]
+        sums_turned = [bank(4 + h, "sums_turned%d" % h) for h in range(2)]
+        for b in range(LANES):
+            nc.vector.reciprocal(rinv[b][:], r1[b][:])
+        for b in range(LANES - 1):
+            nc.vector.tensor_scalar(f_tile[b][:], expd[b][:], rinv[b][:], None, ALU.mult)
+        for h in range(2):
+            cols = slice(h * HALF, (h + 1) * HALF)
+            nc.vector.tensor_scalar(f_tile[3][:, cols], expd[3][:, cols], rinv[3][:], None, ALU.mult)
+        for b in range(LANES):
+            for r in range(LANES):
+                nc.tensor.matmul(
+                    sums_turned[r // 2][:, r % 2, :],
+                    f_tile[b][:, r * P : (r + 1) * P],
+                    ident[:],
+                    start=b == 0 and r % 2 == 0,
+                    stop=b == LANES - 1 and r % 2 == 1,
+                    is_transpose=True,
+                )
+        c1 = [sbuf([P, 2], F32, "c1_%d" % h) for h in range(2)]
+        cinv = [sbuf([P, 2], F32, "cinv%d" % h) for h in range(2)]
+        csv = [sbuf([P, 2], F32, "csv%d" % h) for h in range(2)]
+        for h in range(2):
+            nc.vector.tensor_reduce(c1[h][:], sums_turned[h][:, 0:2, :], mybir.AxisListType.X, ALU.add)
+        for h in range(2):
+            nc.vector.reciprocal(cinv[h][:], c1[h][:])
+        for h in range(2):
+            nc.vector.tensor_tensor(csv[h][:], cinv[h][:], sv_col[:, 2 * h : 2 * h + 2], ALU.mult)
 
         y_turned = [[bank(6 * h + k, "y_turned%d_%d" % (h, k)) for k in range(2)] for h in range(2)]
         for b in range(LANES):
@@ -197,52 +227,22 @@ def tile_attend_gsink_u_pl_kernel(tc, uT, vT, su, sv, y, offs, qoffs, out_0, out
             for r in range(LANES):
                 nc.scalar.activation(y_both[h][:, r, :], lane_of(y_turned[h], r), ACT.Copy, scale=sv_col[:, r : r + 1])
 
-        rinv = [sbuf([P, 1], F32, "rinv%d" % b) for b in range(LANES)]
-        f_even = [sbuf([P, SLOTS], F32, "f_even0", tag="sv_row"), sbuf([P, SLOTS], F32, "f_even1")]
-        f_pair = [[sbuf([P, HALF], F32, "f_pair%d_%d" % (k, h)) for h in range(2)] for k in range(2)]
-        sums_turned = [bank(4 + h, "sums_turned%d" % h) for h in range(2)]
-        for b in range(LANES):
-            nc.vector.reciprocal(rinv[b][:], r1[b][:])
-        for k in range(2):
-            nc.vector.tensor_scalar(f_even[k][:], expd[2 * k][:], rinv[2 * k][:], None, ALU.mult)
-        for k in range(2):
-            for h in range(2):
-                cols = slice(h * HALF, (h + 1) * HALF)
-                nc.vector.scalar_tensor_tensor(
-                    f_pair[k][h][:], expd[2 * k + 1][:, cols], rinv[2 * k + 1][:], f_even[k][:, cols], ALU.mult, ALU.add
-                )
-                for e in range(2):
-                    nc.tensor.matmul(
-                        sums_turned[h][:, e, :],
-                        f_pair[k][h][:, e * P : (e + 1) * P],
-                        ident[:],
-                        start=k == 0 and e == 0,
-                        stop=k == 1 and e == 1,
-                        is_transpose=True,
-                    )
-        c1 = [sbuf([P, 2], F32, "c1_%d" % h) for h in range(2)]
-        cinv = [sbuf([P, 2], F32, "cinv%d" % h) for h in range(2)]
-        csv = [sbuf([P, 2], F32, "csv%d" % h) for h in range(2)]
-        for h in range(2):
-            nc.vector.tensor_reduce(c1[h][:], sums_turned[h][:, 0:2, :], mybir.AxisListType.X, ALU.add)
-        for h in range(2):
-            nc.vector.reciprocal(cinv[h][:], c1[h][:])
-        for h in range(2):
-            nc.vector.tensor_tensor(csv[h][:], cinv[h][:], sv_col[:, 2 * h : 2 * h + 2], ALU.mult)
-
-        f_tags = ["scaled1", "scaled2", "scaled3", "f_pair1_1"]
+        f_tags = ["scaled1", "scaled2", "scaled3", "f_su3"]
         f_su = [sbuf([P, SLOTS], F32, "f_su%d" % b, tag=f_tags[b]) for b in range(LANES)]
         for h in range(2):
             even, odd = 2 * h, 2 * h + 1
-            nc.scalar.activation(f_su[even][:], f_even[h][:], ACT.Copy, scale=su_col[:, even : even + 1])
+            if h == 0:
+                nc.scalar.activation(f_su[even][:], f_tile[even][:], ACT.Copy, scale=su_col[:, even : even + 1])
+            else:
+                nc.vector.tensor_scalar(f_su[even][:], f_tile[even][:], su_col[:, even : even + 1], None, ALU.mult)
             nc.vector.tensor_scalar(f_su[odd][:], expd[odd][:], rinv[odd][:], su_col[:, odd : odd + 1], ALU.mult, ALU.mult)
             if h == 0:
                 finish_y(h)
         f_turned = []
         for h in range(2):
             f_turned.append([bank(2 - 2 * h + k, "f_turned%d_%d" % (h, k)) for k in range(2)])
-            for b in (2 * h, 2 * h + 1):
-                for r in range(LANES):
+            for r in range(LANES):
+                for b in (2 * h, 2 * h + 1):
                     nc.tensor.transpose(quarter(f_turned[h], r, b), f_su[b][:, r * P : (r + 1) * P], ident[:])
 
         tiles = [slice(b * P, (b + 1) * P) for b in range(LANES)]
@@ -254,12 +254,12 @@ def tile_attend_gsink_u_pl_kernel(tc, uT, vT, su, sv, y, offs, qoffs, out_0, out
         g_codes = sbuf([P, SLOTS], U32, "g_codes")
         g_scales = sbuf([P, SLOTS], U8, "g_scales")
         plan = [sbuf([P, LANES, HALF], F32, "plan%d" % h) for h in range(2)]
-        g_by_j = [sbuf([P, HALF, LANES], BF16, "g_by_j%d" % h) for h in range(2)]
+        g_by_j = [sbuf([P, HALF, LANES], BF16, "g_by_j")] * 2
 
         def scale_plan(h):
             for r in range(LANES):
                 factor = csv[r // 2][:, r % 2 : r % 2 + 1]
-                if h == 0 and r < 2:
+                if h == 0 and r % 2 == 0:
                     nc.vector.tensor_scalar(plan[h][:, r, :], lane_of(f_turned[h], r), factor, None, ALU.mult)
                 else:
                     nc.scalar.activation(plan[h][:, r, :], lane_of(f_turned[h], r), ACT.Copy, scale=factor)
@@ -296,7 +296,9 @@ def tile_attend_gsink_u_pl_kernel(tc, uT, vT, su, sv, y, offs, qoffs, out_0, out
             nc.scalar.activation(window[t][:].indirect(entries(h * HALF, HALF)), values, ACT.Copy)
 
         du = [[sbuf([P, HALF], F32, "du%d_%d" % (t, h)) for h in range(2)] for t in range(2)]
-        du = du + [sbuf([P, SLOTS], F32, "du2"), [sbuf([P, HALF], F32, "du3_%d" % h) for h in range(2)]]
+        own_cols = POOL - SHARED_COLS
+        row = sbuf([P, HALF + 2 * own_cols], F32, "row")
+        du = du + [sbuf([P, SLOTS], F32, "du2")]
         ones = sbuf([P, 1], F32, "ones")
         nc.vector.memset(ones[:], 1.0)
         scale_plan(0)
@@ -325,24 +327,25 @@ def tile_attend_gsink_u_pl_kernel(tc, uT, vT, su, sv, y, offs, qoffs, out_0, out
         for t in range(2):
             nc.vector.tensor_copy(window[t][:].indirect(entries(HALF, HALF)), du[t][1][:])
         nc.scalar.copy(du[2][:], product(2, slice(0, SLOTS), 2, "du_c2"))
-        last = product(3, slice(0, SLOTS), 3, "du_c3")
-        for h in range(2):
-            nc.scalar.copy(du[3][h][:], last[:, halves[h]])
+        nc.scalar.copy(row[:, 0:SLOTS], product(3, slice(0, SLOTS), 3, "du_c3"))
         nc.scalar.activation(window[2][:].indirect(ilist[:]), du[2][:], ACT.Copy, scale=ones[:])
-        nc.vector.tensor_copy(window[3][:].indirect(entries(0, HALF)), du[3][0][:])
-        scatter_on_scalar(3, 1, du[3][1][:])
+        nc.vector.tensor_copy(window[3][:].indirect(entries(HALF, HALF)), row[:, halves[1]])
+        scatter_on_scalar(3, 0, row[:, halves[0]])
 
         out_rows = out_0.rearrange("(p t) c -> p t c", t=LANES)
         for t in range(LANES):
             nc.sync.dma_start(out_rows[:, t, :], window[t][:])
 
         shared = sbuf([P, 2, SHARED_COLS, 2], BF16, "shared", tag="u_pool0")
-        own = sbuf([P, 2, POOL - SHARED_COLS, 2], BF16, "own", tag="du3_0")
+        own = row[:, HALF:].bitcast(BF16).rearrange("p (u c e) -> p u c e", u=2, e=2)
         for t in range(2):
             copy_on_gpsimd(shared[:, 0, :, t], window[t][:, 0:SHARED_COLS])
         nc.scalar.copy(shared[:, 1, :, 0], window[2][:, 0:SHARED_COLS])
-        for t in range(LANES):
+        for t in range(LANES - 1):
             nc.vector.tensor_copy(own[:, t // 2, :, t % 2], window[t][:, SHARED_COLS:POOL])
+        for c in range(SHARED, len(WIDTHS)):
+            at = STARTS[c] - SHARED_COLS
+            nc.vector.tensor_copy(own[:, 1, at : at + WIDTHS[c], 1], window[3][:, STARTS[c] : STARTS[c] + WIDTHS[c]])
 
         spare = ["u_pool1", "u_pool3", "sv_pool", "su_pool", "v_pool1", "v_pool2"]
         o_by_d = [sbuf([P, width, LANES], BF16, "o_by_d%d" % c, tag=spare[c]) for c, width in enumerate(WIDTHS)]
@@ -352,8 +355,8 @@ def tile_attend_gsink_u_pl_kernel(tc, uT, vT, su, sv, y, offs, qoffs, out_0, out
         scales_out = out_2.rearrange("a q c -> q (a c)").bitcast(I32)
 
         def weave_out(c, copy):
-            pairs, at = (shared, STARTS[c]) if c < SHARED else (own, STARTS[c] - SHARED_COLS)
-            words = pairs[:].rearrange("p u c e -> p (u c e)").bitcast(F32).rearrange("p (u c) -> p c u", u=2)
+            pairs, at = (shared[:], STARTS[c]) if c < SHARED else (own, STARTS[c] - SHARED_COLS)
+            words = pairs.rearrange("p u c e -> p (u c e)").bitcast(F32).rearrange("p (u c) -> p c u", u=2)
             copy(flat(o_by_d[c][:]).bitcast(F32).rearrange("p (c u) -> p c u", u=2), words[:, at : at + WIDTHS[c], :])
 
         def quantise_out(c):

@@ -125,20 +125,17 @@ def tile_attend_gsink_u_pl_kernel(tc, uT, vT, su, sv, y, offs, qoffs, out_0, out
             )
 
         u_by_d = [sbuf([P, HALF, LANES], BF16, "u_by_d%d" % h) for h in range(2)]
-        u_last = sbuf([P, 2, HALF], BF16, "u_last")
         half_list = [ilist[:, h * HALF_LIST : (h + 1) * HALF_LIST] for h in range(2)]
         for t in range(LANES):
             nc.vector.tensor_copy(u_by_d[0][:, :, t], u_pool[t][:].indirect(half_list[0]))
             if t < 2:
                 nc.vector.tensor_copy(u_by_d[1][:, :, t], u_pool[t][:].indirect(half_list[1]))
             elif t == 2:
-                nc.scalar.activation(u_last[:, 0, :], u_pool[t][:].indirect(half_list[1]), ACT.Copy)
+                nc.scalar.activation(u_by_d[1][:, :, t], u_pool[t][:].indirect(half_list[1]), ACT.Copy)
         tiles = [slice(n * P, (n + 1) * P) for n in range(2)]
         for n in range(2):
             entries = ilist[:, HALF_LIST + n * P // 16 : HALF_LIST + (n + 1) * P // 16]
-            nc.scalar.activation(u_last[:, 1, tiles[n]], u_pool[LANES - 1][:].indirect(entries), ACT.Copy)
-        for n in range(2):
-            nc.scalar.copy(u_by_d[1][:, tiles[n], 2:LANES], u_last[:, :, tiles[n]].rearrange("p e i -> p i e"))
+            nc.scalar.activation(u_by_d[1][:, tiles[n], LANES - 1], u_pool[LANES - 1][:].indirect(entries), ACT.Copy)
         u_codes = sbuf([P, SLOTS], U32, "u_codes")
         u_scales = sbuf([P, SLOTS], U8, "u_scales")
         for first, last in ((b * P, (b + 1) * P) for b in range(LANES)):
@@ -150,7 +147,7 @@ def tile_attend_gsink_u_pl_kernel(tc, uT, vT, su, sv, y, offs, qoffs, out_0, out
         nc.vector.quantize_mx(vj_codes[:].bitcast(E4M3), vj_scales[:], v_by_j[:].rearrange("s t p r -> s (t p r)"))
 
         late = sbuf([P, 2, LANES, P], F32, "late", tag="u_by_d1")
-        early = sbuf([P, 2, LANES, P], F32, "early", tag="u_last")
+        early = sbuf([P, 2, LANES, P], F32, "early", tag="u_pool3")
         y_su = [sbuf([P, LANES, P], F32, "y_su0")[:], early[:, 1, :, :], late[:, 0, :, :], late[:, 1, :, :]]
         scaled = [early[:, 0, :, :]] + [sbuf([P, LANES, P], F32, "scaled%d" % b)[:] for b in range(1, LANES)]
         for b in range(LANES):
@@ -166,19 +163,19 @@ def tile_attend_gsink_u_pl_kernel(tc, uT, vT, su, sv, y, offs, qoffs, out_0, out
         r1 = [sbuf([P, 1], F32, "r1_%d" % b) for b in range(LANES)]
         for b in range(LANES):
             cols = slice(b * P, (b + 1) * P)
-            score = bank(b, "score%d" % b)
-            nc.tensor.matmul_mx(
-                flat(score[:]),
-                lhsT=u_codes[:, cols].bitcast(E4M3),
-                lhsT_scale=u_scales[:, cols],
-                rhs=vd_codes[:].bitcast(E4M3),
-                rhs_scale=vd_scales[:],
-                start=True,
-                stop=True,
-            )
-            nc.vector.tensor_tensor(
-                scaled[b], sv_row[:], score[:], ALU.mult
-            )
+            for number, lanes in ([(0, slice(0, 2)), (5, slice(2, 4))] if b == 0 else [(b, slice(0, LANES))]):
+                score = bank(number, "score%d_%d" % (b, number))
+                slots = slice(lanes.start * P, lanes.stop * P)
+                nc.tensor.matmul_mx(
+                    flat(score[:, lanes, :]),
+                    lhsT=u_codes[:, cols].bitcast(E4M3),
+                    lhsT_scale=u_scales[:, cols],
+                    rhs=vd_codes[:, slots].bitcast(E4M3),
+                    rhs_scale=vd_scales[:, slots],
+                    start=True,
+                    stop=True,
+                )
+                nc.vector.tensor_tensor(scaled[b][:, lanes, :], sv_row[:, lanes, :], score[:, lanes, :], ALU.mult)
             nc.scalar.activation(expd[b][:], flat(scaled[b]), ACT.Exp, scale=su_col[:, b : b + 1], accum_out=r1[b][:])
 
         def quarter(banks, r, b):
@@ -254,7 +251,9 @@ def tile_attend_gsink_u_pl_kernel(tc, uT, vT, su, sv, y, offs, qoffs, out_0, out
         g_codes = sbuf([P, SLOTS], U32, "g_codes")
         g_scales = sbuf([P, SLOTS], U8, "g_scales")
         plan = [sbuf([P, LANES, HALF], F32, "plan%d" % h) for h in range(2)]
-        g_by_j = [sbuf([P, HALF, LANES], BF16, "g_by_j")] * 2
+        own_cols = POOL - SHARED_COLS
+        row = sbuf([P, 3 * HALF + 2 * own_cols], F32, "row")
+        g_by_j = [row[:, 0:SLOTS].bitcast(BF16).rearrange("s (i r) -> s i r", r=LANES)] * 2
 
         def scale_plan(h):
             for r in range(LANES):
@@ -296,9 +295,6 @@ def tile_attend_gsink_u_pl_kernel(tc, uT, vT, su, sv, y, offs, qoffs, out_0, out
             nc.scalar.activation(window[t][:].indirect(entries(h * HALF, HALF)), values, ACT.Copy)
 
         du = [[sbuf([P, HALF], F32, "du%d_%d" % (t, h)) for h in range(2)] for t in range(2)]
-        own_cols = POOL - SHARED_COLS
-        row = sbuf([P, HALF + 2 * own_cols], F32, "row")
-        du = du + [sbuf([P, SLOTS], F32, "du2")]
         ones = sbuf([P, 1], F32, "ones")
         nc.vector.memset(ones[:], 1.0)
         scale_plan(0)
@@ -326,10 +322,17 @@ def tile_attend_gsink_u_pl_kernel(tc, uT, vT, su, sv, y, offs, qoffs, out_0, out
         nc.vector.tensor_copy(du[1][1][:], product(1, halves[1], 3, "du_b1"))
         for t in range(2):
             nc.vector.tensor_copy(window[t][:].indirect(entries(HALF, HALF)), du[t][1][:])
-        nc.scalar.copy(du[2][:], product(2, slice(0, SLOTS), 2, "du_c2"))
-        nc.scalar.copy(row[:, 0:SLOTS], product(3, slice(0, SLOTS), 3, "du_c3"))
-        nc.scalar.activation(window[2][:].indirect(ilist[:]), du[2][:], ACT.Copy, scale=ones[:])
-        nc.vector.tensor_copy(window[3][:].indirect(entries(HALF, HALF)), row[:, halves[1]])
+        for h, planes, number in ((1, (2, 3), 7), (0, (3, 2), 6)):
+            acc = flat(bank(number, "du_late%d" % h)[:])
+            for n, t in enumerate(planes):
+                multiply(t, halves[h], acc[:, halves[n]])
+            if h == 1:
+                nc.scalar.copy(row[:, SLOTS : 2 * SLOTS], acc)
+            else:
+                for n in range(2):
+                    nc.vector.tensor_copy(row[:, halves[n]], acc[:, halves[n]])
+        nc.scalar.activation(window[2][:].indirect(ilist[:]), row[:, HALF : 3 * HALF], ACT.Copy, scale=ones[:])
+        nc.vector.tensor_copy(window[3][:].indirect(entries(HALF, HALF)), row[:, 3 * HALF : 4 * HALF])
         scatter_on_scalar(3, 0, row[:, halves[0]])
 
         out_rows = out_0.rearrange("(p t) c -> p t c", t=LANES)
@@ -337,7 +340,7 @@ def tile_attend_gsink_u_pl_kernel(tc, uT, vT, su, sv, y, offs, qoffs, out_0, out
             nc.sync.dma_start(out_rows[:, t, :], window[t][:])
 
         shared = sbuf([P, 2, SHARED_COLS, 2], BF16, "shared", tag="u_pool0")
-        own = row[:, HALF:].bitcast(BF16).rearrange("p (u c e) -> p u c e", u=2, e=2)
+        own = row[:, 3 * HALF :].bitcast(BF16).rearrange("p (u c e) -> p u c e", u=2, e=2)
         for t in range(2):
             copy_on_gpsimd(shared[:, 0, :, t], window[t][:, 0:SHARED_COLS])
         nc.scalar.copy(shared[:, 1, :, 0], window[2][:, 0:SHARED_COLS])

@@ -25,10 +25,10 @@ HALF_LIST = HALF // 16
 SU_ROW = 63
 RUN = 4
 
-WIDTHS = (512, 256, 256, 512, 512)
-SHARED = 3
-STARTS = [sum(WIDTHS[:c]) for c in range(len(WIDTHS))]
-SHARED_COLS = STARTS[SHARED]
+WIDTHS = (512, 512, 512, 256, 256)
+OWN = 2
+STARTS = [sum(WIDTHS[:c]) for c in range(len(WIDTHS) + 1)]
+GP_FIRST = 1152
 
 
 def tile_attend_gsink_u_pl_kernel(tc, uT, vT, su, sv, y, offs, qoffs, out_0, out_1, out_2):
@@ -185,12 +185,13 @@ def tile_attend_gsink_u_pl_kernel(tc, uT, vT, su, sv, y, offs, qoffs, out_0, out
             return flat(banks[r % 2][:])[:, r // 2 * HALF : (r // 2 + 1) * HALF]
 
         rinv = [sbuf([P, 1], F32, "rinv%d" % b) for b in range(LANES)]
-        f_tile = [sbuf([P, SLOTS], F32, "f%d" % b, tag="sv_row" if b == 0 else None) for b in range(LANES)]
+        held = sbuf([P, 2, SLOTS], F32, "held", tag="scaled3")
+        f_tile = [sbuf([P, SLOTS], F32, "f0", tag="sv_row"), sbuf([P, SLOTS], F32, "f1"), held[:, 0, :], sbuf([P, SLOTS], F32, "f3")]
         sums_turned = [bank(4 + h, "sums_turned%d" % h) for h in range(2)]
         for b in range(LANES):
             nc.vector.reciprocal(rinv[b][:], r1[b][:])
         for b in range(LANES - 1):
-            nc.vector.tensor_scalar(f_tile[b][:], expd[b][:], rinv[b][:], None, ALU.mult)
+            nc.vector.tensor_scalar(f_tile[b][:, 0:SLOTS], expd[b][:], rinv[b][:], None, ALU.mult)
         for h in range(2):
             cols = slice(h * HALF, (h + 1) * HALF)
             nc.vector.tensor_scalar(f_tile[3][:, cols], expd[3][:, cols], rinv[3][:], None, ALU.mult)
@@ -224,15 +225,15 @@ def tile_attend_gsink_u_pl_kernel(tc, uT, vT, su, sv, y, offs, qoffs, out_0, out
             for r in range(LANES):
                 nc.scalar.activation(y_both[h][:, r, :], lane_of(y_turned[h], r), ACT.Copy, scale=sv_col[:, r : r + 1])
 
-        f_tags = ["scaled1", "scaled2", "scaled3", "f_su3"]
-        f_su = [sbuf([P, SLOTS], F32, "f_su%d" % b, tag=f_tags[b]) for b in range(LANES)]
+        f_su = [sbuf([P, SLOTS], F32, "f_su0", tag="scaled1")[:], held[:, 1, :]]
+        f_su += [sbuf([P, SLOTS], F32, "f_su2", tag="scaled2")[:], sbuf([P, SLOTS], F32, "f_su3", tag="f3")[:]]
         for h in range(2):
             even, odd = 2 * h, 2 * h + 1
             if h == 0:
-                nc.scalar.activation(f_su[even][:], f_tile[even][:], ACT.Copy, scale=su_col[:, even : even + 1])
+                nc.scalar.activation(f_su[even], f_tile[even][:, 0:SLOTS], ACT.Copy, scale=su_col[:, even : even + 1])
             else:
-                nc.vector.tensor_scalar(f_su[even][:], f_tile[even][:], su_col[:, even : even + 1], None, ALU.mult)
-            nc.vector.tensor_scalar(f_su[odd][:], expd[odd][:], rinv[odd][:], su_col[:, odd : odd + 1], ALU.mult, ALU.mult)
+                nc.vector.tensor_scalar(f_su[even], f_tile[even][:, 0:SLOTS], su_col[:, even : even + 1], None, ALU.mult)
+            nc.vector.tensor_scalar(f_su[odd], expd[odd][:], rinv[odd][:], su_col[:, odd : odd + 1], ALU.mult, ALU.mult)
             if h == 0:
                 finish_y(h)
         f_turned = []
@@ -251,8 +252,7 @@ def tile_attend_gsink_u_pl_kernel(tc, uT, vT, su, sv, y, offs, qoffs, out_0, out
         g_codes = sbuf([P, SLOTS], U32, "g_codes")
         g_scales = sbuf([P, SLOTS], U8, "g_scales")
         plan = [sbuf([P, LANES, HALF], F32, "plan%d" % h) for h in range(2)]
-        own_cols = POOL - SHARED_COLS
-        row = sbuf([P, 3 * HALF + 2 * own_cols], F32, "row")
+        row = sbuf([P, 3 * HALF + 2 * POOL], F32, "row", tag="u_pool0")
         g_by_j = [row[:, 0:SLOTS].bitcast(BF16).rearrange("s (i r) -> s i r", r=LANES)] * 2
 
         def scale_plan(h):
@@ -339,16 +339,20 @@ def tile_attend_gsink_u_pl_kernel(tc, uT, vT, su, sv, y, offs, qoffs, out_0, out
         for t in range(LANES):
             nc.sync.dma_start(out_rows[:, t, :], window[t][:])
 
-        shared = sbuf([P, 2, SHARED_COLS, 2], BF16, "shared", tag="u_pool0")
-        own = row[:, 3 * HALF :].bitcast(BF16).rearrange("p (u c e) -> p u c e", u=2, e=2)
+        pairs = row[:, 3 * HALF :].bitcast(BF16).rearrange("p (u c e) -> p u c e", u=2, e=2)
+        words = row[:, 3 * HALF :].rearrange("p (u c) -> p c u", u=2)
+
+        def round_lane(copy, t, first, last):
+            copy(pairs[:, t // 2, first:last, t % 2], window[t][:, first:last])
+
         for t in range(2):
-            copy_on_gpsimd(shared[:, 0, :, t], window[t][:, 0:SHARED_COLS])
-        nc.scalar.copy(shared[:, 1, :, 0], window[2][:, 0:SHARED_COLS])
-        for t in range(LANES - 1):
-            nc.vector.tensor_copy(own[:, t // 2, :, t % 2], window[t][:, SHARED_COLS:POOL])
-        for c in range(SHARED, len(WIDTHS)):
-            at = STARTS[c] - SHARED_COLS
-            nc.vector.tensor_copy(own[:, 1, at : at + WIDTHS[c], 1], window[3][:, STARTS[c] : STARTS[c] + WIDTHS[c]])
+            round_lane(copy_on_gpsimd, t, GP_FIRST, POOL)
+        round_lane(nc.scalar.copy, 2, STARTS[OWN], POOL)
+        for t in range(2):
+            round_lane(nc.vector.tensor_copy, t, 0, GP_FIRST)
+        round_lane(nc.vector.tensor_copy, 2, 0, STARTS[OWN])
+        for c in range(OWN):
+            round_lane(nc.vector.tensor_copy, 3, STARTS[c], STARTS[c + 1])
 
         spare = ["u_pool1", "u_pool3", "sv_pool", "su_pool", "v_pool1", "v_pool2"]
         o_by_d = [sbuf([P, width, LANES], BF16, "o_by_d%d" % c, tag=spare[c]) for c, width in enumerate(WIDTHS)]
@@ -358,33 +362,29 @@ def tile_attend_gsink_u_pl_kernel(tc, uT, vT, su, sv, y, offs, qoffs, out_0, out
         scales_out = out_2.rearrange("a q c -> q (a c)").bitcast(I32)
 
         def weave_out(c, copy):
-            pairs, at = (shared[:], STARTS[c]) if c < SHARED else (own, STARTS[c] - SHARED_COLS)
-            words = pairs.rearrange("p u c e -> p (u c e)").bitcast(F32).rearrange("p (u c) -> p c u", u=2)
-            copy(flat(o_by_d[c][:]).bitcast(F32).rearrange("p (c u) -> p c u", u=2), words[:, at : at + WIDTHS[c], :])
+            copy(flat(o_by_d[c][:]).bitcast(F32).rearrange("p (c u) -> p c u", u=2), words[:, STARTS[c] : STARTS[c + 1], :])
 
         def quantise_out(c):
-            cols = slice(STARTS[c], STARTS[c] + WIDTHS[c])
+            cols = slice(STARTS[c], STARTS[c + 1])
             nc.vector.quantize_mx(o_codes[:, cols].bitcast(E4M3), o_scales[:, cols], flat(o_by_d[c][:]))
 
         def store_codes(first, last):
-            cols = slice(STARTS[first], STARTS[last] + WIDTHS[last])
+            cols = slice(STARTS[first], STARTS[last + 1])
             nc.sync.dma_start(words_out[:, cols], o_codes[:, cols].bitcast(I32))
 
-        for c in range(2):
-            cols = slice(c * HALF * 2, (c + 1) * HALF * 2)
-            nc.scalar.copy(shared[:, 1, cols, 1], window[3][:, cols])
+        round_lane(nc.scalar.copy, 3, STARTS[OWN], STARTS[OWN + 1])
+        weave_out(OWN, nc.scalar.copy)
+        round_lane(nc.scalar.copy, 3, STARTS[OWN + 1], POOL)
+        for c in range(OWN + 1, len(WIDTHS)):
             weave_out(c, nc.scalar.copy)
-        for c in range(SHARED, len(WIDTHS)):
+        for c in range(OWN):
             weave_out(c, nc.vector.tensor_copy)
-        for c in range(SHARED, len(WIDTHS)):
+        last = len(WIDTHS) - 1
+        for c in range(len(WIDTHS)):
             quantise_out(c)
-        store_codes(SHARED, len(WIDTHS) - 1)
-        weave_out(2, nc.scalar.copy)
-        quantise_out(0)
-        quantise_out(1)
-        store_codes(0, 1)
-        quantise_out(2)
-        store_codes(2, 2)
-        for q in range(4):
-            queue = nc.scalar if q % 2 else nc.sync
+            if c in (OWN - 1, last - 1):
+                store_codes({OWN - 1: 0, last - 1: OWN}[c], c)
+        for q, queue in ((0, nc.sync), (2, nc.scalar), (1, nc.scalar), (3, nc.sync)):
             queue.dma_start(scales_out[4 * q : 4 * q + 4, :], o_scales[32 * q : 32 * q + 4, :].bitcast(I32))
+            if q == 0:
+                store_codes(last, last)

@@ -28,7 +28,7 @@ RUN = 4
 WIDTHS = (512, 512, 512, 256, 256)
 OWN = 2
 STARTS = [sum(WIDTHS[:c]) for c in range(len(WIDTHS) + 1)]
-GP_FIRST = 1152
+GP_FIRST = 1024
 
 
 def tile_attend_gsink_u_pl_kernel(tc, uT, vT, su, sv, y, offs, qoffs, out_0, out_1, out_2):
@@ -102,6 +102,8 @@ def tile_attend_gsink_u_pl_kernel(tc, uT, vT, su, sv, y, offs, qoffs, out_0, out
             nc.tensor.transpose(sv_turned[:, r, :], sv_listed[:, r::LANES], ident[:])
         sv_col = sbuf([P, LANES], F32, "sv_col")
         nc.scalar.copy(sv_col[:], sv_turned[:, :, P - 1])
+        sv_inv = sbuf([P, LANES], F32, "sv_inv")
+        nc.vector.reciprocal(sv_inv[:], sv_col[:])
         su_turned = bank(1, "su_turned")
         for b in range(LANES):
             nc.tensor.transpose(su_turned[:, b, :], su_listed[:, b * P : (b + 1) * P], ident[:])
@@ -205,15 +207,16 @@ def tile_attend_gsink_u_pl_kernel(tc, uT, vT, su, sv, y, offs, qoffs, out_0, out
                     stop=b == LANES - 1 and r % 2 == 1,
                     is_transpose=True,
                 )
-        c1 = [sbuf([P, 2], F32, "c1_%d" % h) for h in range(2)]
-        cinv = [sbuf([P, 2], F32, "cinv%d" % h) for h in range(2)]
+        over_sv = [sbuf([P, 2], F32, "over_sv%d" % h) for h in range(2)]
         csv = [sbuf([P, 2], F32, "csv%d" % h) for h in range(2)]
+        terms = sbuf([P, LANES, P], F32, "terms")
         for h in range(2):
-            nc.vector.tensor_reduce(c1[h][:], sums_turned[h][:, 0:2, :], mybir.AxisListType.X, ALU.add)
-        for h in range(2):
-            nc.vector.reciprocal(cinv[h][:], c1[h][:])
-        for h in range(2):
-            nc.vector.tensor_tensor(csv[h][:], cinv[h][:], sv_col[:, 2 * h : 2 * h + 2], ALU.mult)
+            for e in range(2):
+                r = 2 * h + e
+                nc.vector.tensor_scalar(
+                    terms[:, r, :], sums_turned[h][:, e, :], sv_inv[:, r : r + 1], 0.0, ALU.mult, ALU.add, accum_out=over_sv[h][:, e : e + 1]
+                )
+            nc.vector.reciprocal(csv[h][:], over_sv[h][:])
 
         y_turned = [[bank(6 * h + k, "y_turned%d_%d" % (h, k)) for k in range(2)] for h in range(2)]
         for b in range(LANES):
@@ -226,15 +229,17 @@ def tile_attend_gsink_u_pl_kernel(tc, uT, vT, su, sv, y, offs, qoffs, out_0, out
                 nc.scalar.activation(y_both[h][:, r, :], lane_of(y_turned[h], r), ACT.Copy, scale=sv_col[:, r : r + 1])
 
         f_su = [sbuf([P, SLOTS], F32, "f_su0", tag="scaled1")[:], held[:, 1, :]]
-        f_su += [sbuf([P, SLOTS], F32, "f_su2", tag="scaled2")[:], sbuf([P, SLOTS], F32, "f_su3", tag="f3")[:]]
+        f_late = sbuf([P, 2, SLOTS], F32, "f_late", tag="expd1")
+        f_su += [f_late[:, 0, :], f_late[:, 1, :]]
         for h in range(2):
             even, odd = 2 * h, 2 * h + 1
             if h == 0:
                 nc.scalar.activation(f_su[even], f_tile[even][:, 0:SLOTS], ACT.Copy, scale=su_col[:, even : even + 1])
             else:
-                nc.vector.tensor_scalar(f_su[even], f_tile[even][:, 0:SLOTS], su_col[:, even : even + 1], None, ALU.mult)
-            nc.vector.tensor_scalar(f_su[odd], expd[odd][:], rinv[odd][:], su_col[:, odd : odd + 1], ALU.mult, ALU.mult)
+                for b in (even, odd):
+                    nc.gpsimd.tensor_scalar(f_su[b], f_tile[b][:, 0:SLOTS], su_col[:, b : b + 1], 0.0, ALU.mult, ALU.add)
             if h == 0:
+                nc.vector.tensor_scalar(f_su[odd], expd[odd][:], rinv[odd][:], su_col[:, odd : odd + 1], ALU.mult, ALU.mult)
                 finish_y(h)
         f_turned = []
         for h in range(2):

@@ -187,7 +187,7 @@ def tile_attend_gsink_u_pl_kernel(tc, uT, vT, su, sv, y, offs, qoffs, out_0, out
             return flat(banks[r % 2][:])[:, r // 2 * HALF : (r // 2 + 1) * HALF]
 
         rinv = [sbuf([P, 1], F32, "rinv%d" % b) for b in range(LANES)]
-        held = sbuf([P, 2, SLOTS], F32, "held", tag="scaled3")
+        held = sbuf([P, 3, SLOTS], F32, "held", tag="scaled3")
         f_tile = [sbuf([P, SLOTS], F32, "f0", tag="sv_row"), sbuf([P, SLOTS], F32, "f1"), held[:, 0, :], sbuf([P, SLOTS], F32, "f3")]
         sums_turned = [bank(4 + h, "sums_turned%d" % h) for h in range(2)]
         for b in range(LANES):
@@ -228,13 +228,13 @@ def tile_attend_gsink_u_pl_kernel(tc, uT, vT, su, sv, y, offs, qoffs, out_0, out
             for r in range(LANES):
                 nc.scalar.activation(y_both[h][:, r, :], lane_of(y_turned[h], r), ACT.Copy, scale=sv_col[:, r : r + 1])
 
-        f_su = [sbuf([P, SLOTS], F32, "f_su0", tag="scaled1")[:], held[:, 1, :]]
+        f_su = [held[:, 2, :], held[:, 1, :]]
         f_late = sbuf([P, 2, SLOTS], F32, "f_late", tag="expd1")
         f_su += [f_late[:, 0, :], f_late[:, 1, :]]
         for h in range(2):
             even, odd = 2 * h, 2 * h + 1
             if h == 0:
-                nc.scalar.activation(f_su[even], f_tile[even][:, 0:SLOTS], ACT.Copy, scale=su_col[:, even : even + 1])
+                nc.vector.tensor_scalar(f_su[even], f_tile[even][:, 0:SLOTS], su_col[:, even : even + 1], None, ALU.mult)
             else:
                 for b in (even, odd):
                     nc.gpsimd.tensor_scalar(f_su[b], f_tile[b][:, 0:SLOTS], su_col[:, b : b + 1], 0.0, ALU.mult, ALU.add)

from contextlib import ExitStack

import concourse.mybir as mybir
from concourse.masks import make_identity

FLOPS = 536870912

F32 = mybir.dt.float32
BF16 = mybir.dt.bfloat16
I32 = mybir.dt.int32
U32 = mybir.dt.uint32
U16 = mybir.dt.uint16
U8 = mybir.dt.uint8
E4M3 = mybir.dt.float8_e4m3fn_x4
E5M2 = mybir.dt.float8_e5m2_x4
ALU = mybir.AluOpType
ACT = mybir.ActivationFunctionType

P = 128
LANES = 4
POOL = 2048
SLOTS = 512
HALF = SLOTS // 2
HALF_LIST = HALF // 16
SU_ROW = 63
RUN = 4

WIDTHS = (512, 512, 512, 256, 256)
OWN = 2
STARTS = [sum(WIDTHS[:c]) for c in range(len(WIDTHS) + 1)]
GP_FIRST = 1024


def tile_attend_gsink_u_pl_kernel(tc, uT, vT, su, sv, y, offs, qoffs, out_0, out_1, out_2):
    nc = tc.nc
    with ExitStack() as ctx:
        lists = ctx.enter_context(tc.tile_pool(name="lists", bufs=1))
        sb = ctx.enter_context(tc.tile_pool(name="sb", bufs=1))
        ps = ctx.enter_context(tc.psum_pool(name="ps", bufs=1))

        def sbuf(shape, dtype, name, tag=None):
            return sb.tile(shape, dtype, name=name, tag=tag or name, align_bytes=64)

        def bank(number, name):
            return ps.tile([P, LANES, P], F32, name=name, tag="bank%d" % number)

        def flat(ap):
            return ap.rearrange("p a b -> p (a b)")

        def copy_on_gpsimd(dst, src):
            nc.gpsimd.tensor_scalar(dst, src, 1.0, 0.0, ALU.mult, ALU.add)

        jlist = lists.tile([P, SLOTS // 16], U16, name="jlist")
        ilist = lists.tile([P, SLOTS // 16], U16, name="ilist")
        v_rows = vT.rearrange("(p t) c -> p t c", t=LANES)
        u_rows = uT.rearrange("(p t) c -> p t c", t=LANES)
        v_pool = [sbuf([P, POOL], F32, "v_pool%d" % t) for t in range(LANES)]
        u_pool = [sbuf([P, POOL], F32, "u_pool%d" % t) for t in range(LANES)]
        sv_pool = sbuf([P, POOL], F32, "sv_pool")
        su_pool = sbuf([P, POOL], F32, "su_pool")
        nc.sync.dma_start(v_pool[0][:], v_rows[:, 0, :])
        nc.sync.dma_start(jlist[:], qoffs)
        nc.sync.dma_start(ilist[:], offs)
        nc.scalar.dma_start(sv_pool[P - 1 : P, :], sv[0:1, :])
        nc.scalar.dma_start(su_pool[SU_ROW : SU_ROW + 1, :], su[0:1, :])
        for t in range(1, LANES):
            nc.sync.dma_start(v_pool[t][:], v_rows[:, t, :])
        for t in range(LANES):
            nc.sync.dma_start(u_pool[t][:], u_rows[:, t, :])

        ident = sbuf([P, P], F32, "ident")
        make_identity(nc, ident[:])
        nc.gpsimd.memset(sv_pool[0 : P - 1, :], 0.0)
        nc.gpsimd.memset(su_pool[0:SU_ROW, :], 0.0)
        nc.gpsimd.memset(su_pool[SU_ROW + 1 : P, :], 0.0)

        window = [sbuf([P, POOL], F32, "window%d" % w) for w in range(LANES)]
        for w in range(LANES):
            nc.gpsimd.memset(window[w][:], 0.0)

        v_by_d = sbuf([P, SLOTS, LANES], BF16, "v_by_d")
        for t in range(LANES):
            nc.vector.tensor_copy(v_by_d[:, :, t], v_pool[t][:].indirect(jlist[:]))
        y_tile = [sbuf([P, SLOTS], F32, "y%d" % b, tag="v_pool%d" % b) for b in range(LANES)]
        for b in range(LANES):
            nc.sync.dma_start(y_tile[b][:], y[b * P : (b + 1) * P, :])
        v_dealt = sbuf([P, SLOTS, LANES], BF16, "v_dealt")
        nc.scalar.copy(
            flat(v_dealt[:]).bitcast(F32).rearrange("p (r c n w) -> p c r n w", r=LANES, n=2, w=2),
            flat(v_by_d[:]).bitcast(F32).rearrange("p (c n r w) -> p c r n w", r=LANES, n=2, w=2),
        )
        vd_codes = sbuf([P, SLOTS], U32, "vd_codes", tag="u_pool1")
        vd_scales = sbuf([P, SLOTS], U8, "vd_scales")
        nc.vector.quantize_mx(vd_codes[:].bitcast(E4M3), vd_scales[:], flat(v_dealt[:]))

        sv_listed = sbuf([P, SLOTS], F32, "sv_listed")
        nc.scalar.activation(sv_listed[:], sv_pool[:].indirect(jlist[:]), ACT.Copy)
        su_listed = sbuf([P, SLOTS], F32, "su_listed")
        nc.scalar.activation(su_listed[:], su_pool[:].indirect(ilist[:]), ACT.Copy)
        sv_turned = bank(0, "sv_turned")
        for r in range(LANES):
            nc.tensor.transpose(sv_turned[:, r, :], sv_listed[:, r::LANES], ident[:])
        sv_col = sbuf([P, LANES], F32, "sv_col")
        nc.scalar.copy(sv_col[:], sv_turned[:, :, P - 1])
        sv_inv = sbuf([P, LANES], F32, "sv_inv")
        nc.vector.reciprocal(sv_inv[:], sv_col[:])
        su_turned = bank(1, "su_turned")
        for b in range(LANES):
            nc.tensor.transpose(su_turned[:, b, :], su_listed[:, b * P : (b + 1) * P], ident[:])
        su_col = sbuf([P, LANES], F32, "su_col")
        nc.scalar.copy(su_col[:], su_turned[:, :, SU_ROW])
        sv_spread = bank(2, "sv_spread")
        for r in range(LANES):
            nc.tensor.transpose(sv_spread[:, r, :], sv_col[:, r : r + 1].to_broadcast([P, P]), ident[:])
        sv_row = sbuf([P, LANES, P], F32, "sv_row")
        nc.scalar.copy(sv_row[:], sv_spread[:])

        v_words = flat(v_dealt[:]).bitcast(F32)
        v_by_j = sbuf([P, LANES, P, LANES], BF16, "v_by_j")
        for pair in range(2):
            v_turned = bank(4 + pair, "v_turned%d" % pair)
            for r in range(LANES):
                nc.tensor.transpose(v_turned[:, r, :], v_words[:, 2 * P * r + pair : 2 * P * (r + 1) : 2], ident[:])
            nc.scalar.copy(
                v_by_j[:, 2 * pair : 2 * pair + 2, :, :],
                flat(v_turned[:]).bitcast(BF16).rearrange("s (r p e) -> s e p r", r=LANES, e=2),
            )

        u_by_d = [sbuf([P, HALF, LANES], BF16, "u_by_d%d" % h) for h in range(2)]
        half_list = [ilist[:, h * HALF_LIST : (h + 1) * HALF_LIST] for h in range(2)]
        for t in range(LANES):
            nc.vector.tensor_copy(u_by_d[0][:, :, t], u_pool[t][:].indirect(half_list[0]))
            if t < 2:
                nc.vector.tensor_copy(u_by_d[1][:, :, t], u_pool[t][:].indirect(half_list[1]))
            elif t == 2:
                nc.scalar.activation(u_by_d[1][:, :, t], u_pool[t][:].indirect(half_list[1]), ACT.Copy)
        tiles = [slice(n * P, (n + 1) * P) for n in range(2)]
        for n in range(2):
            entries = ilist[:, HALF_LIST + n * P // 16 : HALF_LIST + (n + 1) * P // 16]
            nc.scalar.activation(u_by_d[1][:, tiles[n], LANES - 1], u_pool[LANES - 1][:].indirect(entries), ACT.Copy)
        u_codes = sbuf([P, SLOTS], U32, "u_codes")
        u_scales = sbuf([P, SLOTS], U8, "u_scales")
        for first, last in ((b * P, (b + 1) * P) for b in range(LANES)):
            woven = u_by_d[first // HALF][:, first % HALF : first % HALF + last - first, :]
            nc.vector.quantize_mx(u_codes[:, first:last].bitcast(E4M3), u_scales[:, first:last], flat(woven))

        vj_codes = sbuf([P, SLOTS], U32, "vj_codes", tag="u_pool2")
        vj_scales = sbuf([P, SLOTS], U8, "vj_scales")
        nc.vector.quantize_mx(vj_codes[:].bitcast(E4M3), vj_scales[:], v_by_j[:].rearrange("s t p r -> s (t p r)"))

        late = sbuf([P, 2, LANES, P], F32, "late", tag="u_by_d1")
        early = sbuf([P, 2, LANES, P], F32, "early", tag="u_pool3")
        y_su = [sbuf([P, LANES, P], F32, "y_su0")[:], early[:, 1, :, :], late[:, 0, :, :], late[:, 1, :, :]]
        scaled = [early[:, 0, :, :]] + [sbuf([P, LANES, P], F32, "scaled%d" % b)[:] for b in range(1, LANES)]
        for b in range(LANES):
            planes = y_su[b].rearrange("p r (c n) -> p c r n", n=RUN)
            rows = y_tile[b][:].rearrange("p (c n r) -> p c r n", n=RUN, r=LANES)
            if b == 0:
                nc.vector.tensor_scalar(planes, rows, su_col[:, b : b + 1], None, ALU.mult)
            elif b == 1:
                nc.scalar.activation(planes, rows, ACT.Copy, scale=su_col[:, b : b + 1])
            else:
                nc.gpsimd.tensor_scalar(planes, rows, su_col[:, b : b + 1], 0.0, ALU.mult, ALU.add)
        expd = [sbuf([P, SLOTS], F32, "expd%d" % b) for b in range(LANES)]
        r1 = [sbuf([P, 1], F32, "r1_%d" % b) for b in range(LANES)]
        for b in range(LANES):
            cols = slice(b * P, (b + 1) * P)
            for number, lanes in ([(0, slice(0, 2)), (5, slice(2, 4))] if b == 0 else [(b, slice(0, LANES))]):
                score = bank(number, "score%d_%d" % (b, number))
                slots = slice(lanes.start * P, lanes.stop * P)
                nc.tensor.matmul_mx(
                    flat(score[:, lanes, :]),
                    lhsT=u_codes[:, cols].bitcast(E4M3),
                    lhsT_scale=u_scales[:, cols],
                    rhs=vd_codes[:, slots].bitcast(E4M3),
                    rhs_scale=vd_scales[:, slots],
                    start=True,
                    stop=True,
                )
                nc.vector.tensor_tensor(scaled[b][:, lanes, :], sv_row[:, lanes, :], score[:, lanes, :], ALU.mult)
            nc.scalar.activation(expd[b][:], flat(scaled[b]), ACT.Exp, scale=su_col[:, b : b + 1], accum_out=r1[b][:])

        def quarter(banks, r, b):
            return banks[r % 2][:, 2 * (r // 2) + b % 2, :]

        def lane_of(banks, r):
            return flat(banks[r % 2][:])[:, r // 2 * HALF : (r // 2 + 1) * HALF]

        rinv = [sbuf([P, 1], F32, "rinv%d" % b) for b in range(LANES)]
        held = sbuf([P, 3, SLOTS], F32, "held", tag="scaled3")
        f_tile = [sbuf([P, SLOTS], F32, "f0", tag="sv_row"), sbuf([P, SLOTS], F32, "f1"), held[:, 0, :], sbuf([P, SLOTS], F32, "f3")]
        sums_turned = [bank(4 + h, "sums_turned%d" % h) for h in range(2)]
        for b in range(LANES):
            nc.vector.reciprocal(rinv[b][:], r1[b][:])
        for b in range(LANES - 1):
            nc.vector.tensor_scalar(f_tile[b][:, 0:SLOTS], expd[b][:], rinv[b][:], None, ALU.mult)
        for h in range(2):
            cols = slice(h * HALF, (h + 1) * HALF)
            nc.vector.tensor_scalar(f_tile[3][:, cols], expd[3][:, cols], rinv[3][:], None, ALU.mult)
        for b in range(LANES):
            for r in range(LANES):
                nc.tensor.matmul(
                    sums_turned[r // 2][:, r % 2, :],
                    f_tile[b][:, r * P : (r + 1) * P],
                    ident[:],
                    start=b == 0 and r % 2 == 0,
                    stop=b == LANES - 1 and r % 2 == 1,
                    is_transpose=True,
                )
        over_sv = [sbuf([P, 2], F32, "over_sv%d" % h) for h in range(2)]
        csv = [sbuf([P, 2], F32, "csv%d" % h) for h in range(2)]
        terms = sbuf([P, LANES, P], F32, "terms")
        for h in range(2):
            for e in range(2):
                r = 2 * h + e
                nc.vector.tensor_scalar(
                    terms[:, r, :], sums_turned[h][:, e, :], sv_inv[:, r : r + 1], 0.0, ALU.mult, ALU.add, accum_out=over_sv[h][:, e : e + 1]
                )
            nc.vector.reciprocal(csv[h][:], over_sv[h][:])

        y_turned = [[bank(6 * h + k, "y_turned%d_%d" % (h, k)) for k in range(2)] for h in range(2)]
        for b in range(LANES):
            for r in range(LANES):
                nc.tensor.transpose(quarter(y_turned[b // 2], r, b), y_su[b][:, r, :], ident[:])
        y_both = [sbuf([P, LANES, HALF], F32, "y_both%d" % h) for h in range(2)]

        def finish_y(h):
            for r in range(LANES):
                nc.scalar.activation(y_both[h][:, r, :], lane_of(y_turned[h], r), ACT.Copy, scale=sv_col[:, r : r + 1])

        f_su = [held[:, 2, :], held[:, 1, :]]
        f_late = sbuf([P, 2, SLOTS], F32, "f_late", tag="expd1")
        f_su += [f_late[:, 0, :], f_late[:, 1, :]]
        for h in range(2):
            even, odd = 2 * h, 2 * h + 1
            if h == 0:
                nc.vector.tensor_scalar(f_su[even], f_tile[even][:, 0:SLOTS], su_col[:, even : even + 1], None, ALU.mult)
            else:
                for b in (even, odd):
                    nc.gpsimd.tensor_scalar(f_su[b], f_tile[b][:, 0:SLOTS], su_col[:, b : b + 1], 0.0, ALU.mult, ALU.add)
            if h == 0:
                nc.vector.tensor_scalar(f_su[odd], expd[odd][:], rinv[odd][:], su_col[:, odd : odd + 1], ALU.mult, ALU.mult)
                finish_y(h)
        f_turned = []
        for h in range(2):
            f_turned.append([bank(2 - 2 * h + k, "f_turned%d_%d" % (h, k)) for k in range(2)])
            for r in range(LANES):
                for b in (2 * h, 2 * h + 1):
                    nc.tensor.transpose(quarter(f_turned[h], r, b), f_su[b][:, r * P : (r + 1) * P], ident[:])

        tiles = [slice(b * P, (b + 1) * P) for b in range(LANES)]
        halves = [slice(0, HALF), slice(HALF, SLOTS)]

        def entries(first, count):
            return ilist[:, first // 16 : (first + count) // 16]

        g_codes = sbuf([P, SLOTS], U32, "g_codes")
        g_scales = sbuf([P, SLOTS], U8, "g_scales")
        plan = [sbuf([P, LANES, HALF], F32, "plan%d" % h) for h in range(2)]
        row = sbuf([P, 3 * HALF + 2 * POOL], F32, "row", tag="u_pool0")
        g_by_j = [row[:, 0:SLOTS].bitcast(BF16).rearrange("s (i r) -> s i r", r=LANES)] * 2

        def scale_plan(h):
            for r in range(LANES):
                factor = csv[r // 2][:, r % 2 : r % 2 + 1]
                if h == 0 and r % 2 == 0:
                    nc.vector.tensor_scalar(plan[h][:, r, :], lane_of(f_turned[h], r), factor, None, ALU.mult)
                else:
                    nc.scalar.activation(plan[h][:, r, :], lane_of(f_turned[h], r), ACT.Copy, scale=factor)

        def make_g(h, n):
            nc.vector.tensor_tensor(
                g_by_j[h][:, tiles[n], :].rearrange("s (c n) r -> s c r n", n=2),
                plan[h][:, :, tiles[n]].rearrange("s r (c n) -> s c r n", n=2),
                y_both[h][:, :, tiles[n]].rearrange("s r (c n) -> s c r n", n=2),
                ALU.subtract,
            )

        def quantise_g(first, count):
            woven = g_by_j[first // HALF][:, first % HALF : first % HALF + count, :]
            cols = slice(first, first + count)
            nc.vector.quantize_mx(g_codes[:, cols].bitcast(E5M2), g_scales[:, cols], flat(woven))

        def product(t, sources, number, name):
            return multiply(t, sources, flat(bank(number, name)[:])[:, 0 : sources.stop - sources.start])

        def multiply(t, sources, acc):
            nc.tensor.matmul_mx(
                acc,
                lhsT=vj_codes[:, tiles[t]].bitcast(E4M3),
                lhsT_scale=vj_scales[:, tiles[t]],
                rhs=g_codes[:, sources].bitcast(E5M2),
                rhs_scale=g_scales[:, sources],
                start=True,
                stop=True,
            )
            return acc

        def scatter_on_scalar(t, h, values):
            nc.scalar.activation(window[t][:].indirect(entries(h * HALF, HALF)), values, ACT.Copy)

        du = [[sbuf([P, HALF], F32, "du%d_%d" % (t, h)) for h in range(2)] for t in range(2)]
        ones = sbuf([P, 1], F32, "ones")
        nc.vector.memset(ones[:], 1.0)
        scale_plan(0)
        finish_y(1)
        for n in range(2):
            make_g(0, n)
        for n in range(2):
            quantise_g(n * P, P)
        acc = bank(4, "du_a0")
        for n in range(2):
            multiply(0, tiles[n], acc[:, n, :])
        nc.scalar.copy(du[0][0][:], flat(acc[:])[:, 0:HALF])
        nc.scalar.copy(du[1][0][:], product(1, halves[0], 5, "du_a1"))
        scale_plan(1)
        for t in range(2):
            scatter_on_scalar(t, 0, du[t][0][:])
        for n in range(2):
            make_g(1, n)
        for n in range(2):
            quantise_g(HALF + n * P, P)
        acc = bank(2, "du_b0")
        for n in range(2):
            multiply(0, tiles[2 + n], acc[:, n, :])
        nc.vector.tensor_copy(du[0][1][:], flat(acc[:])[:, 0:HALF])
        nc.vector.tensor_copy(du[1][1][:], product(1, halves[1], 3, "du_b1"))
        for t in range(2):
            nc.vector.tensor_copy(window[t][:].indirect(entries(HALF, HALF)), du[t][1][:])
        for h, planes, number in ((1, (2, 3), 7), (0, (3, 2), 6)):
            acc = flat(bank(number, "du_late%d" % h)[:])
            for n, t in enumerate(planes):
                multiply(t, halves[h], acc[:, halves[n]])
            if h == 1:
                nc.scalar.copy(row[:, SLOTS : 2 * SLOTS], acc)
            else:
                for n in range(2):
                    nc.vector.tensor_copy(row[:, halves[n]], acc[:, halves[n]])
        nc.scalar.activation(window[2][:].indirect(ilist[:]), row[:, HALF : 3 * HALF], ACT.Copy, scale=ones[:])
        nc.vector.tensor_copy(window[3][:].indirect(entries(HALF, HALF)), row[:, 3 * HALF : 4 * HALF])
        scatter_on_scalar(3, 0, row[:, halves[0]])

        out_rows = out_0.rearrange("(p t) c -> p t c", t=LANES)
        for t in range(LANES):
            nc.sync.dma_start(out_rows[:, t, :], window[t][:])

        pairs = row[:, 3 * HALF :].bitcast(BF16).rearrange("p (u c e) -> p u c e", u=2, e=2)
        words = row[:, 3 * HALF :].rearrange("p (u c) -> p c u", u=2)

        def round_lane(copy, t, first, last):
            copy(pairs[:, t // 2, first:last, t % 2], window[t][:, first:last])

        for t in range(2):
            round_lane(copy_on_gpsimd, t, GP_FIRST, POOL)
        round_lane(nc.scalar.copy, 2, STARTS[OWN], POOL)
        for t in range(2):
            round_lane(nc.vector.tensor_copy, t, 0, GP_FIRST)
        round_lane(nc.vector.tensor_copy, 2, 0, STARTS[OWN])
        for c in range(OWN):
            round_lane(nc.vector.tensor_copy, 3, STARTS[c], STARTS[c + 1])

        spare = ["u_pool1", "u_pool3", "sv_pool", "su_pool", "v_pool1", "v_pool2"]
        o_by_d = [sbuf([P, width, LANES], BF16, "o_by_d%d" % c, tag=spare[c]) for c, width in enumerate(WIDTHS)]
        o_codes = sbuf([P, POOL], U32, "o_codes", tag="v_pool0")
        o_scales = sbuf([P, POOL], U8, "o_scales")
        words_out = out_1.rearrange("a p c l -> p (a c l)").bitcast(I32)
        scales_out = out_2.rearrange("a q c -> q (a c)").bitcast(I32)

        def weave_out(c, copy):
            copy(flat(o_by_d[c][:]).bitcast(F32).rearrange("p (c u) -> p c u", u=2), words[:, STARTS[c] : STARTS[c + 1], :])

        def quantise_out(c):
            cols = slice(STARTS[c], STARTS[c + 1])
            nc.vector.quantize_mx(o_codes[:, cols].bitcast(E4M3), o_scales[:, cols], flat(o_by_d[c][:]))

        def store_codes(first, last):
            cols = slice(STARTS[first], STARTS[last + 1])
            nc.sync.dma_start(words_out[:, cols], o_codes[:, cols].bitcast(I32))

        round_lane(nc.scalar.copy, 3, STARTS[OWN], STARTS[OWN + 1])
        weave_out(OWN, nc.scalar.copy)
        round_lane(nc.scalar.copy, 3, STARTS[OWN + 1], POOL)
        for c in range(OWN + 1, len(WIDTHS)):
            weave_out(c, nc.scalar.copy)
        for c in range(OWN):
            weave_out(c, nc.vector.tensor_copy)
        last = len(WIDTHS) - 1
        for c in range(len(WIDTHS)):
            quantise_out(c)
            if c in (OWN - 1, last - 1):
                store_codes({OWN - 1: 0, last - 1: OWN}[c], c)
        for q, queue in ((0, nc.sync), (2, nc.scalar), (1, nc.scalar), (3, nc.sync)):
            queue.dma_start(scales_out[4 * q : 4 * q + 4, :], o_scales[32 * q : 32 * q + 4, :].bitcast(I32))
            if q == 0:
                store_codes(last, last)
